import numpy as np
import ml_dtypes


def mxq(x, axis, fmt="e4m3"):
    dtype, down = {"e4m3": (ml_dtypes.float8_e4m3fn, 7), "e5m2": (ml_dtypes.float8_e5m2, 14)}[fmt]
    v = np.moveaxis(np.asarray(x, np.float32).astype(ml_dtypes.bfloat16).astype(np.float64), axis, -1)
    blocks = v.reshape(v.shape[:-1] + (-1, 32))
    amax = np.abs(blocks).max(-1, keepdims=True)
    byte = np.maximum(np.where(amax > 0, np.frexp(amax)[1] - 1 + 127, 0) - down, 1)
    scale = np.exp2(byte - 127.0)
    codes = (blocks / scale).astype(np.float32).astype(dtype).astype(np.float64)
    return np.moveaxis((codes * scale).reshape(v.shape), -1, axis)


WIDE = False


def mx_kscale(k):
    if not WIDE:
        return np.ones(k)
    levels = np.array([10, -10, 5, -5, 0])
    if k % 512:
        return np.exp2(np.random.permutation(np.resize(levels, k // 32))).repeat(32)
    a = np.empty((k // 512, 16))
    for p in range(k // 512):
        a[p, :8] = np.random.permutation(np.resize(levels, 8))
        for g in range(8):
            far = levels[np.abs(levels - a[p, g]) >= 10]
            a[p, g + 8] = far[np.random.randint(len(far))]
    return np.exp2(a.ravel()).repeat(32)


def f64(x):
    return np.asarray(x).astype(np.float64)


def striped(idx):
    return np.tile(idx.reshape(-1, 16).T, (8, 1)).astype(np.uint16)


def unstriped(offs):
    return offs[:16].T.reshape(-1).astype(np.int64)


E2M1 = np.array([0.0, 0.5, 1.0, 1.5, 2.0, 3.0, 4.0, 6.0, -0.0, -0.5, -1.0, -1.5, -2.0, -3.0, -4.0, -6.0])


def pack_weight(w, fmt):
    k, n = w.shape
    w = f64(np.asarray(w, np.float32).astype(ml_dtypes.bfloat16)).reshape(k // 32, 32, n)
    amax = np.abs(w).max(1)
    if fmt == "e4m3":
        byte = np.frexp(amax)[1] - 1 + 127 - 7
    else:
        mant, ex = np.frexp(amax / 6.0)
        byte = np.where(mant > 0.5, ex, ex - 1) + 127
    byte = np.clip(np.where(amax > 0, byte, 1), 1, 254)
    scaled = (w * np.exp2(127.0 - byte)[:, None, :]).reshape(k, n).astype(np.float32)
    by_word = np.ascontiguousarray(scaled.reshape(k // 512, 128, 4, n).transpose(0, 1, 3, 2))
    if fmt == "e4m3":
        words = by_word.astype(ml_dtypes.float8_e4m3fn).view(np.uint8)
    else:
        c = by_word.astype(ml_dtypes.float4_e2m1fn).view(np.uint8) & 0xF
        words = (c[..., 0::2] | (c[..., 1::2] << 4)).reshape(k // 512, 128, 2 * n)
    return np.ascontiguousarray(words), np.ascontiguousarray(byte.astype(np.uint8).reshape(k // 512, 16, n))


def unpack_weight(words, scales, fmt):
    g, _, n = scales.shape
    words = np.ascontiguousarray(words).reshape(g, 128, n, -1)
    if fmt == "e4m3":
        vals = words.view(ml_dtypes.float8_e4m3fn).astype(np.float64)
    else:
        nib = np.empty((g, 128, n, 4), np.uint8)
        nib[..., 0::2] = words & 0xF
        nib[..., 1::2] = words >> 4
        vals = E2M1[nib]
    vals = vals * np.repeat(np.exp2(scales.astype(np.float64) - 127.0), 8, axis=1)[..., None]
    return vals.transpose(0, 1, 3, 2).reshape(g * 512, n)


def gelu(v):
    return 0.5 * v * (1.0 + np.tanh(np.sqrt(2.0 / np.pi) * (v + 0.044715 * v**3)))


K, H, T, S, T2, S2 = 1536, 1024, 2048, 512, 4096, 1024


def setup_inputs():
    n = np.random.standard_normal
    s = mx_kscale(K)[:, None]
    u = mx_kscale(H)[:, None]
    tab_words, tab_scales = pack_weight(n((K, T)) * s, "e4m3")
    tab2_words, tab2_scales = pack_weight(1.5 * n((H, T2)) / np.sqrt(H) / u, "e4m3")
    w1 = (n((K, H)) / np.sqrt(K) / s).astype(np.float32)
    w4_words, w4_scales = pack_weight(n((K, H)) / np.sqrt(K) / s * u.T, "e2m1")
    return {"tab_words": tab_words, "tab_scales": tab_scales,
            "offs": striped(np.random.permutation(T)[:S]),
            "tab2_words": tab2_words, "tab2_scales": tab2_scales,
            "offs2": striped(np.random.permutation(T2)[:S2]),
            "w1": w1, "w4_words": w4_words, "w4_scales": w4_scales}


def reference(tab_words, tab_scales, offs, tab2_words, tab2_scales, offs2, w1, w4_words, w4_scales):
    v = unpack_weight(tab_words, tab_scales, "e4m3")[:, unstriped(offs)]
    v2 = unpack_weight(tab2_words, tab2_scales, "e4m3")[:, unstriped(offs2)]
    w4 = unpack_weight(w4_words, w4_scales, "e2m1")
    a = mxq(f64(w1), 0, "e4m3").T @ v
    b = w4.T @ v
    gate = 0.5 * a * (1.0 + np.tanh(np.sqrt(2.0 / np.pi) * (a + 0.044715 * a * a * a)))
    h = gate * b
    y = v2.T @ mxq(h, 0, "e4m3")
    x = y * y
    return x / (1.0 + x)

@@ -1,0 +1,336 @@
+from contextlib import ExitStack
+
+import concourse.mybir as mybir
+from concourse.masks import make_identity
+
+K, H, T, S, T2, S2 = 1536, 1024, 2048, 512, 4096, 1024
+FLOPS = 2 * (2 * K * H * S + H * S2 * S)
+
+F32 = mybir.dt.float32
+BF16 = mybir.dt.bfloat16
+I32 = mybir.dt.int32
+U32 = mybir.dt.uint32
+U16 = mybir.dt.uint16
+U8 = mybir.dt.uint8
+FP8X4 = mybir.dt.float8_e4m3fn_x4
+FP4X4 = mybir.dt.float4_e2m1fn_x4
+ACT = mybir.ActivationFunctionType
+MULT = mybir.AluOpType.mult
+
+P = 128
+PACK = 4
+PASS = P * PACK
+K_PASSES = K // PASS
+R_PASSES = H // PASS
+J_TILES = S // P
+I_TILES = S2 // P
+QUADS = 4
+ROWS = 4
+VECTOR_COLS = {(0, 0): 0, (1, 0): 0, (2, 0): 0, (0, 1): 512, (1, 1): 0, (2, 1): 320}
+
+
+def tile_list_residue_contact_strength_kernel(
+    tc, tab_words, tab_scales, offs, tab2_words, tab2_scales, offs2, w1, w4_words, w4_scales, out
+):
+    nc = tc.nc
+    with ExitStack() as ctx:
+        keep = ctx.enter_context(tc.tile_pool(name="keep", bufs=1))
+        ring = ctx.enter_context(tc.tile_pool(name="ring", bufs=3))
+        psum = ctx.enter_context(tc.psum_pool(name="psum", bufs=1))
+
+        def held(shape, dtype, name, after=None):
+            return keep.tile(shape, dtype, name=name, tag=after or name, align_bytes=64)
+
+        def bank(number, shape):
+            return psum.tile(shape, F32, name="bank%d" % number, tag="bank%d" % number)
+
+        idx = keep.tile([P, S // 16], U16, name="idx")
+        idx2 = keep.tile([P, S2 // 16], U16, name="idx2")
+        nc.sync.dma_start(idx[:], offs)
+
+        tab_sc = held([P, K_PASSES * T], U8, "tab_sc")
+        w4_sc = held([P, K_PASSES * H], U8, "w4_sc")
+        tab2_sc = held([P, T2], U8, "tab2_sc")
+        nc.vector.memset(tab_sc[:].bitcast(I32), 0)
+        nc.gpsimd.memset(tab2_sc[:].bitcast(I32), 0)
+        nc.vector.memset(w4_sc[:].bitcast(I32), 0)
+
+        def load_planes(queue, plane, scales):
+            for q in range(QUADS):
+                queue.dma_start(
+                    plane[:].bitcast(I32)[32 * q : 32 * q + ROWS, :].rearrange("r (a w) -> r a w", a=K_PASSES),
+                    scales[:, ROWS * q : ROWS * (q + 1), :].rearrange("a r t -> r a t").bitcast(I32),
+                )
+
+        w1_raw = {}
+        tab_w = {}
+        tab2_w = {}
+
+        def load_w1(a, half, after):
+            w1_raw[a, half] = held([P, PACK, PASS], F32, "w1_raw%d%d" % (a, half), after)
+            rows = w1[PASS * a : PASS * (a + 1), PASS * half : PASS * (half + 1)]
+            nc.sync.dma_start(w1_raw[a, half][:], rows.rearrange("(p t) c -> p t c", t=PACK))
+
+        w4 = {}
+
+        def load_w4(half, after):
+            w4[half] = held([P, K_PASSES * 2 * PASS], U8, "w4_%d" % half, after)
+            nc.sync.dma_start(
+                w4[half][:].bitcast(I32).rearrange("p (a w) -> p a w", a=K_PASSES),
+                w4_words[:, :, 2 * PASS * half : 2 * PASS * (half + 1)].rearrange("a p c -> p a c").bitcast(I32),
+            )
+
+        def load_tab(a, after):
+            tab_w[a] = held([P, T], I32, "tab_w%d" % a, after)
+            nc.sync.dma_start(tab_w[a][:], tab_words[a].rearrange("p t i -> p (t i)").bitcast(I32))
+
+        def load_tab2(a, after):
+            tab2_w[a] = held([P, T2], I32, "tab2_w%d" % a, after)
+            nc.sync.dma_start(tab2_w[a][:], tab2_words[a].rearrange("p t i -> p (t i)").bitcast(I32))
+
+        nc.sync.dma_start(idx2[:], offs2)
+        load_w1(0, 0, "A")
+        load_tab(0, "B")
+        load_w1(1, 0, "A2")
+        load_tab(1, "B2")
+        load_planes(nc.scalar, tab_sc, tab_scales)
+        for q in range(QUADS):
+            first = 32 * q + ROWS
+            nc.gpsimd.dma_start(
+                tab2_sc[:].bitcast(I32)[first : first + R_PASSES * ROWS, :],
+                tab2_scales[:, ROWS * q : ROWS * (q + 1), :].bitcast(I32),
+            )
+        load_planes(nc.gpsimd, w4_sc, w4_scales)
+        identity = held([P, P], F32, "identity")
+        make_identity(nc, identity[:])
+
+        zero = held([P, 1], F32, "zero")
+        gelu_bias = held([P, 1], F32, "gelu_bias")
+        nc.vector.memset(zero[:], 0.0)
+        nc.scalar.activation(gelu_bias[:], zero[:], ACT.Gelu_apprx_tanh)
+
+        w1_codes = {}
+        w1_sc = {}
+        w1_grouped = {}
+
+        def round_w1(a, half, after, vector_piece=PASS, scalar_piece=PASS):
+            grouped = held([P, PASS, PACK], BF16, "w1_grouped%d%d" % (a, half), after)
+            w1_grouped[a, half] = grouped
+            split = VECTOR_COLS[a, half]
+            raw = w1_raw[a, half]
+
+            def views(c0, c1):
+                dst = grouped[:, c0:c1, :].rearrange("p (c i) t -> p c t i", i=4)
+                src = raw[:, :, c0:c1].rearrange("p t (c i) -> p c t i", i=4)
+                return dst, src
+
+            for c0 in range(0, split, vector_piece):
+                nc.vector.tensor_copy(*views(c0, min(split, c0 + vector_piece)))
+            for c0 in range(split, PASS, scalar_piece):
+                nc.scalar.copy(*views(c0, min(PASS, c0 + scalar_piece)))
+
+        def quantise_w1(a, half):
+            w1_codes[a, half] = held([P, PASS], U32, "w1_codes%d%d" % (a, half))
+            w1_sc[a, half] = held([P, PASS], U8, "w1_sc%d%d" % (a, half))
+            nc.vector.quantize_mx(
+                out=w1_codes[a, half][:].bitcast(FP8X4),
+                scales=w1_sc[a, half][:],
+                in_=w1_grouped[a, half][:].rearrange("p c t -> p (c t)"),
+            )
+
+        v_w = {}
+        v_sc = {}
+
+        def gather_tab_scales(a):
+            v_sc[a] = held([P, S], U8, "v_sc%d" % a)
+            nc.vector.tensor_copy(v_sc[a][:], tab_sc[:, T * a : T * (a + 1)].indirect(idx[:]))
+
+        def gather_tab(a, pieces, after=None):
+            v_w[a] = held([P, S], U32, "v_w%d" % a, after)
+            n = S // pieces
+            for g in range(pieces):
+                nc.vector.tensor_copy(
+                    v_w[a][:, n * g : n * (g + 1)],
+                    tab_w[a][:].bitcast(U32).indirect(idx[:, n // 16 * g : n // 16 * (g + 1)]),
+                )
+
+        def gate_pass(acc, a, half, jt):
+            cols = slice(P * jt, P * (jt + 1))
+            nc.tensor.matmul_mx(
+                out=acc[:],
+                lhsT=v_w[a][:, cols].bitcast(FP8X4),
+                lhsT_scale=v_sc[a][:, cols],
+                rhs=w1_codes[a, half][:].bitcast(FP8X4),
+                rhs_scale=w1_sc[a, half][:],
+                start=(a == 0),
+                stop=(a == K_PASSES - 1),
+            )
+
+        def value_pass(acc, a, half, jt):
+            cols = slice(P * jt, P * (jt + 1))
+            first = H * a + PASS * half
+            nc.tensor.matmul_mx(
+                out=acc[:],
+                lhsT=v_w[a][:, cols].bitcast(FP8X4),
+                lhsT_scale=v_sc[a][:, cols],
+                rhs=w4[half][:, 2 * PASS * a : 2 * PASS * (a + 1)].bitcast(FP4X4),
+                rhs_scale=w4_sc[:, first : first + PASS],
+                start=(a == 0),
+                stop=(a == K_PASSES - 1),
+            )
+
+        h_codes = {}
+        h_sc = {}
+        gates = {}
+        h_rows = {}
+        h_grouped = {}
+        order = "j (p u e) -> j u p e"
+
+        def gelu(half, jt, acc):
+            gates[half, jt] = held([P, 2, P, 2], F32, "gate%d%d" % (half, jt))
+            nc.scalar.activation(
+                gates[half, jt][:], acc[:].rearrange(order, u=2, e=2), ACT.Gelu_apprx_tanh, bias=gelu_bias[:]
+            )
+
+        def gated(half, jt, acc):
+            h_rows[half, jt] = held([P, 2, P, 2], BF16, "h_rows%d%d" % (half, jt))
+            nc.vector.tensor_tensor(h_rows[half, jt][:], acc[:].rearrange(order, u=2, e=2), gates[half, jt][:], MULT)
+
+        def turn(half, jt):
+            words = h_rows[half, jt][:].rearrange("j u p e -> j (u p e)").bitcast(F32)
+            turned = bank(jt, [P, 2, P])
+            for u in range(2):
+                nc.tensor.transpose(turned[:, u, :], words[:, P * u : P * (u + 1)], identity[:])
+            h_grouped[half, jt] = held([P, P * PACK], BF16, "h_grouped%d%d" % (half, jt))
+            nc.scalar.copy(
+                h_grouped[half, jt][:].bitcast(F32).rearrange("p (j u) -> p j u", u=2),
+                turned[:].rearrange("p u j -> p j u"),
+            )
+
+        def quantise_h(half, jt):
+            cols = slice(P * jt, P * (jt + 1))
+            nc.vector.quantize_mx(
+                out=h_codes[half][:, cols].bitcast(FP8X4), scales=h_sc[half][:, cols], in_=h_grouped[half, jt][:]
+            )
+
+        def finish_h(half, gate_acc, value_acc, freed):
+            for step in range(J_TILES + 2):
+                if step < J_TILES:
+                    gelu(half, step, gate_acc[step])
+                    gated(half, step, value_acc[step])
+                if 1 <= step <= J_TILES:
+                    turn(half, step - 1)
+                    freed(step - 1)
+                if step >= 2:
+                    quantise_h(half, step - 2)
+
+        for half in range(R_PASSES):
+            h_codes[half] = held([P, S], U32, "h_codes%d" % half)
+            h_sc[half] = held([P, S], U8, "h_sc%d" % half)
+
+        gate_acc = [bank(jt, [P, PASS]) for jt in range(J_TILES)]
+        value_acc = [bank(J_TILES + jt, [P, PASS]) for jt in range(J_TILES)]
+
+        def both_passes(a):
+            for jt in range(J_TILES):
+                gate_pass(gate_acc[jt], a, 0, jt)
+                value_pass(value_acc[jt], a, 0, jt)
+
+        def gate_passes(a, half):
+            for jt in range(J_TILES):
+                gate_pass(gate_acc[jt], a, half, jt)
+
+        for a in range(K_PASSES):
+            gather_tab_scales(a)
+        round_w1(0, 0, "C")
+        load_w1(2, 0, "A")
+        quantise_w1(0, 0)
+        gather_tab(0, 1)
+        load_w4(0, "B")
+        gate_passes(0, 0)
+        v2_sc = held([P, S2], U8, "v2_sc", "C")
+        nc.vector.tensor_copy(v2_sc[:], tab2_sc[:].indirect(idx2[:]))
+        round_w1(1, 0, "D")
+        load_tab(2, "A2")
+        quantise_w1(1, 0)
+        load_w4(1, "D")
+        gather_tab(1, 1)
+        load_w1(0, 1, "B2")
+        gate_passes(1, 0)
+        round_w1(2, 0, "E")
+        load_w1(1, 1, "A")
+        quantise_w1(2, 0)
+        for a in range(K_PASSES - 1):
+            for jt in range(J_TILES):
+                value_pass(value_acc[jt], a, 0, jt)
+        gather_tab(2, 2, "E")
+        load_w1(2, 1, "A2")
+        both_passes(2)
+
+        next_value = []
+
+        def start_values(jt):
+            acc = bank(J_TILES + jt, [P, PASS])
+            next_value.append(acc)
+            for a in range(K_PASSES):
+                value_pass(acc, a, 1, jt)
+
+        finish_h(0, gate_acc, value_acc, start_values)
+        value_acc = next_value
+        gate_acc = [bank(jt, [P, PASS]) for jt in range(J_TILES)]
+        load_tab2(0, "gate01")
+        round_w1(0, 1, "gate00", vector_piece=256)
+        load_tab2(1, "B2")
+        round_w1(1, 1, "gate02", scalar_piece=128)
+        quantise_w1(0, 1)
+        round_w1(2, 1, "gate00")
+        quantise_w1(1, 1)
+        quantise_w1(2, 1)
+        for jt in range(J_TILES):
+            for a in range(K_PASSES):
+                gate_pass(gate_acc[jt], a, 1, jt)
+        finish_h(1, gate_acc, value_acc, lambda jt: None)
+
+        one = held([P, 1], F32, "one")
+        nc.scalar.activation(
+            one[:], h_grouped[1, J_TILES - 1][:, 0:1], ACT.Abs_reciprocal_sqrt, bias=1.0, scale=0.0
+        )
+
+        v2_w = {}
+        piece = S2 // 2
+
+        def contact_pass(acc, a, it):
+            cols = slice(P * it, P * (it + 1))
+            nc.tensor.matmul_mx(
+                out=acc[:],
+                lhsT=v2_w[a][:, cols].bitcast(FP8X4),
+                lhsT_scale=v2_sc[ROWS * (a + 1) : P, cols],
+                rhs=h_codes[a][:].bitcast(FP8X4),
+                rhs_scale=h_sc[a][:],
+                start=(a == 0),
+                stop=(a == R_PASSES - 1),
+            )
+
+        y_acc = [bank((J_TILES + it) % I_TILES, [P, S]) for it in range(I_TILES)]
+        for a, after in enumerate(("gate13", "gate01")):
+            v2_w[a] = held([P, S2], U32, "v2_w%d" % a, after)
+            for g in range(2):
+                nc.vector.tensor_copy(
+                    v2_w[a][:, piece * g : piece * (g + 1)],
+                    tab2_w[a][:].bitcast(U32).indirect(idx2[:, piece // 16 * g : piece // 16 * (g + 1)]),
+                )
+                for it in range(I_TILES // 2 * g, I_TILES // 2 * (g + 1)):
+                    contact_pass(y_acc[it], a, it)
+
+        pieces = [(it, 0, S) for it in range(I_TILES - 1)] + [(I_TILES - 1, 0, S // 2), (I_TILES - 1, S // 2, S)]
+        for it, c0, c1 in pieces:
+            y = y_acc[it][:, c0:c1]
+            x = ring.tile([P, c1 - c0], F32, name="x")
+            nc.scalar.activation(x[:], y, ACT.Square)
+            root = ring.tile([P, c1 - c0], F32, name="root")
+            nc.scalar.activation(root[:], x[:], ACT.Abs_reciprocal_sqrt, bias=one[:])
+            unit = ring.tile([P, c1 - c0], F32, name="unit")
+            nc.vector.tensor_tensor(unit[:], y, root[:], MULT)
+            strength = held([P, c1 - c0], F32, "strength%d_%d" % (it, c0))
+            nc.vector.tensor_tensor(strength[:], unit[:], unit[:], MULT)
+            nc.sync.dma_start(out[P * it : P * (it + 1), c0:c1], strength[:])

@@ -26,7 +26,7 @@ J_TILES = S // P
 I_TILES = S2 // P
 QUADS = 4
 ROWS = 4
-VECTOR_COLS = {(0, 0): 0, (1, 0): 0, (2, 0): 0, (0, 1): 512, (1, 1): 0, (2, 1): 320}
+VECTOR_COLS = {(0, 0): 0, (1, 0): 0, (2, 0): 192, (0, 1): 512, (1, 1): 0, (2, 1): 384}
 
 
 def tile_list_residue_contact_strength_kernel(
@@ -35,7 +35,7 @@ def tile_list_residue_contact_strength_kernel(
     nc = tc.nc
     with ExitStack() as ctx:
         keep = ctx.enter_context(tc.tile_pool(name="keep", bufs=1))
-        ring = ctx.enter_context(tc.tile_pool(name="ring", bufs=3))
+        ring = ctx.enter_context(tc.tile_pool(name="ring", bufs=4))
         psum = ctx.enter_context(tc.psum_pool(name="psum", bufs=1))
 
         def held(shape, dtype, name, after=None):
@@ -49,11 +49,9 @@ def tile_list_residue_contact_strength_kernel(
         nc.sync.dma_start(idx[:], offs)
 
         tab_sc = held([P, K_PASSES * T], U8, "tab_sc")
-        w4_sc = held([P, K_PASSES * H], U8, "w4_sc")
         tab2_sc = held([P, T2], U8, "tab2_sc")
         nc.vector.memset(tab_sc[:].bitcast(I32), 0)
         nc.gpsimd.memset(tab2_sc[:].bitcast(I32), 0)
-        nc.vector.memset(w4_sc[:].bitcast(I32), 0)
 
         def load_planes(queue, plane, scales):
             for q in range(QUADS):
@@ -91,24 +89,30 @@ def tile_list_residue_contact_strength_kernel(
         nc.sync.dma_start(idx2[:], offs2)
         load_w1(0, 0, "A")
         load_tab(0, "B")
-        load_w1(1, 0, "A2")
-        load_tab(1, "B2")
-        load_planes(nc.scalar, tab_sc, tab_scales)
+        load_planes(nc.sync, tab_sc, tab_scales)
         for q in range(QUADS):
             first = 32 * q + ROWS
             nc.gpsimd.dma_start(
                 tab2_sc[:].bitcast(I32)[first : first + R_PASSES * ROWS, :],
                 tab2_scales[:, ROWS * q : ROWS * (q + 1), :].bitcast(I32),
             )
-        load_planes(nc.gpsimd, w4_sc, w4_scales)
         identity = held([P, P], F32, "identity")
         make_identity(nc, identity[:])
 
         zero = held([P, 1], F32, "zero")
         gelu_bias = held([P, 1], F32, "gelu_bias")
         nc.vector.memset(zero[:], 0.0)
-        nc.scalar.activation(gelu_bias[:], zero[:], ACT.Gelu_apprx_tanh)
+        tw = held([P, 1], F32, "tw")
+        nc.vector.memset(tw[:], 0.0)
+        ts = held([P, 1], F32, "ts")
+        nc.vector.memset(ts[:], 1.0)
+        nc.scalar.activation(gelu_bias[:], zero[:], ACT.Gelu_apprx_tanh, bias=tw[:], scale=ts[:])
 
+        load_w1(1, 0, "zero")
+        load_tab(1, "tw")
+        w4_sc = held([P, K_PASSES * H], U8, "w4_sc", "ts")
+        nc.vector.memset(w4_sc[:].bitcast(I32), 0)
+        load_planes(nc.sync, w4_sc, w4_scales)
         w1_codes = {}
         w1_sc = {}
         w1_grouped = {}
@@ -196,37 +200,36 @@ def tile_list_residue_contact_strength_kernel(
             h_rows[half, jt] = held([P, 2, P, 2], BF16, "h_rows%d%d" % (half, jt))
             nc.vector.tensor_tensor(h_rows[half, jt][:], acc[:].rearrange(order, u=2, e=2), gates[half, jt][:], MULT)
 
+        turned = {}
+
         def turn(half, jt):
             words = h_rows[half, jt][:].rearrange("j u p e -> j (u p e)").bitcast(F32)
-            turned = bank(jt, [P, 2, P])
+            turned[half, jt] = bank(jt, [P, 2, P])
             for u in range(2):
-                nc.tensor.transpose(turned[:, u, :], words[:, P * u : P * (u + 1)], identity[:])
-            h_grouped[half, jt] = held([P, P * PACK], BF16, "h_grouped%d%d" % (half, jt))
+                nc.tensor.transpose(turned[half, jt][:, u, :], words[:, P * u : P * (u + 1)], identity[:])
+
+        def group_h(half, jt):
             nc.scalar.copy(
-                h_grouped[half, jt][:].bitcast(F32).rearrange("p (j u) -> p j u", u=2),
-                turned[:].rearrange("p u j -> p j u"),
+                h_grouped[half][:, PASS * jt : PASS * (jt + 1)].bitcast(F32).rearrange("p (j u) -> p j u", u=2),
+                turned[half, jt][:].rearrange("p u j -> p j u"),
             )
 
-        def quantise_h(half, jt):
-            cols = slice(P * jt, P * (jt + 1))
-            nc.vector.quantize_mx(
-                out=h_codes[half][:, cols].bitcast(FP8X4), scales=h_sc[half][:, cols], in_=h_grouped[half, jt][:]
-            )
+        def quantise_h(half, after):
+            h_codes[half] = held([P, S], U32, "h_codes%d" % half, after)
+            h_sc[half] = held([P, S], U8, "h_sc%d" % half)
+            nc.vector.quantize_mx(out=h_codes[half][:].bitcast(FP8X4), scales=h_sc[half][:], in_=h_grouped[half][:])
 
         def finish_h(half, gate_acc, value_acc, freed):
-            for step in range(J_TILES + 2):
-                if step < J_TILES:
-                    gelu(half, step, gate_acc[step])
-                    gated(half, step, value_acc[step])
-                if 1 <= step <= J_TILES:
-                    turn(half, step - 1)
-                    freed(step - 1)
-                if step >= 2:
-                    quantise_h(half, step - 2)
+            for jt in range(J_TILES):
+                gelu(half, jt, gate_acc[jt])
+                gated(half, jt, value_acc[jt])
+                turn(half, jt)
+            for jt in range(J_TILES):
+                group_h(half, jt)
+                freed(jt)
 
         for half in range(R_PASSES):
-            h_codes[half] = held([P, S], U32, "h_codes%d" % half)
-            h_sc[half] = held([P, S], U8, "h_sc%d" % half)
+            h_grouped[half] = held([P, S * PACK], BF16, "h_grouped%d" % half)
 
         gate_acc = [bank(jt, [P, PASS]) for jt in range(J_TILES)]
         value_acc = [bank(J_TILES + jt, [P, PASS]) for jt in range(J_TILES)]
@@ -240,31 +243,34 @@ def tile_list_residue_contact_strength_kernel(
             for jt in range(J_TILES):
                 gate_pass(gate_acc[jt], a, half, jt)
 
-        for a in range(K_PASSES):
-            gather_tab_scales(a)
-        round_w1(0, 0, "C")
-        load_w1(2, 0, "A")
-        quantise_w1(0, 0)
-        gather_tab(0, 1)
-        load_w4(0, "B")
-        gate_passes(0, 0)
-        v2_sc = held([P, S2], U8, "v2_sc", "C")
-        nc.vector.tensor_copy(v2_sc[:], tab2_sc[:].indirect(idx2[:]))
-        round_w1(1, 0, "D")
-        load_tab(2, "A2")
-        quantise_w1(1, 0)
-        load_w4(1, "D")
-        gather_tab(1, 1)
-        load_w1(0, 1, "B2")
-        gate_passes(1, 0)
-        round_w1(2, 0, "E")
-        load_w1(1, 1, "A")
-        quantise_w1(2, 0)
-        for a in range(K_PASSES - 1):
+        def value_passes(a):
             for jt in range(J_TILES):
                 value_pass(value_acc[jt], a, 0, jt)
+
+        round_w1(0, 0, "C")
+        load_w4(0, "A")
+        quantise_w1(0, 0)
+        gather_tab(0, 1)
+        load_w1(2, 0, "B")
+        for a in range(K_PASSES):
+            gather_tab_scales(a)
+        gate_passes(0, 0)
+        value_passes(0)
+        round_w1(1, 0, "D")
+        load_tab(2, "zero")
+        quantise_w1(1, 0)
+        load_w1(0, 1, "D")
+        gather_tab(1, 1)
+        gate_passes(1, 0)
+        value_passes(1)
+        v2_sc = held([P, S2], U8, "v2_sc", "tw")
+        nc.vector.tensor_copy(v2_sc[:], tab2_sc[:].indirect(idx2[:]))
+        load_w4(1, "tab2_sc")
+        round_w1(2, 0, "E")
+        load_w1(1, 1, "B")
+        quantise_w1(2, 0)
         gather_tab(2, 2, "E")
-        load_w1(2, 1, "A2")
+        load_w1(2, 1, "zero")
         both_passes(2)
 
         next_value = []
@@ -279,58 +285,90 @@ def tile_list_residue_contact_strength_kernel(
         value_acc = next_value
         gate_acc = [bank(jt, [P, PASS]) for jt in range(J_TILES)]
         load_tab2(0, "gate01")
-        round_w1(0, 1, "gate00", vector_piece=256)
-        load_tab2(1, "B2")
-        round_w1(1, 1, "gate02", scalar_piece=128)
+        round_w1(0, 1, "gate03")
+        load_tab2(1, "D")
+        w1_codes[1, 1] = held([P, PASS], U32, "w1_codes11")
+        w1_sc[1, 1] = held([P, PASS], U8, "w1_sc11")
+        parts = []
+        for g, after in enumerate(("h_rows02", "h_rows03")):
+            cols = slice(PASS // 2 * g, PASS // 2 * (g + 1))
+            part = held([P, PASS // 2, PACK], BF16, "w1_part%d" % g, after)
+            parts.append((cols, part))
+            nc.scalar.copy(
+                part[:].rearrange("p (c i) t -> p c t i", i=4),
+                w1_raw[1, 1][:, :, cols].rearrange("p t (c i) -> p c t i", i=4),
+            )
+
+        def quantise_part(cols, part):
+            nc.vector.quantize_mx(
+                out=w1_codes[1, 1][:, cols].bitcast(FP8X4),
+                scales=w1_sc[1, 1][:, cols],
+                in_=part[:].rearrange("p c t -> p (c t)"),
+            )
+
         quantise_w1(0, 1)
-        round_w1(2, 1, "gate00")
-        quantise_w1(1, 1)
+        quantise_part(*parts[0])
+        round_w1(2, 1, "gate03")
+        quantise_part(*parts[1])
         quantise_w1(2, 1)
+        quantise_h(0, "gate03")
         for jt in range(J_TILES):
             for a in range(K_PASSES):
                 gate_pass(gate_acc[jt], a, 1, jt)
         finish_h(1, gate_acc, value_acc, lambda jt: None)
+        quantise_h(1, None)
 
-        one = held([P, 1], F32, "one")
-        nc.scalar.activation(
-            one[:], h_grouped[1, J_TILES - 1][:, 0:1], ACT.Abs_reciprocal_sqrt, bias=1.0, scale=0.0
-        )
+        one = held([P, 1], F32, "one", "h_rows13")
+        nc.scalar.activation(one[:], gelu_bias[:], ACT.Abs_reciprocal_sqrt, bias=1.0)
 
         v2_w = {}
         piece = S2 // 2
+        y_acc = [bank((J_TILES + it) % I_TILES, [P, S]) for it in range(I_TILES)]
 
-        def contact_pass(acc, a, it):
-            cols = slice(P * it, P * (it + 1))
+        def gather_tab2(a, g, after):
+            v2_w[a, g] = held([P, piece], U32, "v2_w%d%d" % (a, g), after)
+            nc.vector.tensor_copy(
+                v2_w[a, g][:],
+                tab2_w[a][:].bitcast(U32).indirect(idx2[:, piece // 16 * g : piece // 16 * (g + 1)]),
+            )
+
+        def contact_pass(a, it):
+            g, first = divmod(P * it, piece)
             nc.tensor.matmul_mx(
-                out=acc[:],
-                lhsT=v2_w[a][:, cols].bitcast(FP8X4),
-                lhsT_scale=v2_sc[ROWS * (a + 1) : P, cols],
+                out=y_acc[it][:],
+                lhsT=v2_w[a, g][:, first : first + P].bitcast(FP8X4),
+                lhsT_scale=v2_sc[ROWS * (a + 1) : P, P * it : P * (it + 1)],
                 rhs=h_codes[a][:].bitcast(FP8X4),
                 rhs_scale=h_sc[a][:],
                 start=(a == 0),
                 stop=(a == R_PASSES - 1),
             )
 
-        y_acc = [bank((J_TILES + it) % I_TILES, [P, S]) for it in range(I_TILES)]
-        for a, after in enumerate(("gate13", "gate01")):
-            v2_w[a] = held([P, S2], U32, "v2_w%d" % a, after)
-            for g in range(2):
-                nc.vector.tensor_copy(
-                    v2_w[a][:, piece * g : piece * (g + 1)],
-                    tab2_w[a][:].bitcast(U32).indirect(idx2[:, piece // 16 * g : piece // 16 * (g + 1)]),
-                )
-                for it in range(I_TILES // 2 * g, I_TILES // 2 * (g + 1)):
-                    contact_pass(y_acc[it], a, it)
-
-        pieces = [(it, 0, S) for it in range(I_TILES - 1)] + [(I_TILES - 1, 0, S // 2), (I_TILES - 1, S // 2, S)]
-        for it, c0, c1 in pieces:
+        def strength(it, c0, c1, engine):
             y = y_acc[it][:, c0:c1]
-            x = ring.tile([P, c1 - c0], F32, name="x")
+            x = held([P, c1 - c0], F32, "x%d_%d" % (it, c0), "x%d" % (it % 3))
             nc.scalar.activation(x[:], y, ACT.Square)
             root = ring.tile([P, c1 - c0], F32, name="root")
             nc.scalar.activation(root[:], x[:], ACT.Abs_reciprocal_sqrt, bias=one[:])
             unit = ring.tile([P, c1 - c0], F32, name="unit")
             nc.vector.tensor_tensor(unit[:], y, root[:], MULT)
-            strength = held([P, c1 - c0], F32, "strength%d_%d" % (it, c0))
-            nc.vector.tensor_tensor(strength[:], unit[:], unit[:], MULT)
-            nc.sync.dma_start(out[P * it : P * (it + 1), c0:c1], strength[:])
+            result = held([P, c1 - c0], F32, "result%d_%d" % (it, c0))
+            engine.tensor_tensor(result[:], unit[:], unit[:], MULT)
+            nc.sync.dma_start(out[P * it : P * (it + 1), c0:c1], result[:])
+
+        half_tiles = I_TILES // 2
+        gather_tab2(0, 0, "gate13")
+        gather_tab2(0, 1, "h_grouped1")
+        for it in range(I_TILES):
+            contact_pass(0, it)
+        gather_tab2(1, 0, "gate01")
+        for it in range(half_tiles):
+            contact_pass(1, it)
+        gather_tab2(1, 1, "h_grouped1")
+        for it in range(half_tiles, I_TILES):
+            contact_pass(1, it)
+        strength(0, 0, S, nc.vector)
+        for it in range(1, I_TILES - 1):
+            strength(it, 0, S, nc.gpsimd if it < 0 else nc.vector)
+        strength(I_TILES - 1, 0, S // 2, nc.vector)
+        strength(I_TILES - 1, S // 2, S, nc.vector)

@@ -54,10 +54,10 @@ def tile_list_residue_contact_strength_kernel(
         nc.gpsimd.memset(tab2_sc[:].bitcast(I32), 0)
 
         def load_planes(queue, plane, scales):
-            for q in range(QUADS):
+            for r in range(ROWS):
                 queue.dma_start(
-                    plane[:].bitcast(I32)[32 * q : 32 * q + ROWS, :].rearrange("r (a w) -> r a w", a=K_PASSES),
-                    scales[:, ROWS * q : ROWS * (q + 1), :].rearrange("a r t -> r a t").bitcast(I32),
+                    plane[:].bitcast(I32)[r:P:32, :].rearrange("q (a w) -> q a w", a=K_PASSES),
+                    scales.rearrange("a (q r) t -> r q a t", r=ROWS)[r].bitcast(I32),
                 )
 
         w1_raw = {}

@@ -26,7 +26,17 @@ J_TILES = S // P
 I_TILES = S2 // P
 QUADS = 4
 ROWS = 4
-VECTOR_COLS = {(0, 0): 0, (1, 0): 0, (2, 0): 192, (0, 1): 512, (1, 1): 0, (2, 1): 384}
+KIB = 1024
+W1_AT = {(0, 0): 0, (1, 0): 8 * KIB, (2, 0): 59 * KIB, (0, 1): 35 * KIB, (1, 1): 43 * KIB, (2, 1): 51 * KIB}
+TAB_AT = [24 * KIB, 16 * KIB, 67 * KIB]
+FIRST_WAVE_AT = 16 * KIB
+W4_AT = [32 * KIB, 75 * KIB]
+TAB2_AT = [78 * KIB, 94 * KIB]
+SECOND_WAVE_AT = 35 * KIB
+LOADS_END = 110 * KIB
+SHIFTED_ROWS = 112
+HG1_AT = 110 * KIB
+VECTOR_COLS = {(0, 0): 0, (1, 0): 0, (2, 0): 0, (0, 1): 256, (1, 1): 256, (2, 1): 320}
 
 
 def tile_list_residue_contact_strength_kernel(
@@ -35,11 +45,14 @@ def tile_list_residue_contact_strength_kernel(
     nc = tc.nc
     with ExitStack() as ctx:
         keep = ctx.enter_context(tc.tile_pool(name="keep", bufs=1))
-        ring = ctx.enter_context(tc.tile_pool(name="ring", bufs=4))
+        stage = ctx.enter_context(tc.tile_pool(name="stage", bufs=1))
         psum = ctx.enter_context(tc.psum_pool(name="psum", bufs=1))
 
         def held(shape, dtype, name, after=None):
             return keep.tile(shape, dtype, name=name, tag=after or name, align_bytes=64)
+
+        def placed(shape, dtype, name, at):
+            return stage.tile(shape, dtype, name=name, tag=name, align_bytes=64, offset=at)
 
         def bank(number, shape):
             return psum.tile(shape, F32, name="bank%d" % number, tag="bank%d" % number)
@@ -47,10 +60,11 @@ def tile_list_residue_contact_strength_kernel(
         idx = keep.tile([P, S // 16], U16, name="idx")
         idx2 = keep.tile([P, S2 // 16], U16, name="idx2")
         nc.sync.dma_start(idx[:], offs)
+        nc.sync.dma_start(idx2[:], offs2)
 
-        tab_sc = held([P, K_PASSES * T], U8, "tab_sc")
+        tab_sc = placed([P, LOADS_END - SECOND_WAVE_AT], U8, "tab_sc", SECOND_WAVE_AT)
         tab2_sc = held([P, T2], U8, "tab2_sc")
-        nc.vector.memset(tab_sc[:].bitcast(I32), 0)
+        nc.vector.memset(tab_sc[:, :T].bitcast(I32), 0)
         nc.gpsimd.memset(tab2_sc[:].bitcast(I32), 0)
 
         def load_planes(queue, plane, scales):
@@ -63,33 +77,35 @@ def tile_list_residue_contact_strength_kernel(
         w1_raw = {}
         tab_w = {}
         tab2_w = {}
+        w4 = {}
 
-        def load_w1(a, half, after):
-            w1_raw[a, half] = held([P, PACK, PASS], F32, "w1_raw%d%d" % (a, half), after)
+        def load_w1(a, half):
+            w1_raw[a, half] = placed([P, PACK, PASS], F32, "w1_raw%d%d" % (a, half), W1_AT[a, half])
             rows = w1[PASS * a : PASS * (a + 1), PASS * half : PASS * (half + 1)]
             nc.sync.dma_start(w1_raw[a, half][:], rows.rearrange("(p t) c -> p t c", t=PACK))
 
-        w4 = {}
-
-        def load_w4(half, after):
-            w4[half] = held([P, K_PASSES * 2 * PASS], U8, "w4_%d" % half, after)
+        def load_w4(half):
+            w4[half] = placed([P, K_PASSES * 2 * PASS], U8, "w4_%d" % half, W4_AT[half])
             nc.sync.dma_start(
                 w4[half][:].bitcast(I32).rearrange("p (a w) -> p a w", a=K_PASSES),
                 w4_words[:, :, 2 * PASS * half : 2 * PASS * (half + 1)].rearrange("a p c -> p a c").bitcast(I32),
             )
 
-        def load_tab(a, after):
-            tab_w[a] = held([P, T], I32, "tab_w%d" % a, after)
+        def load_tab(a):
+            tab_w[a] = placed([P, T], I32, "tab_w%d" % a, TAB_AT[a])
             nc.sync.dma_start(tab_w[a][:], tab_words[a].rearrange("p t i -> p (t i)").bitcast(I32))
 
-        def load_tab2(a, after):
-            tab2_w[a] = held([P, T2], I32, "tab2_w%d" % a, after)
+        def load_tab2(a):
+            tab2_w[a] = placed([P, T2], I32, "tab2_w%d" % a, TAB2_AT[a])
             nc.sync.dma_start(tab2_w[a][:], tab2_words[a].rearrange("p t i -> p (t i)").bitcast(I32))
 
-        nc.sync.dma_start(idx2[:], offs2)
-        load_w1(0, 0, "A")
-        load_tab(0, "B")
-        load_planes(nc.sync, tab_sc, tab_scales)
+        load_w1(0, 0)
+        load_w1(1, 0)
+        for q in range(QUADS):
+            nc.scalar.dma_start(
+                tab_sc[32 * q : 32 * q + K_PASSES * ROWS, :T].bitcast(I32),
+                tab_scales[:, ROWS * q : ROWS * (q + 1), :].bitcast(I32),
+            )
         for q in range(QUADS):
             first = 32 * q + ROWS
             nc.gpsimd.dma_start(
@@ -99,42 +115,64 @@ def tile_list_residue_contact_strength_kernel(
         identity = held([P, P], F32, "identity")
         make_identity(nc, identity[:])
 
-        zero = held([P, 1], F32, "zero")
-        gelu_bias = held([P, 1], F32, "gelu_bias")
-        nc.vector.memset(zero[:], 0.0)
-        tw = held([P, 1], F32, "tw")
-        nc.vector.memset(tw[:], 0.0)
-        ts = held([P, 1], F32, "ts")
-        nc.vector.memset(ts[:], 1.0)
-        nc.scalar.activation(gelu_bias[:], zero[:], ACT.Gelu_apprx_tanh, bias=tw[:], scale=ts[:])
+        zero = placed([P, (SECOND_WAVE_AT - FIRST_WAVE_AT) // 4], F32, "zero", FIRST_WAVE_AT)
+        nc.vector.memset(zero[:, 0:1], 0.0)
+        origin = held([P, 1], F32, "origin")
+        nc.vector.memset(origin[:], 0.0)
+        gelu_bias = [held([P, 1], F32, "first_bias"), origin]
+        ones = held([P, 1], F32, "ones")
+        nc.vector.memset(ones[:], 1.0)
+        nc.scalar.activation(gelu_bias[0][:], zero[:, 0:1], ACT.Gelu_apprx_tanh, scale=ones[:])
 
-        load_w1(1, 0, "zero")
-        load_tab(1, "tw")
-        w4_sc = held([P, K_PASSES * H], U8, "w4_sc", "ts")
+        load_tab(0)
+        load_w4(0)
+        w4_sc = held([P, K_PASSES * H], U8, "w4_sc", "ones")
         nc.vector.memset(w4_sc[:].bitcast(I32), 0)
         load_planes(nc.sync, w4_sc, w4_scales)
+        load_tab(1)
+        v_planes = held([P, S], U8, "v_planes")
+        nc.vector.tensor_copy(v_planes[:], tab_sc[:, :T].indirect(idx[:]))
+        v_sc = {0: v_planes}
+        for a in range(1, K_PASSES):
+            v_sc[a] = held([P, S], U8, "v_sc%d" % a)
+            nc.vector.memset(v_sc[a][:].bitcast(I32), 0)
+            nc.sync.dma_start(
+                v_sc[a][:SHIFTED_ROWS, :].bitcast(I32),
+                v_planes[ROWS * a : ROWS * a + SHIFTED_ROWS, :].bitcast(I32),
+            )
+        load_w1(2, 0)
+        load_tab(2)
+        load_w1(0, 1)
+        load_w4(1)
+        load_w1(1, 1)
+        load_w1(2, 1)
+        load_tab2(0)
+        load_tab2(1)
+
         w1_codes = {}
         w1_sc = {}
         w1_grouped = {}
 
-        def round_w1(a, half, after, vector_piece=PASS, scalar_piece=PASS):
-            grouped = held([P, PASS, PACK], BF16, "w1_grouped%d%d" % (a, half), after)
+        def interleaved(grouped, raw):
+            return grouped.rearrange("p (c i) t -> p c t i", i=4), raw.rearrange("p t (c i) -> p c t i", i=4)
+
+        def round_w1(a, half, after):
+            name = "w1_grouped%d%d" % (a, half)
+            if isinstance(after, int):
+                grouped = placed([P, PASS, PACK], BF16, name, after)
+            else:
+                grouped = held([P, PASS, PACK], BF16, name, after)
             w1_grouped[a, half] = grouped
             split = VECTOR_COLS[a, half]
             raw = w1_raw[a, half]
+            if split > 0:
+                nc.vector.tensor_copy(*interleaved(grouped[:, :split, :], raw[:, :, :split]))
+            if split < PASS:
+                nc.scalar.copy(*interleaved(grouped[:, split:, :], raw[:, :, split:]))
 
-            def views(c0, c1):
-                dst = grouped[:, c0:c1, :].rearrange("p (c i) t -> p c t i", i=4)
-                src = raw[:, :, c0:c1].rearrange("p t (c i) -> p c t i", i=4)
-                return dst, src
-
-            for c0 in range(0, split, vector_piece):
-                nc.vector.tensor_copy(*views(c0, min(split, c0 + vector_piece)))
-            for c0 in range(split, PASS, scalar_piece):
-                nc.scalar.copy(*views(c0, min(PASS, c0 + scalar_piece)))
-
-        def quantise_w1(a, half):
-            w1_codes[a, half] = held([P, PASS], U32, "w1_codes%d%d" % (a, half))
+        def quantise_w1(a, half, at=None):
+            name = "w1_codes%d%d" % (a, half)
+            w1_codes[a, half] = held([P, PASS], U32, name) if at is None else placed([P, PASS], U32, name, at)
             w1_sc[a, half] = held([P, PASS], U8, "w1_sc%d%d" % (a, half))
             nc.vector.quantize_mx(
                 out=w1_codes[a, half][:].bitcast(FP8X4),
@@ -143,27 +181,18 @@ def tile_list_residue_contact_strength_kernel(
             )
 
         v_w = {}
-        v_sc = {}
 
-        def gather_tab_scales(a):
-            v_sc[a] = held([P, S], U8, "v_sc%d" % a)
-            nc.vector.tensor_copy(v_sc[a][:], tab_sc[:, T * a : T * (a + 1)].indirect(idx[:]))
-
-        def gather_tab(a, pieces, after=None):
-            v_w[a] = held([P, S], U32, "v_w%d" % a, after)
-            n = S // pieces
-            for g in range(pieces):
-                nc.vector.tensor_copy(
-                    v_w[a][:, n * g : n * (g + 1)],
-                    tab_w[a][:].bitcast(U32).indirect(idx[:, n // 16 * g : n // 16 * (g + 1)]),
-                )
+        def gather_tab(a, c0, c1, after=None):
+            if c0 == 0:
+                v_w[a] = held([P, S], U32, "v_w%d" % a, after)
+            nc.vector.tensor_copy(v_w[a][:, c0:c1], tab_w[a][:].bitcast(U32).indirect(idx[:, c0 // 16 : c1 // 16]))
 
         def gate_pass(acc, a, half, jt):
             cols = slice(P * jt, P * (jt + 1))
             nc.tensor.matmul_mx(
                 out=acc[:],
                 lhsT=v_w[a][:, cols].bitcast(FP8X4),
-                lhsT_scale=v_sc[a][:, cols],
+                lhsT_scale=v_planes[ROWS * a : P, cols],
                 rhs=w1_codes[a, half][:].bitcast(FP8X4),
                 rhs_scale=w1_sc[a, half][:],
                 start=(a == 0),
@@ -188,19 +217,18 @@ def tile_list_residue_contact_strength_kernel(
         gates = {}
         h_rows = {}
         h_grouped = {}
+        turned = {}
         order = "j (p u e) -> j u p e"
 
         def gelu(half, jt, acc):
             gates[half, jt] = held([P, 2, P, 2], F32, "gate%d%d" % (half, jt))
             nc.scalar.activation(
-                gates[half, jt][:], acc[:].rearrange(order, u=2, e=2), ACT.Gelu_apprx_tanh, bias=gelu_bias[:]
+                gates[half, jt][:], acc[:].rearrange(order, u=2, e=2), ACT.Gelu_apprx_tanh, bias=gelu_bias[half][:]
             )
 
         def gated(half, jt, acc):
             h_rows[half, jt] = held([P, 2, P, 2], BF16, "h_rows%d%d" % (half, jt))
             nc.vector.tensor_tensor(h_rows[half, jt][:], acc[:].rearrange(order, u=2, e=2), gates[half, jt][:], MULT)
-
-        turned = {}
 
         def turn(half, jt):
             words = h_rows[half, jt][:].rearrange("j u p e -> j (u p e)").bitcast(F32)
@@ -219,25 +247,11 @@ def tile_list_residue_contact_strength_kernel(
             h_sc[half] = held([P, S], U8, "h_sc%d" % half)
             nc.vector.quantize_mx(out=h_codes[half][:].bitcast(FP8X4), scales=h_sc[half][:], in_=h_grouped[half][:])
 
-        def finish_h(half, gate_acc, value_acc, freed):
-            for jt in range(J_TILES):
-                gelu(half, jt, gate_acc[jt])
-                gated(half, jt, value_acc[jt])
-                turn(half, jt)
-            for jt in range(J_TILES):
-                group_h(half, jt)
-                freed(jt)
-
-        for half in range(R_PASSES):
-            h_grouped[half] = held([P, S * PACK], BF16, "h_grouped%d" % half)
+        h_grouped[0] = held([P, S * PACK], BF16, "h_grouped0")
+        h_grouped[1] = placed([P, S * PACK], BF16, "h_grouped1", HG1_AT)
 
         gate_acc = [bank(jt, [P, PASS]) for jt in range(J_TILES)]
         value_acc = [bank(J_TILES + jt, [P, PASS]) for jt in range(J_TILES)]
-
-        def both_passes(a):
-            for jt in range(J_TILES):
-                gate_pass(gate_acc[jt], a, 0, jt)
-                value_pass(value_acc[jt], a, 0, jt)
 
         def gate_passes(a, half):
             for jt in range(J_TILES):
@@ -247,31 +261,25 @@ def tile_list_residue_contact_strength_kernel(
             for jt in range(J_TILES):
                 value_pass(value_acc[jt], a, 0, jt)
 
-        round_w1(0, 0, "C")
-        load_w4(0, "A")
+        round_w1(0, 0, None)
+        round_w1(1, 0, None)
+        round_w1(2, 0, None)
         quantise_w1(0, 0)
-        gather_tab(0, 1)
-        load_w1(2, 0, "B")
-        for a in range(K_PASSES):
-            gather_tab_scales(a)
+        gather_tab(0, 0, S, "w1_grouped00")
+        quantise_w1(1, 0)
         gate_passes(0, 0)
         value_passes(0)
-        round_w1(1, 0, "D")
-        load_tab(2, "zero")
-        quantise_w1(1, 0)
-        load_w1(0, 1, "D")
-        gather_tab(1, 1)
+        gather_tab(1, 0, S, "w1_grouped10")
         gate_passes(1, 0)
         value_passes(1)
-        v2_sc = held([P, S2], U8, "v2_sc", "tw")
+        v2_sc = placed([P, S2], U8, "v2_sc", TAB_AT[1] + 4 * KIB)
         nc.vector.tensor_copy(v2_sc[:], tab2_sc[:].indirect(idx2[:]))
-        load_w4(1, "tab2_sc")
-        round_w1(2, 0, "E")
-        load_w1(1, 1, "B")
-        quantise_w1(2, 0)
-        gather_tab(2, 2, "E")
-        load_w1(2, 1, "zero")
-        both_passes(2)
+        gather_tab(2, 0, S // 2, "tab2_sc")
+        quantise_w1(2, 0, TAB_AT[1] + 6 * KIB)
+        gather_tab(2, S // 2, S)
+        for jt in range(J_TILES):
+            gate_pass(gate_acc[jt], 2, 0, jt)
+            value_pass(value_acc[jt], 2, 0, jt)
 
         next_value = []
 
@@ -281,94 +289,107 @@ def tile_list_residue_contact_strength_kernel(
             for a in range(K_PASSES):
                 value_pass(acc, a, 1, jt)
 
-        finish_h(0, gate_acc, value_acc, start_values)
+        for jt in range(J_TILES):
+            gelu(0, jt, gate_acc[jt])
+        for jt in range(J_TILES):
+            gated(0, jt, value_acc[jt])
+        round_w1(0, 1, "first_bias")
+        quantise_w1(0, 1)
+        round_w1(1, 1, W1_AT[0, 1])
+        for jt in range(J_TILES - 1):
+            start_values(jt)
+        for jt in range(J_TILES):
+            turn(0, jt)
+        start_values(J_TILES - 1)
+        for jt in range(J_TILES):
+            group_h(0, jt)
         value_acc = next_value
         gate_acc = [bank(jt, [P, PASS]) for jt in range(J_TILES)]
-        load_tab2(0, "gate01")
-        round_w1(0, 1, "gate03")
-        load_tab2(1, "D")
-        w1_codes[1, 1] = held([P, PASS], U32, "w1_codes11")
-        w1_sc[1, 1] = held([P, PASS], U8, "w1_sc11")
-        parts = []
-        for g, after in enumerate(("h_rows02", "h_rows03")):
-            cols = slice(PASS // 2 * g, PASS // 2 * (g + 1))
-            part = held([P, PASS // 2, PACK], BF16, "w1_part%d" % g, after)
-            parts.append((cols, part))
-            nc.scalar.copy(
-                part[:].rearrange("p (c i) t -> p c t i", i=4),
-                w1_raw[1, 1][:, :, cols].rearrange("p t (c i) -> p c t i", i=4),
-            )
-
-        def quantise_part(cols, part):
-            nc.vector.quantize_mx(
-                out=w1_codes[1, 1][:, cols].bitcast(FP8X4),
-                scales=w1_sc[1, 1][:, cols],
-                in_=part[:].rearrange("p c t -> p (c t)"),
-            )
-
-        quantise_w1(0, 1)
-        quantise_part(*parts[0])
-        round_w1(2, 1, "gate03")
-        quantise_part(*parts[1])
+        quantise_w1(1, 1)
+        round_w1(2, 1, "h_rows03")
         quantise_w1(2, 1)
-        quantise_h(0, "gate03")
         for jt in range(J_TILES):
             for a in range(K_PASSES):
                 gate_pass(gate_acc[jt], a, 1, jt)
-        finish_h(1, gate_acc, value_acc, lambda jt: None)
-        quantise_h(1, None)
-
-        one = held([P, 1], F32, "one", "h_rows13")
-        nc.scalar.activation(one[:], gelu_bias[:], ACT.Abs_reciprocal_sqrt, bias=1.0)
-
+        quantise_h(0, "h_rows03")
         v2_w = {}
         piece = S2 // 2
-        y_acc = [bank((J_TILES + it) % I_TILES, [P, S]) for it in range(I_TILES)]
 
-        def gather_tab2(a, g, after):
-            v2_w[a, g] = held([P, piece], U32, "v2_w%d%d" % (a, g), after)
+        def gather_tab2(a, g, tile):
+            v2_w[a, g] = tile
             nc.vector.tensor_copy(
-                v2_w[a, g][:],
+                tile[:],
                 tab2_w[a][:].bitcast(U32).indirect(idx2[:, piece // 16 * g : piece // 16 * (g + 1)]),
             )
 
-        def contact_pass(a, it):
-            g, first = divmod(P * it, piece)
-            nc.tensor.matmul_mx(
-                out=y_acc[it][:],
-                lhsT=v2_w[a, g][:, first : first + P].bitcast(FP8X4),
-                lhsT_scale=v2_sc[ROWS * (a + 1) : P, P * it : P * (it + 1)],
-                rhs=h_codes[a][:].bitcast(FP8X4),
-                rhs_scale=h_sc[a][:],
-                start=(a == 0),
-                stop=(a == R_PASSES - 1),
-            )
+        gather_tab2(0, 0, held([P, piece], U32, "v2_w00", "h_grouped0"))
+        for jt in range(J_TILES):
+            gelu(1, jt, gate_acc[jt])
+        for jt in range(J_TILES):
+            gated(1, jt, value_acc[jt])
+            turn(1, jt)
+        for jt in range(J_TILES):
+            group_h(1, jt)
 
-        def strength(it, c0, c1, engine):
-            y = y_acc[it][:, c0:c1]
-            x = held([P, c1 - c0], F32, "x%d_%d" % (it, c0), "x%d" % (it % 3))
-            nc.scalar.activation(x[:], y, ACT.Square)
-            root = ring.tile([P, c1 - c0], F32, name="root")
-            nc.scalar.activation(root[:], x[:], ACT.Abs_reciprocal_sqrt, bias=one[:])
-            unit = ring.tile([P, c1 - c0], F32, name="unit")
-            nc.vector.tensor_tensor(unit[:], y, root[:], MULT)
-            result = held([P, c1 - c0], F32, "result%d_%d" % (it, c0))
-            engine.tensor_tensor(result[:], unit[:], unit[:], MULT)
+        one = held([P, 1], F32, "one", "h_rows13")
+        nc.scalar.activation(one[:], origin[:], ACT.Abs_reciprocal_sqrt, bias=1.0)
+
+        y_acc = [bank((J_TILES + it) % I_TILES, [P, S]) for it in range(I_TILES)]
+
+        def contact_passes(a, g):
+            for it in range(I_TILES // 2 * g, I_TILES // 2 * (g + 1)):
+                first = P * it - piece * g
+                nc.tensor.matmul_mx(
+                    out=y_acc[it][:],
+                    lhsT=v2_w[a, g][:, first : first + P].bitcast(FP8X4),
+                    lhsT_scale=v2_sc[ROWS * (a + 1) : P, P * it : P * (it + 1)],
+                    rhs=h_codes[a][:].bitcast(FP8X4),
+                    rhs_scale=h_sc[a][:],
+                    start=(a == 0),
+                    stop=(a == R_PASSES - 1),
+                )
+
+        gather_tab2(0, 1, held([P, piece], U32, "v2_w01", "gate13"))
+        quantise_h(1, None)
+        contact_passes(0, 0)
+        contact_passes(0, 1)
+        gather_tab2(1, 0, placed([P, piece], U32, "v2_w10", HG1_AT + 2 * KIB))
+        contact_passes(1, 0)
+        gather_tab2(1, 1, placed([P, piece], U32, "v2_w11", HG1_AT))
+        contact_passes(1, 1)
+
+        pieces = [(it, 0, S) for it in range(I_TILES - 1)] + [(I_TILES - 1, 0, S // 2), (I_TILES - 1, S // 2, S)]
+        squares = {}
+        roots = {}
+        units = {}
+
+        def scratch(kind, n, first, depth):
+            it, c0, c1 = pieces[n]
+            return placed([P, c1 - c0], F32, "%s%d" % (kind, n), first + 2 * KIB * (n % depth))
+
+        def square(n):
+            it, c0, c1 = pieces[n]
+            squares[n] = scratch("x", n, W1_AT[0, 1], 4)
+            nc.scalar.activation(squares[n][:], y_acc[it][:, c0:c1], ACT.Square)
+
+        def root(n):
+            roots[n] = scratch("root", n, W1_AT[1, 1], 4)
+            nc.scalar.activation(roots[n][:], squares[n][:], ACT.Abs_reciprocal_sqrt, bias=one[:])
+
+        def unit(n):
+            it, c0, c1 = pieces[n]
+            units[n] = scratch("unit", n, W1_AT[2, 1], 4)
+            nc.vector.tensor_tensor(units[n][:], y_acc[it][:, c0:c1], roots[n][:], MULT)
+
+        def strength(n):
+            it, c0, c1 = pieces[n]
+            result = scratch("result", n, W1_AT[0, 0], len(pieces))
+            engine = nc.gpsimd if n < 4 else nc.vector
+            engine.tensor_tensor(result[:], units[n][:], units[n][:], MULT)
             nc.sync.dma_start(out[P * it : P * (it + 1), c0:c1], result[:])
 
-        half_tiles = I_TILES // 2
-        gather_tab2(0, 0, "gate13")
-        gather_tab2(0, 1, "h_grouped1")
-        for it in range(I_TILES):
-            contact_pass(0, it)
-        gather_tab2(1, 0, "gate01")
-        for it in range(half_tiles):
-            contact_pass(1, it)
-        gather_tab2(1, 1, "h_grouped1")
-        for it in range(half_tiles, I_TILES):
-            contact_pass(1, it)
-        strength(0, 0, S, nc.vector)
-        for it in range(1, I_TILES - 1):
-            strength(it, 0, S, nc.gpsimd if it < 0 else nc.vector)
-        strength(I_TILES - 1, 0, S // 2, nc.vector)
-        strength(I_TILES - 1, S // 2, S, nc.vector)
+        steps = (square, root, unit, strength)
+        for time in range(len(pieces) + len(steps) - 1):
+            for lag, step in enumerate(steps):
+                if 0 <= time - lag < len(pieces):
+                    step(time - lag)

@@ -36,7 +36,7 @@ SECOND_WAVE_AT = 35 * KIB
 LOADS_END = 110 * KIB
 SHIFTED_ROWS = 112
 HG1_AT = 110 * KIB
-VECTOR_COLS = {(0, 0): 0, (1, 0): 0, (2, 0): 0, (0, 1): 256, (1, 1): 256, (2, 1): 320}
+VECTOR_COLS = {(0, 0): 0, (1, 0): 0, (2, 0): 192, (0, 1): 256, (1, 1): 256, (2, 1): 512}
 
 
 def tile_list_residue_contact_strength_kernel(
@@ -59,8 +59,6 @@ def tile_list_residue_contact_strength_kernel(
 
         idx = keep.tile([P, S // 16], U16, name="idx")
         idx2 = keep.tile([P, S2 // 16], U16, name="idx2")
-        nc.sync.dma_start(idx[:], offs)
-        nc.sync.dma_start(idx2[:], offs2)
 
         tab_sc = placed([P, LOADS_END - SECOND_WAVE_AT], U8, "tab_sc", SECOND_WAVE_AT)
         tab2_sc = held([P, T2], U8, "tab2_sc")
@@ -100,6 +98,8 @@ def tile_list_residue_contact_strength_kernel(
             nc.sync.dma_start(tab2_w[a][:], tab2_words[a].rearrange("p t i -> p (t i)").bitcast(I32))
 
         load_w1(0, 0)
+        nc.sync.dma_start(idx[:], offs)
+        nc.sync.dma_start(idx2[:], offs2)
         load_w1(1, 0)
         for q in range(QUADS):
             nc.scalar.dma_start(
@@ -154,7 +154,7 @@ def tile_list_residue_contact_strength_kernel(
         w1_grouped = {}
 
         def interleaved(grouped, raw):
-            return grouped.rearrange("p (c i) t -> p c t i", i=4), raw.rearrange("p t (c i) -> p c t i", i=4)
+            return grouped.rearrange("p (c i) t -> p c t i", i=2), raw.rearrange("p t (c i) -> p c t i", i=2)
 
         def round_w1(a, half, after):
             name = "w1_grouped%d%d" % (a, half)
@@ -184,10 +184,11 @@ def tile_list_residue_contact_strength_kernel(
 
         def gather_tab(a, c0, c1, after=None):
             if c0 == 0:
-                v_w[a] = held([P, S], U32, "v_w%d" % a, after)
+                name = "v_w%d" % a
+                v_w[a] = placed([P, S], U32, name, after) if isinstance(after, int) else held([P, S], U32, name, after)
             nc.vector.tensor_copy(v_w[a][:, c0:c1], tab_w[a][:].bitcast(U32).indirect(idx[:, c0 // 16 : c1 // 16]))
 
-        def gate_pass(acc, a, half, jt):
+        def gate_pass(acc, a, half, jt, passes=(0, 1, 2)):
             cols = slice(P * jt, P * (jt + 1))
             nc.tensor.matmul_mx(
                 out=acc[:],
@@ -195,8 +196,8 @@ def tile_list_residue_contact_strength_kernel(
                 lhsT_scale=v_planes[ROWS * a : P, cols],
                 rhs=w1_codes[a, half][:].bitcast(FP8X4),
                 rhs_scale=w1_sc[a, half][:],
-                start=(a == 0),
-                stop=(a == K_PASSES - 1),
+                start=(a == passes[0]),
+                stop=(a == passes[-1]),
             )
 
         def value_pass(acc, a, half, jt):
@@ -247,7 +248,7 @@ def tile_list_residue_contact_strength_kernel(
             h_sc[half] = held([P, S], U8, "h_sc%d" % half)
             nc.vector.quantize_mx(out=h_codes[half][:].bitcast(FP8X4), scales=h_sc[half][:], in_=h_grouped[half][:])
 
-        h_grouped[0] = held([P, S * PACK], BF16, "h_grouped0")
+        h_grouped[0] = placed([P, S * PACK], BF16, "h_grouped0", W1_AT[1, 1])
         h_grouped[1] = placed([P, S * PACK], BF16, "h_grouped1", HG1_AT)
 
         gate_acc = [bank(jt, [P, PASS]) for jt in range(J_TILES)]
@@ -263,19 +264,25 @@ def tile_list_residue_contact_strength_kernel(
 
         round_w1(0, 0, None)
         round_w1(1, 0, None)
-        round_w1(2, 0, None)
+        piece = S2 // 2
+        v2_sc = {}
+
+        def gather_tab2_scales(g, at):
+            v2_sc[g] = placed([P, piece], U8, "v2_sc%d" % g, at)
+            nc.vector.tensor_copy(v2_sc[g][:], tab2_sc[:].indirect(idx2[:, piece // 16 * g : piece // 16 * (g + 1)]))
         quantise_w1(0, 0)
         gather_tab(0, 0, S, "w1_grouped00")
         quantise_w1(1, 0)
         gate_passes(0, 0)
         value_passes(0)
+        gather_tab2_scales(0, TAB_AT[0])
         gather_tab(1, 0, S, "w1_grouped10")
         gate_passes(1, 0)
         value_passes(1)
-        v2_sc = placed([P, S2], U8, "v2_sc", TAB_AT[1] + 4 * KIB)
-        nc.vector.tensor_copy(v2_sc[:], tab2_sc[:].indirect(idx2[:]))
-        gather_tab(2, 0, S // 2, "tab2_sc")
-        quantise_w1(2, 0, TAB_AT[1] + 6 * KIB)
+        gather_tab2_scales(1, TAB_AT[1] + 4 * KIB)
+        round_w1(2, 0, TAB_AT[1])
+        quantise_w1(2, 0)
+        gather_tab(2, 0, S // 2, TAB_AT[1] + 2 * KIB)
         gather_tab(2, S // 2, S)
         for jt in range(J_TILES):
             gate_pass(gate_acc[jt], 2, 0, jt)
@@ -308,12 +315,11 @@ def tile_list_residue_contact_strength_kernel(
         quantise_w1(1, 1)
         round_w1(2, 1, "h_rows03")
         quantise_w1(2, 1)
-        for jt in range(J_TILES):
-            for a in range(K_PASSES):
-                gate_pass(gate_acc[jt], a, 1, jt)
+        for jt, passes in enumerate(((0, 1, 2), (0, 1, 2), (0, 2, 1), (2, 0, 1))):
+            for a in passes:
+                gate_pass(gate_acc[jt], a, 1, jt, passes)
         quantise_h(0, "h_rows03")
         v2_w = {}
-        piece = S2 // 2
 
         def gather_tab2(a, g, tile):
             v2_w[a, g] = tile
@@ -322,7 +328,6 @@ def tile_list_residue_contact_strength_kernel(
                 tab2_w[a][:].bitcast(U32).indirect(idx2[:, piece // 16 * g : piece // 16 * (g + 1)]),
             )
 
-        gather_tab2(0, 0, held([P, piece], U32, "v2_w00", "h_grouped0"))
         for jt in range(J_TILES):
             gelu(1, jt, gate_acc[jt])
         for jt in range(J_TILES):
@@ -342,20 +347,21 @@ def tile_list_residue_contact_strength_kernel(
                 nc.tensor.matmul_mx(
                     out=y_acc[it][:],
                     lhsT=v2_w[a, g][:, first : first + P].bitcast(FP8X4),
-                    lhsT_scale=v2_sc[ROWS * (a + 1) : P, P * it : P * (it + 1)],
+                    lhsT_scale=v2_sc[g][ROWS * (a + 1) : P, first : first + P],
                     rhs=h_codes[a][:].bitcast(FP8X4),
                     rhs_scale=h_sc[a][:],
                     start=(a == 0),
                     stop=(a == R_PASSES - 1),
                 )
 
-        gather_tab2(0, 1, held([P, piece], U32, "v2_w01", "gate13"))
+        gather_tab2(0, 0, held([P, piece], U32, "v2_w00", "gate13"))
         quantise_h(1, None)
         contact_passes(0, 0)
+        gather_tab2(0, 1, placed([P, piece], U32, "v2_w01", HG1_AT))
         contact_passes(0, 1)
         gather_tab2(1, 0, placed([P, piece], U32, "v2_w10", HG1_AT + 2 * KIB))
         contact_passes(1, 0)
-        gather_tab2(1, 1, placed([P, piece], U32, "v2_w11", HG1_AT))
+        gather_tab2(1, 1, placed([P, piece], U32, "v2_w11", TAB2_AT[0]))
         contact_passes(1, 1)
 
         pieces = [(it, 0, S) for it in range(I_TILES - 1)] + [(I_TILES - 1, 0, S // 2), (I_TILES - 1, S // 2, S)]
@@ -369,7 +375,7 @@ def tile_list_residue_contact_strength_kernel(
 
         def square(n):
             it, c0, c1 = pieces[n]
-            squares[n] = scratch("x", n, W1_AT[0, 1], 4)
+            squares[n] = scratch("x", n, W1_AT[0, 1], 2)
             nc.scalar.activation(squares[n][:], y_acc[it][:, c0:c1], ACT.Square)
 
         def root(n):
@@ -384,7 +390,7 @@ def tile_list_residue_contact_strength_kernel(
         def strength(n):
             it, c0, c1 = pieces[n]
             result = scratch("result", n, W1_AT[0, 0], len(pieces))
-            engine = nc.gpsimd if n < 4 else nc.vector
+            engine = nc.gpsimd if n in (2, 4, 6) else nc.vector
             engine.tensor_tensor(result[:], units[n][:], units[n][:], MULT)
             nc.sync.dma_start(out[P * it : P * (it + 1), c0:c1], result[:])
 

@@ -27,16 +27,16 @@ I_TILES = S2 // P
 QUADS = 4
 ROWS = 4
 KIB = 1024
-W1_AT = {(0, 0): 0, (1, 0): 8 * KIB, (2, 0): 59 * KIB, (0, 1): 35 * KIB, (1, 1): 43 * KIB, (2, 1): 51 * KIB}
-TAB_AT = [24 * KIB, 16 * KIB, 67 * KIB]
-FIRST_WAVE_AT = 16 * KIB
-W4_AT = [32 * KIB, 75 * KIB]
+W1_AT = {(0, 0): 0, (1, 0): 24 * KIB, (2, 0): 38 * KIB, (1, 1): 46 * KIB, (2, 1): 54 * KIB}
+TAB_AT = [114 * KIB, 62 * KIB, 70 * KIB]
+FIRST_WAVE_AT = 24 * KIB
+W4_AT = 32 * KIB
 TAB2_AT = [78 * KIB, 94 * KIB]
-SECOND_WAVE_AT = 35 * KIB
+SECOND_WAVE_AT = 38 * KIB
 LOADS_END = 110 * KIB
 SHIFTED_ROWS = 112
 HG1_AT = 110 * KIB
-VECTOR_COLS = {(0, 0): 0, (1, 0): 0, (2, 0): 192, (0, 1): 256, (1, 1): 256, (2, 1): 512}
+VECTOR_COLS = {(0, 0): 0, (1, 0): 0, (2, 0): 192, (0, 1): 0, (1, 1): 256, (2, 1): 512}
 
 
 def tile_list_residue_contact_strength_kernel(
@@ -75,19 +75,12 @@ def tile_list_residue_contact_strength_kernel(
         w1_raw = {}
         tab_w = {}
         tab2_w = {}
-        w4 = {}
 
         def load_w1(a, half):
             w1_raw[a, half] = placed([P, PACK, PASS], F32, "w1_raw%d%d" % (a, half), W1_AT[a, half])
             rows = w1[PASS * a : PASS * (a + 1), PASS * half : PASS * (half + 1)]
             nc.sync.dma_start(w1_raw[a, half][:], rows.rearrange("(p t) c -> p t c", t=PACK))
 
-        def load_w4(half):
-            w4[half] = placed([P, K_PASSES * 2 * PASS], U8, "w4_%d" % half, W4_AT[half])
-            nc.sync.dma_start(
-                w4[half][:].bitcast(I32).rearrange("p (a w) -> p a w", a=K_PASSES),
-                w4_words[:, :, 2 * PASS * half : 2 * PASS * (half + 1)].rearrange("a p c -> p a c").bitcast(I32),
-            )
 
         def load_tab(a):
             tab_w[a] = placed([P, T], I32, "tab_w%d" % a, TAB_AT[a])
@@ -97,10 +90,13 @@ def tile_list_residue_contact_strength_kernel(
             tab2_w[a] = placed([P, T2], I32, "tab2_w%d" % a, TAB2_AT[a])
             nc.sync.dma_start(tab2_w[a][:], tab2_words[a].rearrange("p t i -> p (t i)").bitcast(I32))
 
-        load_w1(0, 0)
+        first_pass = placed([P, PACK, H], F32, "w1_first_pass", W1_AT[0, 0])
+        nc.sync.dma_start(first_pass[:], w1[:PASS, :].rearrange("(p t) c -> p t c", t=PACK))
+        for half in range(R_PASSES):
+            w1_raw[0, half] = first_pass[:, :, PASS * half : PASS * (half + 1)]
         nc.sync.dma_start(idx[:], offs)
         nc.sync.dma_start(idx2[:], offs2)
-        load_w1(1, 0)
+        load_tab(0)
         for q in range(QUADS):
             nc.scalar.dma_start(
                 tab_sc[32 * q : 32 * q + K_PASSES * ROWS, :T].bitcast(I32),
@@ -124,12 +120,15 @@ def tile_list_residue_contact_strength_kernel(
         nc.vector.memset(ones[:], 1.0)
         nc.scalar.activation(gelu_bias[0][:], zero[:, 0:1], ACT.Gelu_apprx_tanh, scale=ones[:])
 
-        load_tab(0)
-        load_w4(0)
+        w4 = placed([P, K_PASSES * 2 * H], U8, "w4", W4_AT)
+        nc.sync.dma_start(
+            w4[:].bitcast(I32).rearrange("p (a w) -> p a w", a=K_PASSES),
+            w4_words.rearrange("a p c -> p a c").bitcast(I32),
+        )
         w4_sc = held([P, K_PASSES * H], U8, "w4_sc", "ones")
         nc.vector.memset(w4_sc[:].bitcast(I32), 0)
         load_planes(nc.sync, w4_sc, w4_scales)
-        load_tab(1)
+        load_w1(1, 0)
         v_planes = held([P, S], U8, "v_planes")
         nc.vector.tensor_copy(v_planes[:], tab_sc[:, :T].indirect(idx[:]))
         v_sc = {0: v_planes}
@@ -140,10 +139,9 @@ def tile_list_residue_contact_strength_kernel(
                 v_sc[a][:SHIFTED_ROWS, :].bitcast(I32),
                 v_planes[ROWS * a : ROWS * a + SHIFTED_ROWS, :].bitcast(I32),
             )
+        load_tab(1)
         load_w1(2, 0)
         load_tab(2)
-        load_w1(0, 1)
-        load_w4(1)
         load_w1(1, 1)
         load_w1(2, 1)
         load_tab2(0)
@@ -154,7 +152,7 @@ def tile_list_residue_contact_strength_kernel(
         w1_grouped = {}
 
         def interleaved(grouped, raw):
-            return grouped.rearrange("p (c i) t -> p c t i", i=2), raw.rearrange("p t (c i) -> p c t i", i=2)
+            return grouped.rearrange("p (c i) t -> p c t i", i=4), raw.rearrange("p t (c i) -> p c t i", i=4)
 
         def round_w1(a, half, after):
             name = "w1_grouped%d%d" % (a, half)
@@ -207,7 +205,7 @@ def tile_list_residue_contact_strength_kernel(
                 out=acc[:],
                 lhsT=v_w[a][:, cols].bitcast(FP8X4),
                 lhsT_scale=v_sc[a][:, cols],
-                rhs=w4[half][:, 2 * PASS * a : 2 * PASS * (a + 1)].bitcast(FP4X4),
+                rhs=w4[:, 2 * first : 2 * (first + PASS)].bitcast(FP4X4),
                 rhs_scale=w4_sc[:, first : first + PASS],
                 start=(a == 0),
                 stop=(a == K_PASSES - 1),
@@ -263,23 +261,26 @@ def tile_list_residue_contact_strength_kernel(
                 value_pass(value_acc[jt], a, 0, jt)
 
         round_w1(0, 0, None)
+        round_w1(0, 1, None)
         round_w1(1, 0, None)
         piece = S2 // 2
         v2_sc = {}
 
         def gather_tab2_scales(g, at):
-            v2_sc[g] = placed([P, piece], U8, "v2_sc%d" % g, at)
+            name = "v2_sc%d" % g
+            v2_sc[g] = placed([P, piece], U8, name, at) if isinstance(at, int) else held([P, piece], U8, name, at)
             nc.vector.tensor_copy(v2_sc[g][:], tab2_sc[:].indirect(idx2[:, piece // 16 * g : piece // 16 * (g + 1)]))
         quantise_w1(0, 0)
         gather_tab(0, 0, S, "w1_grouped00")
-        quantise_w1(1, 0)
         gate_passes(0, 0)
         value_passes(0)
         gather_tab2_scales(0, TAB_AT[0])
+        quantise_w1(0, 1)
+        gather_tab2_scales(1, "w1_grouped01")
+        quantise_w1(1, 0)
         gather_tab(1, 0, S, "w1_grouped10")
         gate_passes(1, 0)
         value_passes(1)
-        gather_tab2_scales(1, TAB_AT[1] + 4 * KIB)
         round_w1(2, 0, TAB_AT[1])
         quantise_w1(2, 0)
         gather_tab(2, 0, S // 2, TAB_AT[1] + 2 * KIB)
@@ -300,9 +301,7 @@ def tile_list_residue_contact_strength_kernel(
             gelu(0, jt, gate_acc[jt])
         for jt in range(J_TILES):
             gated(0, jt, value_acc[jt])
-        round_w1(0, 1, "first_bias")
-        quantise_w1(0, 1)
-        round_w1(1, 1, W1_AT[0, 1])
+        round_w1(1, 1, "first_bias")
         for jt in range(J_TILES - 1):
             start_values(jt)
         for jt in range(J_TILES):
@@ -350,19 +349,19 @@ def tile_list_residue_contact_strength_kernel(
                     lhsT_scale=v2_sc[g][ROWS * (a + 1) : P, first : first + P],
                     rhs=h_codes[a][:].bitcast(FP8X4),
                     rhs_scale=h_sc[a][:],
-                    start=(a == 0),
-                    stop=(a == R_PASSES - 1),
+                    start=(a == g),
+                    stop=(a != g),
                 )
 
         gather_tab2(0, 0, held([P, piece], U32, "v2_w00", "gate13"))
         quantise_h(1, None)
         contact_passes(0, 0)
-        gather_tab2(0, 1, placed([P, piece], U32, "v2_w01", HG1_AT))
-        contact_passes(0, 1)
         gather_tab2(1, 0, placed([P, piece], U32, "v2_w10", HG1_AT + 2 * KIB))
         contact_passes(1, 0)
-        gather_tab2(1, 1, placed([P, piece], U32, "v2_w11", TAB2_AT[0]))
+        gather_tab2(1, 1, placed([P, piece], U32, "v2_w11", HG1_AT))
         contact_passes(1, 1)
+        gather_tab2(0, 1, placed([P, piece], U32, "v2_w01", TAB2_AT[1]))
+        contact_passes(0, 1)
 
         pieces = [(it, 0, S) for it in range(I_TILES - 1)] + [(I_TILES - 1, 0, S // 2), (I_TILES - 1, S // 2, S)]
         squares = {}
@@ -375,7 +374,7 @@ def tile_list_residue_contact_strength_kernel(
 
         def square(n):
             it, c0, c1 = pieces[n]
-            squares[n] = scratch("x", n, W1_AT[0, 1], 2)
+            squares[n] = scratch("x", n, W1_AT[2, 0], 2)
             nc.scalar.activation(squares[n][:], y_acc[it][:, c0:c1], ACT.Square)
 
         def root(n):
@@ -390,7 +389,7 @@ def tile_list_residue_contact_strength_kernel(
         def strength(n):
             it, c0, c1 = pieces[n]
             result = scratch("result", n, W1_AT[0, 0], len(pieces))
-            engine = nc.gpsimd if n in (2, 4, 6) else nc.vector
+            engine = nc.gpsimd if n < 4 else nc.vector
             engine.tensor_tensor(result[:], units[n][:], units[n][:], MULT)
             nc.sync.dma_start(out[P * it : P * (it + 1), c0:c1], result[:])
 

@@ -21,22 +21,27 @@ P = 128
 PACK = 4
 PASS = P * PACK
 K_PASSES = K // PASS
-R_PASSES = H // PASS
+HALVES = H // PASS
 J_TILES = S // P
 I_TILES = S2 // P
 QUADS = 4
 ROWS = 4
 KIB = 1024
-W1_AT = {(0, 0): 0, (1, 0): 24 * KIB, (2, 0): 38 * KIB, (1, 1): 46 * KIB, (2, 1): 54 * KIB}
-TAB_AT = [114 * KIB, 62 * KIB, 70 * KIB]
-FIRST_WAVE_AT = 24 * KIB
-W4_AT = 32 * KIB
-TAB2_AT = [78 * KIB, 94 * KIB]
-SECOND_WAVE_AT = 38 * KIB
-LOADS_END = 110 * KIB
 SHIFTED_ROWS = 112
-HG1_AT = 110 * KIB
-VECTOR_COLS = {(0, 0): 0, (1, 0): 0, (2, 0): 192, (0, 1): 0, (1, 1): 256, (2, 1): 512}
+W4_AT = 34 * KIB
+TAB_AT = [104 * KIB, 64 * KIB, 0]
+V_W_AT = [58 * KIB, 56 * KIB, 64 * KIB]
+TAB_EXTENT = [8 * KIB, 8 * KIB, 34 * KIB]
+V2_SC_AT = 32 * KIB
+TAB_SC_AT = 40 * KIB
+FIRST_WAVE_AT = 0
+FIRST_WAVE_END = 40 * KIB
+W1_AT = [40 * KIB, 0]
+W1_LAST_AT = [16 * KIB, 24 * KIB]
+TAB2_AT = [40 * KIB, 0]
+GROUPED_AT = 72 * KIB
+VECTOR_COLS = {(0, 0): 512, (0, 1): 192, (1, 0): 320, (1, 1): 0, (2, 0): 512, (2, 1): 320}
+H_GROUPED_AT = [96 * KIB, 100 * KIB]
 
 
 def tile_list_residue_contact_strength_kernel(
@@ -60,143 +65,94 @@ def tile_list_residue_contact_strength_kernel(
         idx = keep.tile([P, S // 16], U16, name="idx")
         idx2 = keep.tile([P, S2 // 16], U16, name="idx2")
 
-        tab_sc = placed([P, LOADS_END - SECOND_WAVE_AT], U8, "tab_sc", SECOND_WAVE_AT)
-        tab2_sc = held([P, T2], U8, "tab2_sc")
-        nc.vector.memset(tab_sc[:, :T].bitcast(I32), 0)
-        nc.gpsimd.memset(tab2_sc[:].bitcast(I32), 0)
-
-        def load_planes(queue, plane, scales):
-            for r in range(ROWS):
-                queue.dma_start(
-                    plane[:].bitcast(I32)[r:P:32, :].rearrange("q (a w) -> q a w", a=K_PASSES),
-                    scales.rearrange("a (q r) t -> r q a t", r=ROWS)[r].bitcast(I32),
-                )
-
-        w1_raw = {}
         tab_w = {}
         tab2_w = {}
-
-        def load_w1(a, half):
-            w1_raw[a, half] = placed([P, PACK, PASS], F32, "w1_raw%d%d" % (a, half), W1_AT[a, half])
-            rows = w1[PASS * a : PASS * (a + 1), PASS * half : PASS * (half + 1)]
-            nc.sync.dma_start(w1_raw[a, half][:], rows.rearrange("(p t) c -> p t c", t=PACK))
-
+        w1_raw = {}
 
         def load_tab(a):
-            tab_w[a] = placed([P, T], I32, "tab_w%d" % a, TAB_AT[a])
-            nc.sync.dma_start(tab_w[a][:], tab_words[a].rearrange("p t i -> p (t i)").bitcast(I32))
+            tab_w[a] = placed([P, TAB_EXTENT[a] // 4], I32, "tab_w%d" % a, TAB_AT[a])
+            nc.sync.dma_start(tab_w[a][:, :T], tab_words[a].rearrange("p t i -> p (t i)").bitcast(I32))
 
         def load_tab2(a):
             tab2_w[a] = placed([P, T2], I32, "tab2_w%d" % a, TAB2_AT[a])
             nc.sync.dma_start(tab2_w[a][:], tab2_words[a].rearrange("p t i -> p (t i)").bitcast(I32))
 
-        first_pass = placed([P, PACK, H], F32, "w1_first_pass", W1_AT[0, 0])
-        nc.sync.dma_start(first_pass[:], w1[:PASS, :].rearrange("(p t) c -> p t c", t=PACK))
-        for half in range(R_PASSES):
-            w1_raw[0, half] = first_pass[:, :, PASS * half : PASS * (half + 1)]
+        def load_w1_rows(a, width):
+            whole = placed([P, width], F32, "w1_rows%d" % a, W1_AT[a])
+            rows = whole[:, : PACK * H].rearrange("p (t c) -> p t c", t=PACK)
+            nc.sync.dma_start(rows, w1[PASS * a : PASS * (a + 1), :].rearrange("(p t) c -> p t c", t=PACK))
+            for half in range(HALVES):
+                w1_raw[a, half] = rows[:, :, PASS * half : PASS * (half + 1)]
+
+        def load_w1_half(a, half):
+            tile = placed([P, PACK, PASS], F32, "w1_raw%d%d" % (a, half), W1_LAST_AT[half])
+            rows = w1[PASS * a : PASS * (a + 1), PASS * half : PASS * (half + 1)]
+            nc.sync.dma_start(tile[:], rows.rearrange("(p t) c -> p t c", t=PACK))
+            w1_raw[a, half] = tile[:]
+
         nc.sync.dma_start(idx[:], offs)
         nc.sync.dma_start(idx2[:], offs2)
         load_tab(0)
+        load_tab(1)
+
+        tab_sc = placed([P, 18 * KIB], U8, "tab_sc", TAB_SC_AT)
+        tab2_sc = held([P, T2], U8, "tab2_sc")
+        nc.vector.memset(tab_sc[:, :T].bitcast(I32), 0)
         for q in range(QUADS):
             nc.scalar.dma_start(
                 tab_sc[32 * q : 32 * q + K_PASSES * ROWS, :T].bitcast(I32),
                 tab_scales[:, ROWS * q : ROWS * (q + 1), :].bitcast(I32),
             )
+        w4_sc = held([P, K_PASSES * H], U8, "w4_sc")
+        nc.gpsimd.memset(w4_sc[:].bitcast(I32), 0)
+
+        def load_w4_scales(queue, r):
+            queue.dma_start(
+                w4_sc[:].bitcast(I32)[r:P:32, :].rearrange("q (a w) -> q a w", a=K_PASSES),
+                w4_scales.rearrange("a (q r) t -> r q a t", r=ROWS)[r].bitcast(I32),
+            )
+
+        for r in range(ROWS):
+            load_w4_scales(nc.gpsimd if r < ROWS - 1 else nc.scalar, r)
+        nc.vector.memset(tab2_sc[:].bitcast(I32), 0)
         for q in range(QUADS):
             first = 32 * q + ROWS
             nc.gpsimd.dma_start(
-                tab2_sc[:].bitcast(I32)[first : first + R_PASSES * ROWS, :],
+                tab2_sc[:].bitcast(I32)[first : first + HALVES * ROWS, :],
                 tab2_scales[:, ROWS * q : ROWS * (q + 1), :].bitcast(I32),
             )
         identity = held([P, P], F32, "identity")
         make_identity(nc, identity[:])
 
-        zero = placed([P, (SECOND_WAVE_AT - FIRST_WAVE_AT) // 4], F32, "zero", FIRST_WAVE_AT)
+        zero = placed([P, (FIRST_WAVE_END - FIRST_WAVE_AT) // 4], F32, "zero", FIRST_WAVE_AT)
         nc.vector.memset(zero[:, 0:1], 0.0)
-        origin = held([P, 1], F32, "origin")
-        nc.vector.memset(origin[:], 0.0)
-        gelu_bias = [held([P, 1], F32, "first_bias"), origin]
-        ones = held([P, 1], F32, "ones")
-        nc.vector.memset(ones[:], 1.0)
-        nc.scalar.activation(gelu_bias[0][:], zero[:, 0:1], ACT.Gelu_apprx_tanh, scale=ones[:])
+        gelu_bias = held([P, 1], F32, "gelu_bias")
+        nc.scalar.activation(gelu_bias[:], zero[:, 0:1], ACT.Gelu_apprx_tanh)
 
         w4 = placed([P, K_PASSES * 2 * H], U8, "w4", W4_AT)
         nc.sync.dma_start(
             w4[:].bitcast(I32).rearrange("p (a w) -> p a w", a=K_PASSES),
             w4_words.rearrange("a p c -> p a c").bitcast(I32),
         )
-        w4_sc = held([P, K_PASSES * H], U8, "w4_sc", "ones")
-        nc.vector.memset(w4_sc[:].bitcast(I32), 0)
-        load_planes(nc.sync, w4_sc, w4_scales)
-        load_w1(1, 0)
+        load_tab(2)
+
         v_planes = held([P, S], U8, "v_planes")
-        nc.vector.tensor_copy(v_planes[:], tab_sc[:, :T].indirect(idx[:]))
         v_sc = {0: v_planes}
         for a in range(1, K_PASSES):
             v_sc[a] = held([P, S], U8, "v_sc%d" % a)
             nc.vector.memset(v_sc[a][:].bitcast(I32), 0)
+        nc.vector.tensor_copy(v_planes[:], tab_sc[:, :T].indirect(idx[:]))
+        for a in range(1, K_PASSES):
             nc.sync.dma_start(
                 v_sc[a][:SHIFTED_ROWS, :].bitcast(I32),
                 v_planes[ROWS * a : ROWS * a + SHIFTED_ROWS, :].bitcast(I32),
             )
-        load_tab(1)
-        load_w1(2, 0)
-        load_tab(2)
-        load_w1(1, 1)
-        load_w1(2, 1)
-        load_tab2(0)
-        load_tab2(1)
-
-        w1_codes = {}
-        w1_sc = {}
-        w1_grouped = {}
-
-        def interleaved(grouped, raw):
-            return grouped.rearrange("p (c i) t -> p c t i", i=4), raw.rearrange("p t (c i) -> p c t i", i=4)
-
-        def round_w1(a, half, after):
-            name = "w1_grouped%d%d" % (a, half)
-            if isinstance(after, int):
-                grouped = placed([P, PASS, PACK], BF16, name, after)
-            else:
-                grouped = held([P, PASS, PACK], BF16, name, after)
-            w1_grouped[a, half] = grouped
-            split = VECTOR_COLS[a, half]
-            raw = w1_raw[a, half]
-            if split > 0:
-                nc.vector.tensor_copy(*interleaved(grouped[:, :split, :], raw[:, :, :split]))
-            if split < PASS:
-                nc.scalar.copy(*interleaved(grouped[:, split:, :], raw[:, :, split:]))
-
-        def quantise_w1(a, half, at=None):
-            name = "w1_codes%d%d" % (a, half)
-            w1_codes[a, half] = held([P, PASS], U32, name) if at is None else placed([P, PASS], U32, name, at)
-            w1_sc[a, half] = held([P, PASS], U8, "w1_sc%d%d" % (a, half))
-            nc.vector.quantize_mx(
-                out=w1_codes[a, half][:].bitcast(FP8X4),
-                scales=w1_sc[a, half][:],
-                in_=w1_grouped[a, half][:].rearrange("p c t -> p (c t)"),
-            )
 
         v_w = {}
 
-        def gather_tab(a, c0, c1, after=None):
-            if c0 == 0:
-                name = "v_w%d" % a
-                v_w[a] = placed([P, S], U32, name, after) if isinstance(after, int) else held([P, S], U32, name, after)
-            nc.vector.tensor_copy(v_w[a][:, c0:c1], tab_w[a][:].bitcast(U32).indirect(idx[:, c0 // 16 : c1 // 16]))
-
-        def gate_pass(acc, a, half, jt, passes=(0, 1, 2)):
-            cols = slice(P * jt, P * (jt + 1))
-            nc.tensor.matmul_mx(
-                out=acc[:],
-                lhsT=v_w[a][:, cols].bitcast(FP8X4),
-                lhsT_scale=v_planes[ROWS * a : P, cols],
-                rhs=w1_codes[a, half][:].bitcast(FP8X4),
-                rhs_scale=w1_sc[a, half][:],
-                start=(a == passes[0]),
-                stop=(a == passes[-1]),
-            )
+        def gather_tab(a):
+            v_w[a] = placed([P, S], U32, "v_w%d" % a, V_W_AT[a])
+            nc.vector.tensor_copy(v_w[a][:], tab_w[a][:, :T].bitcast(U32).indirect(idx[:]))
 
         def value_pass(acc, a, half, jt):
             cols = slice(P * jt, P * (jt + 1))
@@ -211,134 +167,160 @@ def tile_list_residue_contact_strength_kernel(
                 stop=(a == K_PASSES - 1),
             )
 
+        tiles = [(half, jt) for half in range(HALVES) for jt in range(J_TILES)]
+        acc = {(half, jt): bank(J_TILES * half + jt, [P, PASS]) for half, jt in tiles}
+        load_w1_rows(0, PACK * H)
+        for a in range(K_PASSES):
+            gather_tab(a)
+        load_w1_rows(1, PACK * H)
+        load_w1_half(2, 0)
+        load_w1_half(2, 1)
+        for half in range(HALVES):
+            for a in range(K_PASSES):
+                for jt in range(J_TILES):
+                    value_pass(acc[half, jt], a, half, jt)
+
+        piece = S2 // 2
+        v2_sc = {}
+
+        def gather_tab2_scales(g):
+            v2_sc[g] = placed([P, piece], U8, "v2_sc%d" % g, V2_SC_AT + KIB * g)
+            nc.vector.tensor_copy(v2_sc[g][:], tab2_sc[:].indirect(idx2[:, piece // 16 * g : piece // 16 * (g + 1)]))
+
+        gather_tab2_scales(0)
+        gather_tab2_scales(1)
+        order = "j (p u e) -> j u p e"
+        values = {}
+        for half, jt in tiles:
+            values[half, jt] = held([P, 2, P, 2], F32, "values%d%d" % (half, jt))
+            nc.scalar.copy(values[half, jt][:], acc[half, jt][:].rearrange(order, u=2, e=2))
+
+        w1_codes = {}
+        w1_sc = {}
+        w1_grouped = {}
+
+        def interleaved(grouped, raw):
+            return grouped.rearrange("p (c i) t -> p c t i", i=4), raw.rearrange("p t (c i) -> p c t i", i=4)
+
+        def round_w1(a, half):
+            grouped = placed([P, PASS, PACK], BF16, "w1_grouped%d%d" % (a, half), GROUPED_AT + 4 * KIB * (2 * a + half))
+            w1_grouped[a, half] = grouped
+            split = VECTOR_COLS[a, half]
+            raw = w1_raw[a, half]
+            if split > 0:
+                nc.vector.tensor_copy(*interleaved(grouped[:, :split, :], raw[:, :, :split]))
+            if split < PASS:
+                nc.scalar.copy(*interleaved(grouped[:, split:, :], raw[:, :, split:]))
+
+        def quantise_w1(a, half):
+            w1_codes[a, half] = held([P, PASS], U32, "w1_codes%d%d" % (a, half))
+            w1_sc[a, half] = held([P, PASS], U8, "w1_sc%d%d" % (a, half))
+            nc.vector.quantize_mx(
+                out=w1_codes[a, half][:].bitcast(FP8X4),
+                scales=w1_sc[a, half][:],
+                in_=w1_grouped[a, half][:].rearrange("p c t -> p (c t)"),
+            )
+
+        acc = {(half, jt): bank(J_TILES * half + jt, [P, PASS]) for half, jt in tiles}
+
+        def gate_passes(a, half):
+            for jt in range(J_TILES):
+                cols = slice(P * jt, P * (jt + 1))
+                nc.tensor.matmul_mx(
+                    out=acc[half, jt][:],
+                    lhsT=v_w[a][:, cols].bitcast(FP8X4),
+                    lhsT_scale=v_planes[ROWS * a : P, cols],
+                    rhs=w1_codes[a, half][:].bitcast(FP8X4),
+                    rhs_scale=w1_sc[a, half][:],
+                    start=(a == 0),
+                    stop=(a == K_PASSES - 1),
+                )
+
         h_codes = {}
         h_sc = {}
         gates = {}
         h_rows = {}
         h_grouped = {}
         turned = {}
-        order = "j (p u e) -> j u p e"
 
-        def gelu(half, jt, acc):
-            gates[half, jt] = held([P, 2, P, 2], F32, "gate%d%d" % (half, jt))
+        def gelu(half, jt):
+            gates[half, jt] = held([P, 2, P, 2], F32, "gate%d%d" % (half, jt), "gate%d" % jt)
             nc.scalar.activation(
-                gates[half, jt][:], acc[:].rearrange(order, u=2, e=2), ACT.Gelu_apprx_tanh, bias=gelu_bias[half][:]
+                gates[half, jt][:], acc[half, jt][:].rearrange(order, u=2, e=2), ACT.Gelu_apprx_tanh, bias=gelu_bias[:]
             )
 
-        def gated(half, jt, acc):
+        def gated(half, jt):
             h_rows[half, jt] = held([P, 2, P, 2], BF16, "h_rows%d%d" % (half, jt))
-            nc.vector.tensor_tensor(h_rows[half, jt][:], acc[:].rearrange(order, u=2, e=2), gates[half, jt][:], MULT)
+            nc.vector.tensor_tensor(h_rows[half, jt][:], values[half, jt][:], gates[half, jt][:], MULT)
 
         def turn(half, jt):
             words = h_rows[half, jt][:].rearrange("j u p e -> j (u p e)").bitcast(F32)
-            turned[half, jt] = bank(jt, [P, 2, P])
+            turned[half, jt] = bank(J_TILES * half + jt, [P, 2, P])
             for u in range(2):
                 nc.tensor.transpose(turned[half, jt][:, u, :], words[:, P * u : P * (u + 1)], identity[:])
 
         def group_h(half, jt):
+            if jt == 0:
+                h_grouped[half] = placed([P, S * PACK], BF16, "h_grouped%d" % half, H_GROUPED_AT[half])
             nc.scalar.copy(
                 h_grouped[half][:, PASS * jt : PASS * (jt + 1)].bitcast(F32).rearrange("p (j u) -> p j u", u=2),
                 turned[half, jt][:].rearrange("p u j -> p j u"),
             )
 
-        def quantise_h(half, after):
-            h_codes[half] = held([P, S], U32, "h_codes%d" % half, after)
+        def quantise_h(half):
+            h_codes[half] = held([P, S], U32, "h_codes%d" % half)
             h_sc[half] = held([P, S], U8, "h_sc%d" % half)
             nc.vector.quantize_mx(out=h_codes[half][:].bitcast(FP8X4), scales=h_sc[half][:], in_=h_grouped[half][:])
 
-        h_grouped[0] = placed([P, S * PACK], BF16, "h_grouped0", W1_AT[1, 1])
-        h_grouped[1] = placed([P, S * PACK], BF16, "h_grouped1", HG1_AT)
-
-        gate_acc = [bank(jt, [P, PASS]) for jt in range(J_TILES)]
-        value_acc = [bank(J_TILES + jt, [P, PASS]) for jt in range(J_TILES)]
-
-        def gate_passes(a, half):
-            for jt in range(J_TILES):
-                gate_pass(gate_acc[jt], a, half, jt)
-
-        def value_passes(a):
-            for jt in range(J_TILES):
-                value_pass(value_acc[jt], a, 0, jt)
-
-        round_w1(0, 0, None)
-        round_w1(0, 1, None)
-        round_w1(1, 0, None)
-        piece = S2 // 2
-        v2_sc = {}
-
-        def gather_tab2_scales(g, at):
-            name = "v2_sc%d" % g
-            v2_sc[g] = placed([P, piece], U8, name, at) if isinstance(at, int) else held([P, piece], U8, name, at)
-            nc.vector.tensor_copy(v2_sc[g][:], tab2_sc[:].indirect(idx2[:, piece // 16 * g : piece // 16 * (g + 1)]))
+        round_w1(0, 0)
+        round_w1(0, 1)
+        load_tab2(0)
         quantise_w1(0, 0)
-        gather_tab(0, 0, S, "w1_grouped00")
         gate_passes(0, 0)
-        value_passes(0)
-        gather_tab2_scales(0, TAB_AT[0])
         quantise_w1(0, 1)
-        gather_tab2_scales(1, "w1_grouped01")
+        gate_passes(0, 1)
+        round_w1(1, 0)
+        round_w1(1, 1)
+        load_tab2(1)
         quantise_w1(1, 0)
-        gather_tab(1, 0, S, "w1_grouped10")
         gate_passes(1, 0)
-        value_passes(1)
-        round_w1(2, 0, TAB_AT[1])
+        round_w1(2, 0)
         quantise_w1(2, 0)
-        gather_tab(2, 0, S // 2, TAB_AT[1] + 2 * KIB)
-        gather_tab(2, S // 2, S)
+        gate_passes(2, 0)
+        round_w1(2, 1)
+        quantise_w1(1, 1)
+        gate_passes(1, 1)
+        quantise_w1(2, 1)
+        gate_passes(2, 1)
         for jt in range(J_TILES):
-            gate_pass(gate_acc[jt], 2, 0, jt)
-            value_pass(value_acc[jt], 2, 0, jt)
-
-        next_value = []
-
-        def start_values(jt):
-            acc = bank(J_TILES + jt, [P, PASS])
-            next_value.append(acc)
-            for a in range(K_PASSES):
-                value_pass(acc, a, 1, jt)
-
+            gelu(0, jt)
         for jt in range(J_TILES):
-            gelu(0, jt, gate_acc[jt])
-        for jt in range(J_TILES):
-            gated(0, jt, value_acc[jt])
-        round_w1(1, 1, "first_bias")
-        for jt in range(J_TILES - 1):
-            start_values(jt)
+            gated(0, jt)
         for jt in range(J_TILES):
             turn(0, jt)
-        start_values(J_TILES - 1)
+        for jt in range(J_TILES):
+            gelu(1, jt)
         for jt in range(J_TILES):
             group_h(0, jt)
-        value_acc = next_value
-        gate_acc = [bank(jt, [P, PASS]) for jt in range(J_TILES)]
-        quantise_w1(1, 1)
-        round_w1(2, 1, "h_rows03")
-        quantise_w1(2, 1)
-        for jt, passes in enumerate(((0, 1, 2), (0, 1, 2), (0, 2, 1), (2, 0, 1))):
-            for a in passes:
-                gate_pass(gate_acc[jt], a, 1, jt, passes)
-        quantise_h(0, "h_rows03")
+        for jt in range(J_TILES):
+            gated(1, jt)
+        for jt in range(J_TILES):
+            turn(1, jt)
+        for jt in range(J_TILES):
+            group_h(1, jt)
         v2_w = {}
 
         def gather_tab2(a, g, tile):
             v2_w[a, g] = tile
             nc.vector.tensor_copy(
-                tile[:],
+                v2_w[a, g][:],
                 tab2_w[a][:].bitcast(U32).indirect(idx2[:, piece // 16 * g : piece // 16 * (g + 1)]),
             )
 
-        for jt in range(J_TILES):
-            gelu(1, jt, gate_acc[jt])
-        for jt in range(J_TILES):
-            gated(1, jt, value_acc[jt])
-            turn(1, jt)
-        for jt in range(J_TILES):
-            group_h(1, jt)
-
         one = held([P, 1], F32, "one", "h_rows13")
-        nc.scalar.activation(one[:], origin[:], ACT.Abs_reciprocal_sqrt, bias=1.0)
+        nc.scalar.activation(one[:], gelu_bias[:], ACT.Abs_reciprocal_sqrt, bias=1.0)
 
-        y_acc = [bank((J_TILES + it) % I_TILES, [P, S]) for it in range(I_TILES)]
+        y_acc = [bank(it, [P, S]) for it in range(I_TILES)]
 
         def contact_passes(a, g):
             for it in range(I_TILES // 2 * g, I_TILES // 2 * (g + 1)):
@@ -353,12 +335,13 @@ def tile_list_residue_contact_strength_kernel(
                     stop=(a != g),
                 )
 
-        gather_tab2(0, 0, held([P, piece], U32, "v2_w00", "gate13"))
-        quantise_h(1, None)
+        gather_tab2(0, 0, held([P, piece], U32, "v2_w00", "gate3"))
+        quantise_h(0)
         contact_passes(0, 0)
-        gather_tab2(1, 0, placed([P, piece], U32, "v2_w10", HG1_AT + 2 * KIB))
+        quantise_h(1)
+        gather_tab2(1, 0, placed([P, piece], U32, "v2_w10", H_GROUPED_AT[1]))
         contact_passes(1, 0)
-        gather_tab2(1, 1, placed([P, piece], U32, "v2_w11", HG1_AT))
+        gather_tab2(1, 1, placed([P, piece], U32, "v2_w11", H_GROUPED_AT[1] + 2 * KIB))
         contact_passes(1, 1)
         gather_tab2(0, 1, placed([P, piece], U32, "v2_w01", TAB2_AT[1]))
         contact_passes(0, 1)
@@ -368,27 +351,27 @@ def tile_list_residue_contact_strength_kernel(
         roots = {}
         units = {}
 
-        def scratch(kind, n, first, depth):
+        def scratch(kind, n, ring):
             it, c0, c1 = pieces[n]
-            return placed([P, c1 - c0], F32, "%s%d" % (kind, n), first + 2 * KIB * (n % depth))
+            return held([P, c1 - c0], F32, "%s%d" % (kind, n), ring[n % len(ring)])
 
         def square(n):
             it, c0, c1 = pieces[n]
-            squares[n] = scratch("x", n, W1_AT[2, 0], 2)
+            squares[n] = scratch("x", n, ["w1_codes00", "w1_codes01"])
             nc.scalar.activation(squares[n][:], y_acc[it][:, c0:c1], ACT.Square)
 
         def root(n):
-            roots[n] = scratch("root", n, W1_AT[1, 1], 4)
+            roots[n] = scratch("root", n, ["w1_codes10", "w1_codes11", "w1_codes20", "w1_codes21"])
             nc.scalar.activation(roots[n][:], squares[n][:], ACT.Abs_reciprocal_sqrt, bias=one[:])
 
         def unit(n):
             it, c0, c1 = pieces[n]
-            units[n] = scratch("unit", n, W1_AT[2, 1], 4)
+            units[n] = scratch("unit", n, ["unit0", "unit1", "unit2", "unit3"])
             nc.vector.tensor_tensor(units[n][:], y_acc[it][:, c0:c1], roots[n][:], MULT)
 
         def strength(n):
             it, c0, c1 = pieces[n]
-            result = scratch("result", n, W1_AT[0, 0], len(pieces))
+            result = scratch("result", n, ["values%d%d" % tile for tile in tiles] + ["gate2"])
             engine = nc.gpsimd if n < 4 else nc.vector
             engine.tensor_tensor(result[:], units[n][:], units[n][:], MULT)
             nc.sync.dma_start(out[P * it : P * (it + 1), c0:c1], result[:])

@@ -29,17 +29,21 @@ ROWS = 4
 KIB = 1024
 SHIFTED_ROWS = 112
 W4_AT = 34 * KIB
-TAB_AT = [104 * KIB, 64 * KIB, 0]
+TAB_AT = [8 * KIB, 64 * KIB, 0]
 V_W_AT = [58 * KIB, 56 * KIB, 64 * KIB]
 TAB_EXTENT = [8 * KIB, 8 * KIB, 34 * KIB]
 V2_SC_AT = 32 * KIB
 TAB_SC_AT = 40 * KIB
-FIRST_WAVE_AT = 0
+FIRST_WAVE_AT = 34 * KIB
 FIRST_WAVE_END = 40 * KIB
 W1_AT = [40 * KIB, 0]
 W1_LAST_AT = [16 * KIB, 24 * KIB]
 TAB2_AT = [40 * KIB, 0]
 GROUPED_AT = 72 * KIB
+VECTOR_SQUARES = (6,)
+GPSIMD_FINALS = (1, 2, 3, 5)
+SCALAR_FINALS = (6, 8)
+VECTOR_LEAD = 3
 VECTOR_COLS = {(0, 0): 512, (0, 1): 192, (1, 0): 320, (1, 1): 0, (2, 0): 512, (2, 1): 320}
 H_GROUPED_AT = [96 * KIB, 100 * KIB]
 
@@ -93,16 +97,21 @@ def tile_list_residue_contact_strength_kernel(
         nc.sync.dma_start(idx[:], offs)
         nc.sync.dma_start(idx2[:], offs2)
         load_tab(0)
-        load_tab(1)
 
         tab_sc = placed([P, 18 * KIB], U8, "tab_sc", TAB_SC_AT)
         tab2_sc = held([P, T2], U8, "tab2_sc")
         nc.vector.memset(tab_sc[:, :T].bitcast(I32), 0)
         for q in range(QUADS):
-            nc.scalar.dma_start(
+            queue = nc.scalar if q < QUADS // 2 else nc.sync
+            queue.dma_start(
                 tab_sc[32 * q : 32 * q + K_PASSES * ROWS, :T].bitcast(I32),
                 tab_scales[:, ROWS * q : ROWS * (q + 1), :].bitcast(I32),
             )
+        cleared = placed([P, 1], F32, "cleared", TAB_AT[1])
+        nc.vector.memset(cleared[:], 0.0)
+        origin = held([P, 1], F32, "origin")
+        nc.vector.tensor_copy(origin[:], cleared[:])
+        load_tab(1)
         w4_sc = held([P, K_PASSES * H], U8, "w4_sc")
         nc.gpsimd.memset(w4_sc[:].bitcast(I32), 0)
 
@@ -127,32 +136,33 @@ def tile_list_residue_contact_strength_kernel(
         zero = placed([P, (FIRST_WAVE_END - FIRST_WAVE_AT) // 4], F32, "zero", FIRST_WAVE_AT)
         nc.vector.memset(zero[:, 0:1], 0.0)
         gelu_bias = held([P, 1], F32, "gelu_bias")
-        nc.scalar.activation(gelu_bias[:], zero[:, 0:1], ACT.Gelu_apprx_tanh)
+        nc.scalar.activation(gelu_bias[:], zero[:, 0:1], ACT.Gelu_apprx_tanh, bias=origin[:])
 
         w4 = placed([P, K_PASSES * 2 * H], U8, "w4", W4_AT)
         nc.sync.dma_start(
             w4[:].bitcast(I32).rearrange("p (a w) -> p a w", a=K_PASSES),
             w4_words.rearrange("a p c -> p a c").bitcast(I32),
         )
-        load_tab(2)
-
-        v_planes = held([P, S], U8, "v_planes")
-        v_sc = {0: v_planes}
-        for a in range(1, K_PASSES):
-            v_sc[a] = held([P, S], U8, "v_sc%d" % a)
-            nc.vector.memset(v_sc[a][:].bitcast(I32), 0)
-        nc.vector.tensor_copy(v_planes[:], tab_sc[:, :T].indirect(idx[:]))
-        for a in range(1, K_PASSES):
-            nc.sync.dma_start(
-                v_sc[a][:SHIFTED_ROWS, :].bitcast(I32),
-                v_planes[ROWS * a : ROWS * a + SHIFTED_ROWS, :].bitcast(I32),
-            )
 
         v_w = {}
 
         def gather_tab(a):
             v_w[a] = placed([P, S], U32, "v_w%d" % a, V_W_AT[a])
             nc.vector.tensor_copy(v_w[a][:], tab_w[a][:, :T].bitcast(U32).indirect(idx[:]))
+
+        v_planes = held([P, S], U8, "v_planes")
+        v_sc = {0: v_planes}
+        for a in range(1, K_PASSES):
+            v_sc[a] = held([P, S], U8, "v_sc%d" % a)
+            nc.vector.memset(v_sc[a][:].bitcast(I32), 0)
+        gather_tab(0)
+        load_tab(2)
+        nc.vector.tensor_copy(v_planes[:], tab_sc[:, :T].indirect(idx[:]))
+        for a in range(1, K_PASSES):
+            nc.sync.dma_start(
+                v_sc[a][:SHIFTED_ROWS, :].bitcast(I32),
+                v_planes[ROWS * a : ROWS * a + SHIFTED_ROWS, :].bitcast(I32),
+            )
 
         def value_pass(acc, a, half, jt):
             cols = slice(P * jt, P * (jt + 1))
@@ -170,7 +180,7 @@ def tile_list_residue_contact_strength_kernel(
         tiles = [(half, jt) for half in range(HALVES) for jt in range(J_TILES)]
         acc = {(half, jt): bank(J_TILES * half + jt, [P, PASS]) for half, jt in tiles}
         load_w1_rows(0, PACK * H)
-        for a in range(K_PASSES):
+        for a in range(1, K_PASSES):
             gather_tab(a)
         load_w1_rows(1, PACK * H)
         load_w1_half(2, 0)
@@ -357,8 +367,14 @@ def tile_list_residue_contact_strength_kernel(
 
         def square(n):
             it, c0, c1 = pieces[n]
-            squares[n] = scratch("x", n, ["w1_codes00", "w1_codes01"])
-            nc.scalar.activation(squares[n][:], y_acc[it][:, c0:c1], ACT.Square)
+            if n in VECTOR_SQUARES:
+                plain = scratch("y", n, ["gate0"])
+                squares[n] = scratch("x", n, ["gate1"])
+                nc.vector.tensor_copy(plain[:], y_acc[it][:, c0:c1])
+                nc.vector.tensor_tensor(squares[n][:], y_acc[it][:, c0:c1], plain[:], MULT)
+            else:
+                squares[n] = scratch("x", n, ["w1_codes00", "w1_codes01"])
+                nc.scalar.activation(squares[n][:], y_acc[it][:, c0:c1], ACT.Square)
 
         def root(n):
             roots[n] = scratch("root", n, ["w1_codes10", "w1_codes11", "w1_codes20", "w1_codes21"])
@@ -366,18 +382,24 @@ def tile_list_residue_contact_strength_kernel(
 
         def unit(n):
             it, c0, c1 = pieces[n]
-            units[n] = scratch("unit", n, ["unit0", "unit1", "unit2", "unit3"])
+            units[n] = placed([P, c1 - c0], F32, "unit%d" % n, GROUPED_AT + 2 * KIB * n)
             nc.vector.tensor_tensor(units[n][:], y_acc[it][:, c0:c1], roots[n][:], MULT)
 
         def strength(n):
             it, c0, c1 = pieces[n]
             result = scratch("result", n, ["values%d%d" % tile for tile in tiles] + ["gate2"])
-            engine = nc.gpsimd if n < 4 else nc.vector
-            engine.tensor_tensor(result[:], units[n][:], units[n][:], MULT)
+            if n in SCALAR_FINALS:
+                nc.scalar.activation(result[:], units[n][:], ACT.Square)
+            else:
+                engine = nc.gpsimd if n in GPSIMD_FINALS else nc.vector
+                engine.tensor_tensor(result[:], units[n][:], units[n][:], MULT)
             nc.sync.dma_start(out[P * it : P * (it + 1), c0:c1], result[:])
 
         steps = (square, root, unit, strength)
         for time in range(len(pieces) + len(steps) - 1):
             for lag, step in enumerate(steps):
-                if 0 <= time - lag < len(pieces):
-                    step(time - lag)
+                n = time - lag
+                if 0 <= n < len(pieces) and not (step is square and n in VECTOR_SQUARES):
+                    step(n)
+            if time + VECTOR_LEAD in VECTOR_SQUARES:
+                square(time + VECTOR_LEAD)

@@ -112,18 +112,7 @@ def tile_list_residue_contact_strength_kernel(
         origin = held([P, 1], F32, "origin")
         nc.vector.tensor_copy(origin[:], cleared[:])
         load_tab(1)
-        w4_sc = held([P, K_PASSES * H], U8, "w4_sc")
-        nc.gpsimd.memset(w4_sc[:].bitcast(I32), 0)
-
-        def load_w4_scales(queue, r):
-            queue.dma_start(
-                w4_sc[:].bitcast(I32)[r:P:32, :].rearrange("q (a w) -> q a w", a=K_PASSES),
-                w4_scales.rearrange("a (q r) t -> r q a t", r=ROWS)[r].bitcast(I32),
-            )
-
-        for r in range(ROWS):
-            load_w4_scales(nc.gpsimd if r < ROWS - 1 else nc.scalar, r)
-        nc.vector.memset(tab2_sc[:].bitcast(I32), 0)
+        nc.gpsimd.memset(tab2_sc[:].bitcast(I32), 0)
         for q in range(QUADS):
             first = 32 * q + ROWS
             nc.gpsimd.dma_start(
@@ -137,12 +126,19 @@ def tile_list_residue_contact_strength_kernel(
         nc.vector.memset(zero[:, 0:1], 0.0)
         gelu_bias = held([P, 1], F32, "gelu_bias")
         nc.scalar.activation(gelu_bias[:], zero[:, 0:1], ACT.Gelu_apprx_tanh, bias=origin[:])
+        w4_sc = held([P, K_PASSES * H], U8, "w4_sc", "origin")
+        nc.vector.memset(w4_sc[:].bitcast(I32), 0)
 
         w4 = placed([P, K_PASSES * 2 * H], U8, "w4", W4_AT)
         nc.sync.dma_start(
             w4[:].bitcast(I32).rearrange("p (a w) -> p a w", a=K_PASSES),
             w4_words.rearrange("a p c -> p a c").bitcast(I32),
         )
+        for r in range(ROWS):
+            nc.scalar.dma_start(
+                w4_sc[:].bitcast(I32)[r:P:32, :].rearrange("q (a w) -> q a w", a=K_PASSES),
+                w4_scales.rearrange("a (q r) t -> r q a t", r=ROWS)[r].bitcast(I32),
+            )
 
         v_w = {}
 
@@ -212,15 +208,11 @@ def tile_list_residue_contact_strength_kernel(
         def interleaved(grouped, raw):
             return grouped.rearrange("p (c i) t -> p c t i", i=4), raw.rearrange("p t (c i) -> p c t i", i=4)
 
-        def round_w1(a, half):
-            grouped = placed([P, PASS, PACK], BF16, "w1_grouped%d%d" % (a, half), GROUPED_AT + 4 * KIB * (2 * a + half))
-            w1_grouped[a, half] = grouped
-            split = VECTOR_COLS[a, half]
-            raw = w1_raw[a, half]
-            if split > 0:
-                nc.vector.tensor_copy(*interleaved(grouped[:, :split, :], raw[:, :, :split]))
-            if split < PASS:
-                nc.scalar.copy(*interleaved(grouped[:, split:, :], raw[:, :, split:]))
+        def round_w1(copy, a, half, c0, c1):
+            if (a, half) not in w1_grouped:
+                at = GROUPED_AT + 4 * KIB * (HALVES * a + half)
+                w1_grouped[a, half] = placed([P, PASS, PACK], BF16, "w1_grouped%d%d" % (a, half), at)
+            copy(*interleaved(w1_grouped[a, half][:, c0:c1, :], w1_raw[a, half][:, :, c0:c1]))
 
         def quantise_w1(a, half):
             w1_codes[a, half] = held([P, PASS], U32, "w1_codes%d%d" % (a, half))
@@ -282,30 +274,39 @@ def tile_list_residue_contact_strength_kernel(
             h_sc[half] = held([P, S], U8, "h_sc%d" % half)
             nc.vector.quantize_mx(out=h_codes[half][:].bitcast(FP8X4), scales=h_sc[half][:], in_=h_grouped[half][:])
 
-        round_w1(0, 0)
-        round_w1(0, 1)
+        vector, scalar = nc.vector.tensor_copy, nc.scalar.copy
+        round_w1(vector, 0, 0, 0, PASS)
+        round_w1(vector, 0, 1, 0, PASS)
         load_tab2(0)
         quantise_w1(0, 0)
         gate_passes(0, 0)
         quantise_w1(0, 1)
-        gate_passes(0, 1)
-        round_w1(1, 0)
-        round_w1(1, 1)
-        load_tab2(1)
+        round_w1(vector, 1, 0, 0, 320)
+        round_w1(scalar, 1, 0, 320, PASS)
+        round_w1(scalar, 1, 1, 0, 320)
         quantise_w1(1, 0)
         gate_passes(1, 0)
-        round_w1(2, 0)
+        round_w1(vector, 2, 0, 0, 320)
+        round_w1(scalar, 2, 0, 320, PASS)
+        round_w1(scalar, 1, 1, 320, PASS)
+        load_tab2(1)
         quantise_w1(2, 0)
         gate_passes(2, 0)
-        round_w1(2, 1)
+        gate_passes(0, 1)
         quantise_w1(1, 1)
         gate_passes(1, 1)
+        round_w1(vector, 2, 1, 0, 320)
+        gelu(0, 0)
+        gelu(0, 1)
+        round_w1(scalar, 2, 1, 320, PASS)
+        gated(0, 0)
+        gated(0, 1)
         quantise_w1(2, 1)
         gate_passes(2, 1)
-        for jt in range(J_TILES):
-            gelu(0, jt)
-        for jt in range(J_TILES):
-            gated(0, jt)
+        gelu(0, 2)
+        gelu(0, 3)
+        gated(0, 2)
+        gated(0, 3)
         for jt in range(J_TILES):
             turn(0, jt)
         for jt in range(J_TILES):

@@ -28,24 +28,24 @@ QUADS = 4
 ROWS = 4
 KIB = 1024
 SHIFTED_ROWS = 112
-W4_AT = 34 * KIB
-TAB_AT = [8 * KIB, 64 * KIB, 0]
-V_W_AT = [58 * KIB, 56 * KIB, 64 * KIB]
+TAB_AT = [0, 8 * KIB, 16 * KIB]
 TAB_EXTENT = [8 * KIB, 8 * KIB, 34 * KIB]
-V2_SC_AT = 32 * KIB
-TAB_SC_AT = 40 * KIB
-FIRST_WAVE_AT = 34 * KIB
-FIRST_WAVE_END = 40 * KIB
-W1_AT = [40 * KIB, 0]
-W1_LAST_AT = [16 * KIB, 24 * KIB]
-TAB2_AT = [40 * KIB, 0]
-GROUPED_AT = 72 * KIB
+CLEARED_EXTENT = 20 * KIB
+V_W_AT = [72 * KIB, 0, 8 * KIB]
+V2_SC_AT = 48 * KIB
+W4_AT = 50 * KIB
+TAB_SC_AT = 56 * KIB
+W1_AT = [56 * KIB, 16 * KIB]
+W1_LAST_AT = [32 * KIB, 40 * KIB]
+TAB2_AT = [56 * KIB, 16 * KIB]
+GROUPED_AT = 76 * KIB
+BLOCK = 8
 VECTOR_SQUARES = (6,)
 GPSIMD_FINALS = (1, 2, 3, 5)
 SCALAR_FINALS = (6, 8)
 VECTOR_LEAD = 3
 VECTOR_COLS = {(0, 0): 512, (0, 1): 192, (1, 0): 320, (1, 1): 0, (2, 0): 512, (2, 1): 320}
-H_GROUPED_AT = [96 * KIB, 100 * KIB]
+H_GROUPED_AT = [100 * KIB, 104 * KIB]
 
 
 def tile_list_residue_contact_strength_kernel(
@@ -96,22 +96,33 @@ def tile_list_residue_contact_strength_kernel(
 
         nc.sync.dma_start(idx[:], offs)
         nc.sync.dma_start(idx2[:], offs2)
-        load_tab(0)
+        w4 = placed([P, K_PASSES * 2 * H], U8, "w4", W4_AT)
+        nc.sync.dma_start(
+            w4[:].bitcast(I32).rearrange("p (a w) -> p a w", a=K_PASSES),
+            w4_words.rearrange("a p c -> p a c").bitcast(I32),
+        )
 
         tab_sc = placed([P, 18 * KIB], U8, "tab_sc", TAB_SC_AT)
-        tab2_sc = held([P, T2], U8, "tab2_sc")
-        nc.vector.memset(tab_sc[:, :T].bitcast(I32), 0)
-        for q in range(QUADS):
-            queue = nc.scalar if q < QUADS // 2 else nc.sync
-            queue.dma_start(
-                tab_sc[32 * q : 32 * q + K_PASSES * ROWS, :T].bitcast(I32),
-                tab_scales[:, ROWS * q : ROWS * (q + 1), :].bitcast(I32),
+        nc.gpsimd.memset(tab_sc[:, :T].bitcast(I32), 0)
+        nc.vector.memset(tab_sc[:, T : K_PASSES * T].bitcast(I32), 0)
+        nc.sync.dma_start(
+            tab_sc[:, : K_PASSES * T].bitcast(I32)[0:P:BLOCK, :].rearrange("q (a w) -> q a w", a=K_PASSES),
+            tab_scales.rearrange("a q t -> q a t").bitcast(I32),
+        )
+        w4_sc = held([P, K_PASSES * H], U8, "w4_sc")
+        nc.vector.memset(w4_sc[:].bitcast(I32), 0)
+        for r in range(ROWS):
+            nc.sync.dma_start(
+                w4_sc[:].bitcast(I32)[r:P:32, :].rearrange("q (a w) -> q a w", a=K_PASSES),
+                w4_scales.rearrange("a (q r) t -> r q a t", r=ROWS)[r].bitcast(I32),
             )
-        cleared = placed([P, 1], F32, "cleared", TAB_AT[1])
-        nc.vector.memset(cleared[:], 0.0)
+        cleared = placed([P, CLEARED_EXTENT // 4], F32, "cleared", TAB_AT[0])
+        nc.vector.memset(cleared[:, 0:1], 0.0)
         origin = held([P, 1], F32, "origin")
-        nc.vector.tensor_copy(origin[:], cleared[:])
-        load_tab(1)
+        nc.vector.tensor_copy(origin[:], cleared[:, 0:1])
+        for a in range(K_PASSES):
+            load_tab(a)
+        tab2_sc = held([P, T2], U8, "tab2_sc")
         nc.gpsimd.memset(tab2_sc[:].bitcast(I32), 0)
         for q in range(QUADS):
             first = 32 * q + ROWS
@@ -122,23 +133,8 @@ def tile_list_residue_contact_strength_kernel(
         identity = held([P, P], F32, "identity")
         make_identity(nc, identity[:])
 
-        zero = placed([P, (FIRST_WAVE_END - FIRST_WAVE_AT) // 4], F32, "zero", FIRST_WAVE_AT)
-        nc.vector.memset(zero[:, 0:1], 0.0)
         gelu_bias = held([P, 1], F32, "gelu_bias")
-        nc.scalar.activation(gelu_bias[:], zero[:, 0:1], ACT.Gelu_apprx_tanh, bias=origin[:])
-        w4_sc = held([P, K_PASSES * H], U8, "w4_sc", "origin")
-        nc.vector.memset(w4_sc[:].bitcast(I32), 0)
-
-        w4 = placed([P, K_PASSES * 2 * H], U8, "w4", W4_AT)
-        nc.sync.dma_start(
-            w4[:].bitcast(I32).rearrange("p (a w) -> p a w", a=K_PASSES),
-            w4_words.rearrange("a p c -> p a c").bitcast(I32),
-        )
-        for r in range(ROWS):
-            nc.scalar.dma_start(
-                w4_sc[:].bitcast(I32)[r:P:32, :].rearrange("q (a w) -> q a w", a=K_PASSES),
-                w4_scales.rearrange("a (q r) t -> r q a t", r=ROWS)[r].bitcast(I32),
-            )
+        nc.scalar.activation(gelu_bias[:], origin[:], ACT.Gelu_apprx_tanh)
 
         v_w = {}
 
@@ -146,19 +142,14 @@ def tile_list_residue_contact_strength_kernel(
             v_w[a] = placed([P, S], U32, "v_w%d" % a, V_W_AT[a])
             nc.vector.tensor_copy(v_w[a][:], tab_w[a][:, :T].bitcast(U32).indirect(idx[:]))
 
-        v_planes = held([P, S], U8, "v_planes")
-        v_sc = {0: v_planes}
-        for a in range(1, K_PASSES):
-            v_sc[a] = held([P, S], U8, "v_sc%d" % a)
-            nc.vector.memset(v_sc[a][:].bitcast(I32), 0)
-        gather_tab(0)
-        load_tab(2)
-        nc.vector.tensor_copy(v_planes[:], tab_sc[:, :T].indirect(idx[:]))
-        for a in range(1, K_PASSES):
-            nc.sync.dma_start(
-                v_sc[a][:SHIFTED_ROWS, :].bitcast(I32),
-                v_planes[ROWS * a : ROWS * a + SHIFTED_ROWS, :].bitcast(I32),
-            )
+        v_planes = held([P, K_PASSES * S], U8, "v_planes")
+        nc.vector.memset(v_planes[:].bitcast(I32), 0)
+        v_rows = held([P, K_PASSES * S], U8, "v_rows")
+        for a in range(K_PASSES):
+            nc.vector.tensor_copy(v_rows[:, S * a : S * (a + 1)], tab_sc[:, T * a : T * (a + 1)].indirect(idx[:]))
+        for r in range(ROWS):
+            nc.sync.dma_start(v_planes[:].bitcast(I32)[r:P:32, :], v_rows[:].bitcast(I32)[BLOCK * r : P : 32, :])
+        v_sc = {a: v_planes[:, S * a : S * (a + 1)] for a in range(K_PASSES)}
 
         def value_pass(acc, a, half, jt):
             cols = slice(P * jt, P * (jt + 1))
@@ -176,15 +167,14 @@ def tile_list_residue_contact_strength_kernel(
         tiles = [(half, jt) for half in range(HALVES) for jt in range(J_TILES)]
         acc = {(half, jt): bank(J_TILES * half + jt, [P, PASS]) for half, jt in tiles}
         load_w1_rows(0, PACK * H)
-        for a in range(1, K_PASSES):
+        for a in range(K_PASSES):
             gather_tab(a)
         load_w1_rows(1, PACK * H)
         load_w1_half(2, 0)
         load_w1_half(2, 1)
-        for half in range(HALVES):
+        for half, jt in tiles:
             for a in range(K_PASSES):
-                for jt in range(J_TILES):
-                    value_pass(acc[half, jt], a, half, jt)
+                value_pass(acc[half, jt], a, half, jt)
 
         piece = S2 // 2
         v2_sc = {}
@@ -231,7 +221,7 @@ def tile_list_residue_contact_strength_kernel(
                 nc.tensor.matmul_mx(
                     out=acc[half, jt][:],
                     lhsT=v_w[a][:, cols].bitcast(FP8X4),
-                    lhsT_scale=v_planes[ROWS * a : P, cols],
+                    lhsT_scale=v_sc[a][:, cols],
                     rhs=w1_codes[a, half][:].bitcast(FP8X4),
                     rhs_scale=w1_sc[a, half][:],
                     start=(a == 0),

@@ -110,9 +110,9 @@ def tile_list_residue_contact_strength_kernel(
             tab_scales.rearrange("a q t -> q a t").bitcast(I32),
         )
         w4_sc = held([P, K_PASSES * H], U8, "w4_sc")
-        nc.vector.memset(w4_sc[:].bitcast(I32), 0)
+        nc.gpsimd.memset(w4_sc[:].bitcast(I32), 0)
         for r in range(ROWS):
-            nc.sync.dma_start(
+            nc.gpsimd.dma_start(
                 w4_sc[:].bitcast(I32)[r:P:32, :].rearrange("q (a w) -> q a w", a=K_PASSES),
                 w4_scales.rearrange("a (q r) t -> r q a t", r=ROWS)[r].bitcast(I32),
             )
@@ -123,13 +123,11 @@ def tile_list_residue_contact_strength_kernel(
         for a in range(K_PASSES):
             load_tab(a)
         tab2_sc = held([P, T2], U8, "tab2_sc")
-        nc.gpsimd.memset(tab2_sc[:].bitcast(I32), 0)
-        for q in range(QUADS):
-            first = 32 * q + ROWS
-            nc.gpsimd.dma_start(
-                tab2_sc[:].bitcast(I32)[first : first + HALVES * ROWS, :],
-                tab2_scales[:, ROWS * q : ROWS * (q + 1), :].bitcast(I32),
-            )
+        nc.vector.memset(tab2_sc[:].bitcast(I32), 0)
+        nc.sync.dma_start(
+            tab2_sc[:].bitcast(I32)[0 : P : BLOCK // HALVES, :],
+            tab2_scales.rearrange("a q t -> q a t").bitcast(I32),
+        )
         identity = held([P, P], F32, "identity")
         make_identity(nc, identity[:])
 
@@ -177,14 +175,20 @@ def tile_list_residue_contact_strength_kernel(
                 value_pass(acc[half, jt], a, half, jt)
 
         piece = S2 // 2
-        v2_sc = {}
-
-        def gather_tab2_scales(g):
-            v2_sc[g] = placed([P, piece], U8, "v2_sc%d" % g, V2_SC_AT + KIB * g)
-            nc.vector.tensor_copy(v2_sc[g][:], tab2_sc[:].indirect(idx2[:, piece // 16 * g : piece // 16 * (g + 1)]))
-
-        gather_tab2_scales(0)
-        gather_tab2_scales(1)
+        v2_planes = held([P, S2], U8, "v2_planes")
+        nc.vector.memset(v2_planes[:].bitcast(I32), 0)
+        v2_rows = placed([P, S2], U8, "v2_rows", V2_SC_AT)
+        for g in range(2):
+            nc.vector.tensor_copy(
+                v2_rows[:, piece * g : piece * (g + 1)],
+                tab2_sc[:].indirect(idx2[:, piece // 16 * g : piece // 16 * (g + 1)]),
+            )
+        for a in range(HALVES):
+            for r in range(ROWS):
+                nc.gpsimd.dma_start(
+                    v2_planes[:].bitcast(I32)[ROWS * (a + 1) + r : P : 32, :],
+                    v2_rows[:].bitcast(I32)[BLOCK * r + ROWS * a : P : 32, :],
+                )
         order = "j (p u e) -> j u p e"
         values = {}
         for half, jt in tiles:
@@ -329,7 +333,7 @@ def tile_list_residue_contact_strength_kernel(
                 nc.tensor.matmul_mx(
                     out=y_acc[it][:],
                     lhsT=v2_w[a, g][:, first : first + P].bitcast(FP8X4),
-                    lhsT_scale=v2_sc[g][ROWS * (a + 1) : P, first : first + P],
+                    lhsT_scale=v2_planes[ROWS * (a + 1) : P, P * it : P * (it + 1)],
                     rhs=h_codes[a][:].bitcast(FP8X4),
                     rhs_scale=h_sc[a][:],
                     start=(a == g),

@@ -28,16 +28,17 @@ QUADS = 4
 ROWS = 4
 KIB = 1024
 SHIFTED_ROWS = 112
-TAB_AT = [0, 8 * KIB, 16 * KIB]
+TAB_AT = [0, 8 * KIB, 24 * KIB]
 TAB_EXTENT = [8 * KIB, 8 * KIB, 34 * KIB]
-CLEARED_EXTENT = 20 * KIB
-V_W_AT = [72 * KIB, 0, 8 * KIB]
-V2_SC_AT = 48 * KIB
-W4_AT = 50 * KIB
-TAB_SC_AT = 56 * KIB
-W1_AT = [56 * KIB, 16 * KIB]
-W1_LAST_AT = [32 * KIB, 40 * KIB]
-TAB2_AT = [56 * KIB, 16 * KIB]
+CLEARED_EXTENT = 9 * KIB
+W4_AT = 16 * KIB
+FIRST_SC_AT = 22 * KIB
+LATER_SC_AT = 58 * KIB
+V_W_AT = [74 * KIB, 0, 8 * KIB]
+V2_SC_AT = 56 * KIB
+W1_AT = [58 * KIB, 24 * KIB]
+W1_LAST_AT = [40 * KIB, 48 * KIB]
+TAB2_AT = [58 * KIB, 24 * KIB]
 GROUPED_AT = 76 * KIB
 BLOCK = 8
 VECTOR_SQUARES = (6,)
@@ -96,32 +97,34 @@ def tile_list_residue_contact_strength_kernel(
 
         nc.sync.dma_start(idx[:], offs)
         nc.sync.dma_start(idx2[:], offs2)
+        load_tab(0)
+
+        first_sc = placed([P, 2 * T], U8, "first_sc", FIRST_SC_AT)
+        nc.gpsimd.memset(first_sc[:, :T].bitcast(I32), 0)
+        nc.sync.dma_start(first_sc[:, :T].bitcast(I32)[ROWS:P:BLOCK, :], tab_scales[0].bitcast(I32))
+        later_sc = placed([P, 9 * T], U8, "later_sc", LATER_SC_AT)
+        nc.vector.memset(later_sc[:, : 2 * T].bitcast(I32), 0)
+        nc.sync.dma_start(
+            later_sc[:, : 2 * T].bitcast(I32)[ROWS:P:BLOCK, :].rearrange("q (a w) -> q a w", a=2),
+            tab_scales[1:].rearrange("a q t -> q a t").bitcast(I32),
+        )
+        w4_sc = held([P, K_PASSES * H], U8, "w4_sc")
+        nc.gpsimd.memset(w4_sc[:].bitcast(I32), 0)
+        for r in range(ROWS):
+            nc.sync.dma_start(
+                w4_sc[:].bitcast(I32)[r:P:32, :].rearrange("q (a w) -> q a w", a=K_PASSES),
+                w4_scales.rearrange("a (q r) t -> r q a t", r=ROWS)[r].bitcast(I32),
+            )
+        cleared = placed([P, CLEARED_EXTENT // 4], F32, "cleared", TAB_AT[1])
+        nc.vector.memset(cleared[:, 0:1], 0.0)
+        origin = held([P, 1], F32, "origin")
+        nc.vector.tensor_copy(origin[:], cleared[:, 0:1])
+        load_tab(1)
         w4 = placed([P, K_PASSES * 2 * H], U8, "w4", W4_AT)
         nc.sync.dma_start(
             w4[:].bitcast(I32).rearrange("p (a w) -> p a w", a=K_PASSES),
             w4_words.rearrange("a p c -> p a c").bitcast(I32),
         )
-
-        tab_sc = placed([P, 18 * KIB], U8, "tab_sc", TAB_SC_AT)
-        nc.gpsimd.memset(tab_sc[:, :T].bitcast(I32), 0)
-        nc.vector.memset(tab_sc[:, T : K_PASSES * T].bitcast(I32), 0)
-        nc.sync.dma_start(
-            tab_sc[:, : K_PASSES * T].bitcast(I32)[0:P:BLOCK, :].rearrange("q (a w) -> q a w", a=K_PASSES),
-            tab_scales.rearrange("a q t -> q a t").bitcast(I32),
-        )
-        w4_sc = held([P, K_PASSES * H], U8, "w4_sc")
-        nc.gpsimd.memset(w4_sc[:].bitcast(I32), 0)
-        for r in range(ROWS):
-            nc.gpsimd.dma_start(
-                w4_sc[:].bitcast(I32)[r:P:32, :].rearrange("q (a w) -> q a w", a=K_PASSES),
-                w4_scales.rearrange("a (q r) t -> r q a t", r=ROWS)[r].bitcast(I32),
-            )
-        cleared = placed([P, CLEARED_EXTENT // 4], F32, "cleared", TAB_AT[0])
-        nc.vector.memset(cleared[:, 0:1], 0.0)
-        origin = held([P, 1], F32, "origin")
-        nc.vector.tensor_copy(origin[:], cleared[:, 0:1])
-        for a in range(K_PASSES):
-            load_tab(a)
         tab2_sc = held([P, T2], U8, "tab2_sc")
         nc.vector.memset(tab2_sc[:].bitcast(I32), 0)
         nc.sync.dma_start(
@@ -140,14 +143,22 @@ def tile_list_residue_contact_strength_kernel(
             v_w[a] = placed([P, S], U32, "v_w%d" % a, V_W_AT[a])
             nc.vector.tensor_copy(v_w[a][:], tab_w[a][:, :T].bitcast(U32).indirect(idx[:]))
 
-        v_planes = held([P, K_PASSES * S], U8, "v_planes")
-        nc.vector.memset(v_planes[:].bitcast(I32), 0)
-        v_rows = held([P, K_PASSES * S], U8, "v_rows")
-        for a in range(K_PASSES):
-            nc.vector.tensor_copy(v_rows[:, S * a : S * (a + 1)], tab_sc[:, T * a : T * (a + 1)].indirect(idx[:]))
-        for r in range(ROWS):
-            nc.sync.dma_start(v_planes[:].bitcast(I32)[r:P:32, :], v_rows[:].bitcast(I32)[BLOCK * r : P : 32, :])
-        v_sc = {a: v_planes[:, S * a : S * (a + 1)] for a in range(K_PASSES)}
+        def planes_from(windows, name):
+            width = S * len(windows)
+            planes = held([P, width], U8, name + "_planes")
+            nc.vector.memset(planes[:].bitcast(I32), 0)
+            rows = held([P, width], U8, name + "_rows")
+            for n, window in enumerate(windows):
+                nc.vector.tensor_copy(rows[:, S * n : S * (n + 1)], window.indirect(idx[:]))
+            for r in range(ROWS):
+                nc.sync.dma_start(
+                    planes[:].bitcast(I32)[r:P:32, :], rows[:].bitcast(I32)[BLOCK * r + ROWS : P : 32, :]
+                )
+            return [planes[:, S * n : S * (n + 1)] for n in range(len(windows))]
+
+        v_sc = planes_from([first_sc[:, :T]], "first")
+        load_tab(2)
+        v_sc.extend(planes_from([later_sc[:, :T], later_sc[:, T : 2 * T]], "later"))
 
         def value_pass(acc, a, half, jt):
             cols = slice(P * jt, P * (jt + 1))
@@ -171,7 +182,9 @@ def tile_list_residue_contact_strength_kernel(
         load_w1_half(2, 0)
         load_w1_half(2, 1)
         for half, jt in tiles:
-            for a in range(K_PASSES):
+            value_pass(acc[half, jt], 0, half, jt)
+        for half, jt in tiles:
+            for a in range(1, K_PASSES):
                 value_pass(acc[half, jt], a, half, jt)
 
         piece = S2 // 2

@@ -95,9 +95,9 @@ def tile_list_residue_contact_strength_kernel(
             nc.sync.dma_start(tile[:], rows.rearrange("(p t) c -> p t c", t=PACK))
             w1_raw[a, half] = tile[:]
 
+        load_tab(0)
         nc.sync.dma_start(idx[:], offs)
         nc.sync.dma_start(idx2[:], offs2)
-        load_tab(0)
 
         first_sc = placed([P, 2 * T], U8, "first_sc", FIRST_SC_AT)
         nc.gpsimd.memset(first_sc[:, :T].bitcast(I32), 0)
@@ -111,7 +111,7 @@ def tile_list_residue_contact_strength_kernel(
         w4_sc = held([P, K_PASSES * H], U8, "w4_sc")
         nc.gpsimd.memset(w4_sc[:].bitcast(I32), 0)
         for r in range(ROWS):
-            nc.sync.dma_start(
+            nc.gpsimd.dma_start(
                 w4_sc[:].bitcast(I32)[r:P:32, :].rearrange("q (a w) -> q a w", a=K_PASSES),
                 w4_scales.rearrange("a (q r) t -> r q a t", r=ROWS)[r].bitcast(I32),
             )

@@ -100,7 +100,7 @@ def tile_list_residue_contact_strength_kernel(
         nc.sync.dma_start(idx2[:], offs2)
 
         first_sc = placed([P, 2 * T], U8, "first_sc", FIRST_SC_AT)
-        nc.gpsimd.memset(first_sc[:, :T].bitcast(I32), 0)
+        nc.vector.memset(first_sc[:, :T].bitcast(I32), 0)
         nc.sync.dma_start(first_sc[:, :T].bitcast(I32)[ROWS:P:BLOCK, :], tab_scales[0].bitcast(I32))
         later_sc = placed([P, 9 * T], U8, "later_sc", LATER_SC_AT)
         nc.vector.memset(later_sc[:, : 2 * T].bitcast(I32), 0)
@@ -126,7 +126,8 @@ def tile_list_residue_contact_strength_kernel(
             w4_words.rearrange("a p c -> p a c").bitcast(I32),
         )
         tab2_sc = held([P, T2], U8, "tab2_sc")
-        nc.vector.memset(tab2_sc[:].bitcast(I32), 0)
+        for words in (slice(0, T2 // 8 + 1), slice(T2 // 8 + 1, T2 // 4)):
+            nc.vector.memset(tab2_sc[:].bitcast(I32)[:, words], 0)
         nc.sync.dma_start(
             tab2_sc[:].bitcast(I32)[0 : P : BLOCK // HALVES, :],
             tab2_scales.rearrange("a q t -> q a t").bitcast(I32),

@@ -24,29 +24,34 @@ K_PASSES = K // PASS
 HALVES = H // PASS
 J_TILES = S // P
 I_TILES = S2 // P
-QUADS = 4
+QUADRANT = 32
 ROWS = 4
+BLOCK = 8
+LIST_ROWS = 16
+GROUP = S2 // 2
 KIB = 1024
-SHIFTED_ROWS = 112
+
 TAB_AT = [0, 8 * KIB, 24 * KIB]
 TAB_EXTENT = [8 * KIB, 8 * KIB, 34 * KIB]
 CLEARED_EXTENT = 9 * KIB
 W4_AT = 16 * KIB
 FIRST_SC_AT = 22 * KIB
+FIRST_SC_EXTENT = 4 * KIB
 LATER_SC_AT = 58 * KIB
+LATER_SC_EXTENT = 18 * KIB
 V_W_AT = [74 * KIB, 0, 8 * KIB]
-V2_SC_AT = 56 * KIB
+V2_ROWS_AT = 56 * KIB
 W1_AT = [58 * KIB, 24 * KIB]
 W1_LAST_AT = [40 * KIB, 48 * KIB]
 TAB2_AT = [58 * KIB, 24 * KIB]
 GROUPED_AT = 76 * KIB
-BLOCK = 8
-VECTOR_SQUARES = (6,)
-GPSIMD_FINALS = (1, 2, 3, 5)
-SCALAR_FINALS = (6, 8)
-VECTOR_LEAD = 3
-VECTOR_COLS = {(0, 0): 512, (0, 1): 192, (1, 0): 320, (1, 1): 0, (2, 0): 512, (2, 1): 320}
 H_GROUPED_AT = [100 * KIB, 104 * KIB]
+
+VECTOR_COLS = 320
+VECTOR_SQUARES = (6,)
+VECTOR_LEAD = 3
+GPSIMD_FINALS = (1, 2, 3)
+SCALAR_FINALS = (4, 8)
 
 
 def tile_list_residue_contact_strength_kernel(
@@ -67,8 +72,8 @@ def tile_list_residue_contact_strength_kernel(
         def bank(number, shape):
             return psum.tile(shape, F32, name="bank%d" % number, tag="bank%d" % number)
 
-        idx = keep.tile([P, S // 16], U16, name="idx")
-        idx2 = keep.tile([P, S2 // 16], U16, name="idx2")
+        idx = keep.tile([P, S // LIST_ROWS], U16, name="idx")
+        idx2 = keep.tile([P, S2 // LIST_ROWS], U16, name="idx2")
 
         tab_w = {}
         tab2_w = {}
@@ -82,8 +87,8 @@ def tile_list_residue_contact_strength_kernel(
             tab2_w[a] = placed([P, T2], I32, "tab2_w%d" % a, TAB2_AT[a])
             nc.sync.dma_start(tab2_w[a][:], tab2_words[a].rearrange("p t i -> p (t i)").bitcast(I32))
 
-        def load_w1_rows(a, width):
-            whole = placed([P, width], F32, "w1_rows%d" % a, W1_AT[a])
+        def load_w1_rows(a):
+            whole = placed([P, PACK * H], F32, "w1_rows%d" % a, W1_AT[a])
             rows = whole[:, : PACK * H].rearrange("p (t c) -> p t c", t=PACK)
             nc.sync.dma_start(rows, w1[PASS * a : PASS * (a + 1), :].rearrange("(p t) c -> p t c", t=PACK))
             for half in range(HALVES):
@@ -99,10 +104,10 @@ def tile_list_residue_contact_strength_kernel(
         nc.sync.dma_start(idx[:], offs)
         nc.sync.dma_start(idx2[:], offs2)
 
-        first_sc = placed([P, 2 * T], U8, "first_sc", FIRST_SC_AT)
+        first_sc = placed([P, FIRST_SC_EXTENT], U8, "first_sc", FIRST_SC_AT)
         nc.vector.memset(first_sc[:, :T].bitcast(I32), 0)
         nc.sync.dma_start(first_sc[:, :T].bitcast(I32)[ROWS:P:BLOCK, :], tab_scales[0].bitcast(I32))
-        later_sc = placed([P, 9 * T], U8, "later_sc", LATER_SC_AT)
+        later_sc = placed([P, LATER_SC_EXTENT], U8, "later_sc", LATER_SC_AT)
         nc.vector.memset(later_sc[:, : 2 * T].bitcast(I32), 0)
         nc.sync.dma_start(
             later_sc[:, : 2 * T].bitcast(I32)[ROWS:P:BLOCK, :].rearrange("q (a w) -> q a w", a=2),
@@ -112,7 +117,7 @@ def tile_list_residue_contact_strength_kernel(
         nc.gpsimd.memset(w4_sc[:].bitcast(I32), 0)
         for r in range(ROWS):
             nc.gpsimd.dma_start(
-                w4_sc[:].bitcast(I32)[r:P:32, :].rearrange("q (a w) -> q a w", a=K_PASSES),
+                w4_sc[:].bitcast(I32)[r:P:QUADRANT, :].rearrange("q (a w) -> q a w", a=K_PASSES),
                 w4_scales.rearrange("a (q r) t -> r q a t", r=ROWS)[r].bitcast(I32),
             )
         cleared = placed([P, CLEARED_EXTENT // 4], F32, "cleared", TAB_AT[1])
@@ -153,7 +158,7 @@ def tile_list_residue_contact_strength_kernel(
                 nc.vector.tensor_copy(rows[:, S * n : S * (n + 1)], window.indirect(idx[:]))
             for r in range(ROWS):
                 nc.sync.dma_start(
-                    planes[:].bitcast(I32)[r:P:32, :], rows[:].bitcast(I32)[BLOCK * r + ROWS : P : 32, :]
+                    planes[:].bitcast(I32)[r:P:QUADRANT, :], rows[:].bitcast(I32)[BLOCK * r + ROWS : P : QUADRANT, :]
                 )
             return [planes[:, S * n : S * (n + 1)] for n in range(len(windows))]
 
@@ -161,11 +166,11 @@ def tile_list_residue_contact_strength_kernel(
         load_tab(2)
         v_sc.extend(planes_from([later_sc[:, :T], later_sc[:, T : 2 * T]], "later"))
 
-        def value_pass(acc, a, half, jt):
+        def value_pass(half, jt, a):
             cols = slice(P * jt, P * (jt + 1))
             first = H * a + PASS * half
             nc.tensor.matmul_mx(
-                out=acc[:],
+                out=value_acc[half, jt][:],
                 lhsT=v_w[a][:, cols].bitcast(FP8X4),
                 lhsT_scale=v_sc[a][:, cols],
                 rhs=w4[:, 2 * first : 2 * (first + PASS)].bitcast(FP4X4),
@@ -175,52 +180,51 @@ def tile_list_residue_contact_strength_kernel(
             )
 
         tiles = [(half, jt) for half in range(HALVES) for jt in range(J_TILES)]
-        acc = {(half, jt): bank(J_TILES * half + jt, [P, PASS]) for half, jt in tiles}
-        load_w1_rows(0, PACK * H)
+        value_acc = {(half, jt): bank(J_TILES * half + jt, [P, PASS]) for half, jt in tiles}
+        load_w1_rows(0)
         for a in range(K_PASSES):
             gather_tab(a)
-        load_w1_rows(1, PACK * H)
+        load_w1_rows(1)
         load_w1_half(2, 0)
         load_w1_half(2, 1)
         for half, jt in tiles:
-            value_pass(acc[half, jt], 0, half, jt)
+            value_pass(half, jt, 0)
         for half, jt in tiles:
             for a in range(1, K_PASSES):
-                value_pass(acc[half, jt], a, half, jt)
+                value_pass(half, jt, a)
 
-        piece = S2 // 2
+        def group_offsets(g):
+            return idx2[:, GROUP // LIST_ROWS * g : GROUP // LIST_ROWS * (g + 1)]
+
         v2_planes = held([P, S2], U8, "v2_planes")
         nc.vector.memset(v2_planes[:].bitcast(I32), 0)
-        v2_rows = placed([P, S2], U8, "v2_rows", V2_SC_AT)
-        for g in range(2):
-            nc.vector.tensor_copy(
-                v2_rows[:, piece * g : piece * (g + 1)],
-                tab2_sc[:].indirect(idx2[:, piece // 16 * g : piece // 16 * (g + 1)]),
-            )
+        v2_rows = placed([P, S2], U8, "v2_rows", V2_ROWS_AT)
+        for g in range(S2 // GROUP):
+            nc.vector.tensor_copy(v2_rows[:, GROUP * g : GROUP * (g + 1)], tab2_sc[:].indirect(group_offsets(g)))
         for a in range(HALVES):
             for r in range(ROWS):
                 nc.gpsimd.dma_start(
-                    v2_planes[:].bitcast(I32)[ROWS * (a + 1) + r : P : 32, :],
-                    v2_rows[:].bitcast(I32)[BLOCK * r + ROWS * a : P : 32, :],
+                    v2_planes[:].bitcast(I32)[ROWS * (a + 1) + r : P : QUADRANT, :],
+                    v2_rows[:].bitcast(I32)[BLOCK * r + ROWS * a : P : QUADRANT, :],
                 )
-        order = "j (p u e) -> j u p e"
+        pair_order = "j (p u e) -> j u p e"
         values = {}
         for half, jt in tiles:
             values[half, jt] = held([P, 2, P, 2], F32, "values%d%d" % (half, jt))
-            nc.scalar.copy(values[half, jt][:], acc[half, jt][:].rearrange(order, u=2, e=2))
+            nc.scalar.copy(values[half, jt][:], value_acc[half, jt][:].rearrange(pair_order, u=2, e=2))
 
         w1_codes = {}
         w1_sc = {}
         w1_grouped = {}
 
-        def interleaved(grouped, raw):
-            return grouped.rearrange("p (c i) t -> p c t i", i=4), raw.rearrange("p t (c i) -> p c t i", i=4)
-
         def round_w1(copy, a, half, c0, c1):
             if (a, half) not in w1_grouped:
                 at = GROUPED_AT + 4 * KIB * (HALVES * a + half)
                 w1_grouped[a, half] = placed([P, PASS, PACK], BF16, "w1_grouped%d%d" % (a, half), at)
-            copy(*interleaved(w1_grouped[a, half][:, c0:c1, :], w1_raw[a, half][:, :, c0:c1]))
+            copy(
+                w1_grouped[a, half][:, c0:c1, :].rearrange("p (c i) t -> p c t i", i=4),
+                w1_raw[a, half][:, :, c0:c1].rearrange("p t (c i) -> p c t i", i=4),
+            )
 
         def quantise_w1(a, half):
             w1_codes[a, half] = held([P, PASS], U32, "w1_codes%d%d" % (a, half))
@@ -231,13 +235,13 @@ def tile_list_residue_contact_strength_kernel(
                 in_=w1_grouped[a, half][:].rearrange("p c t -> p (c t)"),
             )
 
-        acc = {(half, jt): bank(J_TILES * half + jt, [P, PASS]) for half, jt in tiles}
+        gate_acc = {(half, jt): bank(J_TILES * half + jt, [P, PASS]) for half, jt in tiles}
 
         def gate_passes(a, half):
             for jt in range(J_TILES):
                 cols = slice(P * jt, P * (jt + 1))
                 nc.tensor.matmul_mx(
-                    out=acc[half, jt][:],
+                    out=gate_acc[half, jt][:],
                     lhsT=v_w[a][:, cols].bitcast(FP8X4),
                     lhsT_scale=v_sc[a][:, cols],
                     rhs=w1_codes[a, half][:].bitcast(FP8X4),
@@ -256,7 +260,10 @@ def tile_list_residue_contact_strength_kernel(
         def gelu(half, jt):
             gates[half, jt] = held([P, 2, P, 2], F32, "gate%d%d" % (half, jt), "gate%d" % jt)
             nc.scalar.activation(
-                gates[half, jt][:], acc[half, jt][:].rearrange(order, u=2, e=2), ACT.Gelu_apprx_tanh, bias=gelu_bias[:]
+                gates[half, jt][:],
+                gate_acc[half, jt][:].rearrange(pair_order, u=2, e=2),
+                ACT.Gelu_apprx_tanh,
+                bias=gelu_bias[:],
             )
 
         def gated(half, jt):
@@ -289,24 +296,24 @@ def tile_list_residue_contact_strength_kernel(
         quantise_w1(0, 0)
         gate_passes(0, 0)
         quantise_w1(0, 1)
-        round_w1(vector, 1, 0, 0, 320)
-        round_w1(scalar, 1, 0, 320, PASS)
-        round_w1(scalar, 1, 1, 0, 320)
+        round_w1(vector, 1, 0, 0, VECTOR_COLS)
+        round_w1(scalar, 1, 0, VECTOR_COLS, PASS)
+        round_w1(scalar, 1, 1, 0, VECTOR_COLS)
         quantise_w1(1, 0)
         gate_passes(1, 0)
-        round_w1(vector, 2, 0, 0, 320)
-        round_w1(scalar, 2, 0, 320, PASS)
-        round_w1(scalar, 1, 1, 320, PASS)
+        round_w1(vector, 2, 0, 0, VECTOR_COLS)
+        round_w1(scalar, 2, 0, VECTOR_COLS, PASS)
+        round_w1(scalar, 1, 1, VECTOR_COLS, PASS)
         load_tab2(1)
         quantise_w1(2, 0)
         gate_passes(2, 0)
         gate_passes(0, 1)
         quantise_w1(1, 1)
         gate_passes(1, 1)
-        round_w1(vector, 2, 1, 0, 320)
+        round_w1(vector, 2, 1, 0, VECTOR_COLS)
         gelu(0, 0)
         gelu(0, 1)
-        round_w1(scalar, 2, 1, 320, PASS)
+        round_w1(scalar, 2, 1, VECTOR_COLS, PASS)
         gated(0, 0)
         gated(0, 1)
         quantise_w1(2, 1)
@@ -315,26 +322,14 @@ def tile_list_residue_contact_strength_kernel(
         gelu(0, 3)
         gated(0, 2)
         gated(0, 3)
-        for jt in range(J_TILES):
-            turn(0, jt)
-        for jt in range(J_TILES):
-            gelu(1, jt)
-        for jt in range(J_TILES):
-            group_h(0, jt)
-        for jt in range(J_TILES):
-            gated(1, jt)
-        for jt in range(J_TILES):
-            turn(1, jt)
-        for jt in range(J_TILES):
-            group_h(1, jt)
+        for step, half in ((turn, 0), (gelu, 1), (group_h, 0), (gated, 1), (turn, 1), (group_h, 1)):
+            for jt in range(J_TILES):
+                step(half, jt)
         v2_w = {}
 
         def gather_tab2(a, g, tile):
             v2_w[a, g] = tile
-            nc.vector.tensor_copy(
-                v2_w[a, g][:],
-                tab2_w[a][:].bitcast(U32).indirect(idx2[:, piece // 16 * g : piece // 16 * (g + 1)]),
-            )
+            nc.vector.tensor_copy(v2_w[a, g][:], tab2_w[a][:].bitcast(U32).indirect(group_offsets(g)))
 
         one = held([P, 1], F32, "one", "h_rows13")
         nc.scalar.activation(one[:], gelu_bias[:], ACT.Abs_reciprocal_sqrt, bias=1.0)
@@ -343,7 +338,7 @@ def tile_list_residue_contact_strength_kernel(
 
         def contact_passes(a, g):
             for it in range(I_TILES // 2 * g, I_TILES // 2 * (g + 1)):
-                first = P * it - piece * g
+                first = P * it - GROUP * g
                 nc.tensor.matmul_mx(
                     out=y_acc[it][:],
                     lhsT=v2_w[a, g][:, first : first + P].bitcast(FP8X4),
@@ -354,21 +349,21 @@ def tile_list_residue_contact_strength_kernel(
                     stop=(a != g),
                 )
 
-        gather_tab2(0, 0, held([P, piece], U32, "v2_w00", "gate3"))
+        gather_tab2(0, 0, held([P, GROUP], U32, "v2_w00", "gate3"))
         quantise_h(0)
         contact_passes(0, 0)
         quantise_h(1)
-        gather_tab2(1, 0, placed([P, piece], U32, "v2_w10", H_GROUPED_AT[1]))
+        gather_tab2(1, 0, placed([P, GROUP], U32, "v2_w10", H_GROUPED_AT[1]))
         contact_passes(1, 0)
-        gather_tab2(1, 1, placed([P, piece], U32, "v2_w11", H_GROUPED_AT[1] + 2 * KIB))
+        gather_tab2(1, 1, placed([P, GROUP], U32, "v2_w11", H_GROUPED_AT[1] + 2 * KIB))
         contact_passes(1, 1)
-        gather_tab2(0, 1, placed([P, piece], U32, "v2_w01", TAB2_AT[1]))
+        gather_tab2(0, 1, placed([P, GROUP], U32, "v2_w01", TAB2_AT[1]))
         contact_passes(0, 1)
 
         pieces = [(it, 0, S) for it in range(I_TILES - 1)] + [(I_TILES - 1, 0, S // 2), (I_TILES - 1, S // 2, S)]
         squares = {}
         roots = {}
-        units = {}
+        normalised = {}
 
         def scratch(kind, n, ring):
             it, c0, c1 = pieces[n]
@@ -389,22 +384,22 @@ def tile_list_residue_contact_strength_kernel(
             roots[n] = scratch("root", n, ["w1_codes10", "w1_codes11", "w1_codes20", "w1_codes21"])
             nc.scalar.activation(roots[n][:], squares[n][:], ACT.Abs_reciprocal_sqrt, bias=one[:])
 
-        def unit(n):
+        def normalise(n):
             it, c0, c1 = pieces[n]
-            units[n] = placed([P, c1 - c0], F32, "unit%d" % n, GROUPED_AT + 2 * KIB * n)
-            nc.vector.tensor_tensor(units[n][:], y_acc[it][:, c0:c1], roots[n][:], MULT)
+            normalised[n] = placed([P, c1 - c0], F32, "unit%d" % n, GROUPED_AT + 2 * KIB * n)
+            nc.vector.tensor_tensor(normalised[n][:], y_acc[it][:, c0:c1], roots[n][:], MULT)
 
         def strength(n):
             it, c0, c1 = pieces[n]
             result = scratch("result", n, ["values%d%d" % tile for tile in tiles] + ["gate2"])
             if n in SCALAR_FINALS:
-                nc.scalar.activation(result[:], units[n][:], ACT.Square)
+                nc.scalar.activation(result[:], normalised[n][:], ACT.Square)
             else:
                 engine = nc.gpsimd if n in GPSIMD_FINALS else nc.vector
-                engine.tensor_tensor(result[:], units[n][:], units[n][:], MULT)
+                engine.tensor_tensor(result[:], normalised[n][:], normalised[n][:], MULT)
             nc.sync.dma_start(out[P * it : P * (it + 1), c0:c1], result[:])
 
-        steps = (square, root, unit, strength)
+        steps = (square, root, normalise, strength)
         for time in range(len(pieces) + len(steps) - 1):
             for lag, step in enumerate(steps):
                 n = time - lag

@@ -28,30 +28,28 @@ QUADRANT = 32
 ROWS = 4
 BLOCK = 8
 LIST_ROWS = 16
-GROUP = S2 // 2
 KIB = 1024
 
-TAB_AT = [0, 8 * KIB, 24 * KIB]
-TAB_EXTENT = [8 * KIB, 8 * KIB, 34 * KIB]
-CLEARED_EXTENT = 9 * KIB
-W4_AT = 16 * KIB
-FIRST_SC_AT = 22 * KIB
-FIRST_SC_EXTENT = 4 * KIB
-LATER_SC_AT = 58 * KIB
-LATER_SC_EXTENT = 18 * KIB
-V_W_AT = [74 * KIB, 0, 8 * KIB]
-V2_ROWS_AT = 56 * KIB
-W1_AT = [58 * KIB, 24 * KIB]
-W1_LAST_AT = [40 * KIB, 48 * KIB]
-TAB2_AT = [58 * KIB, 24 * KIB]
-GROUPED_AT = 76 * KIB
-H_GROUPED_AT = [100 * KIB, 104 * KIB]
+TAB_AT = [0, 20 * KIB, 28 * KIB]
+W4_AT = [8 * KIB, 60 * KIB]
+W1_AT = {(0, 0): 12, (1, 0): 36, (2, 0): 44, (0, 1): 52, (1, 1): 64, (2, 1): 72}
+TAB2_AT = [80 * KIB, 96 * KIB]
+CLEARED_AT, CLEARED_EXTENT = 8 * KIB, 20 * KIB
+TAB_SC_AT, TAB_SC_EXTENT = 28 * KIB, 86 * KIB
+V_W_AT = [112 * KIB, 114 * KIB, 116 * KIB]
+GROUPED_AT = {(0, 0): 118, (1, 0): 28, (2, 0): 36, (0, 1): 36, (1, 1): 118, (2, 1): 122}
+H_ROWS_AT = [52 * KIB, 53 * KIB, 54 * KIB, 55 * KIB]
+H_GROUPED_AT = [70 * KIB, 126 * KIB]
+H_CODES_AT = [130 * KIB, TAB2_AT[0]]
+VALUES_AT = 132 * KIB
+UNIT_AT = 28 * KIB
+SQUARE_AT = 20 * KIB
 
-VECTOR_COLS = 320
-VECTOR_SQUARES = (6,)
-VECTOR_LEAD = 3
-GPSIMD_FINALS = (1, 2, 3)
-SCALAR_FINALS = (4, 8)
+VECTOR_COLS = {(2, 0): 320, (2, 1): 256}
+LAST_GATHERS = [(0, 2), (2, 4), (4, 8)]
+VECTOR_SQUARES = {5: 0, 6: 2}
+GPSIMD_FINALS = (0, 1, 3)
+SCALAR_FINALS = (2, 6, 8)
 
 
 def tile_list_residue_contact_strength_kernel(
@@ -78,41 +76,46 @@ def tile_list_residue_contact_strength_kernel(
         tab_w = {}
         tab2_w = {}
         w1_raw = {}
+        w4 = {}
 
         def load_tab(a):
-            tab_w[a] = placed([P, TAB_EXTENT[a] // 4], I32, "tab_w%d" % a, TAB_AT[a])
-            nc.sync.dma_start(tab_w[a][:, :T], tab_words[a].rearrange("p t i -> p (t i)").bitcast(I32))
+            tab_w[a] = placed([P, T], I32, "tab_w%d" % a, TAB_AT[a])
+            nc.sync.dma_start(tab_w[a][:], tab_words[a].rearrange("p t i -> p (t i)").bitcast(I32))
 
         def load_tab2(a):
             tab2_w[a] = placed([P, T2], I32, "tab2_w%d" % a, TAB2_AT[a])
             nc.sync.dma_start(tab2_w[a][:], tab2_words[a].rearrange("p t i -> p (t i)").bitcast(I32))
 
-        def load_w1_rows(a):
-            whole = placed([P, PACK * H], F32, "w1_rows%d" % a, W1_AT[a])
-            rows = whole[:, : PACK * H].rearrange("p (t c) -> p t c", t=PACK)
-            nc.sync.dma_start(rows, w1[PASS * a : PASS * (a + 1), :].rearrange("(p t) c -> p t c", t=PACK))
-            for half in range(HALVES):
-                w1_raw[a, half] = rows[:, :, PASS * half : PASS * (half + 1)]
-
-        def load_w1_half(a, half):
-            tile = placed([P, PACK, PASS], F32, "w1_raw%d%d" % (a, half), W1_LAST_AT[half])
+        def load_w1(a, half):
+            tile = placed([P, PACK, PASS], F32, "w1_raw%d%d" % (a, half), KIB * W1_AT[a, half])
             rows = w1[PASS * a : PASS * (a + 1), PASS * half : PASS * (half + 1)]
             nc.sync.dma_start(tile[:], rows.rearrange("(p t) c -> p t c", t=PACK))
             w1_raw[a, half] = tile[:]
+
+        def load_w4(half):
+            w4[half] = placed([P, K_PASSES * 2 * PASS], U8, "w4_%d" % half, W4_AT[half])
+            nc.sync.dma_start(
+                w4[half][:].bitcast(I32).rearrange("p (a w) -> p a w", a=K_PASSES),
+                w4_words[:, :, 2 * PASS * half : 2 * PASS * (half + 1)].rearrange("a p c -> p a c").bitcast(I32),
+            )
 
         load_tab(0)
         nc.sync.dma_start(idx[:], offs)
         nc.sync.dma_start(idx2[:], offs2)
 
-        first_sc = placed([P, FIRST_SC_EXTENT], U8, "first_sc", FIRST_SC_AT)
-        nc.vector.memset(first_sc[:, :T].bitcast(I32), 0)
-        nc.sync.dma_start(first_sc[:, :T].bitcast(I32)[ROWS:P:BLOCK, :], tab_scales[0].bitcast(I32))
-        later_sc = placed([P, LATER_SC_EXTENT], U8, "later_sc", LATER_SC_AT)
-        nc.vector.memset(later_sc[:, : 2 * T].bitcast(I32), 0)
+        cleared = placed([P, CLEARED_EXTENT // 4], F32, "cleared", CLEARED_AT)
+        nc.vector.memset(cleared[:, 0:1], 0.0)
+        tab_sc = placed([P, TAB_SC_EXTENT], U8, "tab_sc", TAB_SC_AT)
+        nc.vector.memset(tab_sc[:, : 2 * T].bitcast(I32), 0)
         nc.sync.dma_start(
-            later_sc[:, : 2 * T].bitcast(I32)[ROWS:P:BLOCK, :].rearrange("q (a w) -> q a w", a=2),
-            tab_scales[1:].rearrange("a q t -> q a t").bitcast(I32),
+            tab_sc[:, :T].bitcast(I32)[0:P:ROWS, :], tab_scales[:2].rearrange("a q t -> q a t").bitcast(I32)
         )
+        nc.sync.dma_start(tab_sc[:, T : 2 * T].bitcast(I32)[ROWS:P:BLOCK, :], tab_scales[2].bitcast(I32))
+        tab2_sc = held([P, T2], U8, "tab2_sc")
+        nc.vector.memset(tab2_sc[:].bitcast(I32), 0)
+        nc.sync.dma_start(tab2_sc[:].bitcast(I32)[0:P:ROWS, :], tab2_scales.rearrange("a q t -> q a t").bitcast(I32))
+        origin = held([P, 1], F32, "origin")
+        nc.vector.tensor_copy(origin[:], cleared[:, 0:1])
         w4_sc = held([P, K_PASSES * H], U8, "w4_sc")
         nc.gpsimd.memset(w4_sc[:].bitcast(I32), 0)
         for r in range(ROWS):
@@ -120,98 +123,69 @@ def tile_list_residue_contact_strength_kernel(
                 w4_sc[:].bitcast(I32)[r:P:QUADRANT, :].rearrange("q (a w) -> q a w", a=K_PASSES),
                 w4_scales.rearrange("a (q r) t -> r q a t", r=ROWS)[r].bitcast(I32),
             )
-        cleared = placed([P, CLEARED_EXTENT // 4], F32, "cleared", TAB_AT[1])
-        nc.vector.memset(cleared[:, 0:1], 0.0)
-        origin = held([P, 1], F32, "origin")
-        nc.vector.tensor_copy(origin[:], cleared[:, 0:1])
+        load_w4(0)
+        load_w1(0, 0)
         load_tab(1)
-        w4 = placed([P, K_PASSES * 2 * H], U8, "w4", W4_AT)
-        nc.sync.dma_start(
-            w4[:].bitcast(I32).rearrange("p (a w) -> p a w", a=K_PASSES),
-            w4_words.rearrange("a p c -> p a c").bitcast(I32),
-        )
-        tab2_sc = held([P, T2], U8, "tab2_sc")
-        for words in (slice(0, T2 // 8 + 1), slice(T2 // 8 + 1, T2 // 4)):
-            nc.vector.memset(tab2_sc[:].bitcast(I32)[:, words], 0)
-        nc.sync.dma_start(
-            tab2_sc[:].bitcast(I32)[0 : P : BLOCK // HALVES, :],
-            tab2_scales.rearrange("a q t -> q a t").bitcast(I32),
-        )
         identity = held([P, P], F32, "identity")
         make_identity(nc, identity[:])
 
         gelu_bias = held([P, 1], F32, "gelu_bias")
         nc.scalar.activation(gelu_bias[:], origin[:], ACT.Gelu_apprx_tanh)
 
+        v_planes = held([P, K_PASSES * S], U8, "v_planes")
+        nc.vector.memset(v_planes[:].bitcast(I32), 0)
+        v2_planes = held([P, S2], U8, "v2_planes")
+        nc.vector.memset(v2_planes[:].bitcast(I32), 0)
+        v_rows = held([P, 2 * S], U8, "v_rows")
+        for n in range(2):
+            nc.vector.tensor_copy(v_rows[:, S * n : S * (n + 1)], tab_sc[:, T * n : T * (n + 1)].indirect(idx[:]))
+
+        def move_planes(first, c0, width):
+            for r in range(ROWS):
+                nc.sync.dma_start(
+                    v_planes[:, c0 : c0 + width].bitcast(I32)[r:P:QUADRANT, :],
+                    v_rows[:, :width].bitcast(I32)[BLOCK * r + first : P : QUADRANT, :],
+                )
+
+        move_planes(0, 0, S)
+        load_tab(2)
+        move_planes(ROWS, S, 2 * S)
+        v_sc = [v_planes[:, S * a : S * (a + 1)] for a in range(K_PASSES)]
+        load_w1(1, 0)
+        load_w1(2, 0)
+        load_w1(0, 1)
+        load_w4(1)
+        load_w1(1, 1)
+        load_w1(2, 1)
+        for a in range(HALVES):
+            load_tab2(a)
+
         v_w = {}
 
         def gather_tab(a):
             v_w[a] = placed([P, S], U32, "v_w%d" % a, V_W_AT[a])
-            nc.vector.tensor_copy(v_w[a][:], tab_w[a][:, :T].bitcast(U32).indirect(idx[:]))
+            nc.vector.tensor_copy(v_w[a][:], tab_w[a][:].bitcast(U32).indirect(idx[:]))
 
-        def planes_from(windows, name):
-            width = S * len(windows)
-            planes = held([P, width], U8, name + "_planes")
-            nc.vector.memset(planes[:].bitcast(I32), 0)
-            rows = held([P, width], U8, name + "_rows")
-            for n, window in enumerate(windows):
-                nc.vector.tensor_copy(rows[:, S * n : S * (n + 1)], window.indirect(idx[:]))
-            for r in range(ROWS):
-                nc.sync.dma_start(
-                    planes[:].bitcast(I32)[r:P:QUADRANT, :], rows[:].bitcast(I32)[BLOCK * r + ROWS : P : QUADRANT, :]
+        def key_offsets(first, last):
+            return idx2[:, P // LIST_ROWS * first : P // LIST_ROWS * last]
+
+        value_acc = {}
+
+        def value_passes(a, half, j_tiles=range(J_TILES)):
+            for jt in j_tiles:
+                if a == 0:
+                    value_acc[half, jt] = bank(J_TILES + jt, [P, PASS])
+                cols = slice(P * jt, P * (jt + 1))
+                first = H * a + PASS * half
+                nc.tensor.matmul_mx(
+                    out=value_acc[half, jt][:],
+                    lhsT=v_w[a][:, cols].bitcast(FP8X4),
+                    lhsT_scale=v_sc[a][:, cols],
+                    rhs=w4[half][:, 2 * PASS * a : 2 * PASS * (a + 1)].bitcast(FP4X4),
+                    rhs_scale=w4_sc[:, first : first + PASS],
+                    start=(a == 0),
+                    stop=(a == K_PASSES - 1),
                 )
-            return [planes[:, S * n : S * (n + 1)] for n in range(len(windows))]
-
-        v_sc = planes_from([first_sc[:, :T]], "first")
-        load_tab(2)
-        v_sc.extend(planes_from([later_sc[:, :T], later_sc[:, T : 2 * T]], "later"))
-
-        def value_pass(half, jt, a):
-            cols = slice(P * jt, P * (jt + 1))
-            first = H * a + PASS * half
-            nc.tensor.matmul_mx(
-                out=value_acc[half, jt][:],
-                lhsT=v_w[a][:, cols].bitcast(FP8X4),
-                lhsT_scale=v_sc[a][:, cols],
-                rhs=w4[:, 2 * first : 2 * (first + PASS)].bitcast(FP4X4),
-                rhs_scale=w4_sc[:, first : first + PASS],
-                start=(a == 0),
-                stop=(a == K_PASSES - 1),
-            )
-
-        tiles = [(half, jt) for half in range(HALVES) for jt in range(J_TILES)]
-        value_acc = {(half, jt): bank(J_TILES * half + jt, [P, PASS]) for half, jt in tiles}
-        load_w1_rows(0)
-        for a in range(K_PASSES):
-            gather_tab(a)
-        load_w1_rows(1)
-        load_w1_half(2, 0)
-        load_w1_half(2, 1)
-        for half, jt in tiles:
-            value_pass(half, jt, 0)
-        for half, jt in tiles:
-            for a in range(1, K_PASSES):
-                value_pass(half, jt, a)
-
-        def group_offsets(g):
-            return idx2[:, GROUP // LIST_ROWS * g : GROUP // LIST_ROWS * (g + 1)]
-
-        v2_planes = held([P, S2], U8, "v2_planes")
-        nc.vector.memset(v2_planes[:].bitcast(I32), 0)
-        v2_rows = placed([P, S2], U8, "v2_rows", V2_ROWS_AT)
-        for g in range(S2 // GROUP):
-            nc.vector.tensor_copy(v2_rows[:, GROUP * g : GROUP * (g + 1)], tab2_sc[:].indirect(group_offsets(g)))
-        for a in range(HALVES):
-            for r in range(ROWS):
-                nc.gpsimd.dma_start(
-                    v2_planes[:].bitcast(I32)[ROWS * (a + 1) + r : P : QUADRANT, :],
-                    v2_rows[:].bitcast(I32)[BLOCK * r + ROWS * a : P : QUADRANT, :],
-                )
-        pair_order = "j (p u e) -> j u p e"
-        values = {}
-        for half, jt in tiles:
-            values[half, jt] = held([P, 2, P, 2], F32, "values%d%d" % (half, jt))
-            nc.scalar.copy(values[half, jt][:], value_acc[half, jt][:].rearrange(pair_order, u=2, e=2))
 
         w1_codes = {}
         w1_sc = {}
@@ -219,7 +193,7 @@ def tile_list_residue_contact_strength_kernel(
 
         def round_w1(copy, a, half, c0, c1):
             if (a, half) not in w1_grouped:
-                at = GROUPED_AT + 4 * KIB * (HALVES * a + half)
+                at = KIB * GROUPED_AT[a, half]
                 w1_grouped[a, half] = placed([P, PASS, PACK], BF16, "w1_grouped%d%d" % (a, half), at)
             copy(
                 w1_grouped[a, half][:, c0:c1, :].rearrange("p (c i) t -> p c t i", i=4),
@@ -235,20 +209,45 @@ def tile_list_residue_contact_strength_kernel(
                 in_=w1_grouped[a, half][:].rearrange("p c t -> p (c t)"),
             )
 
-        gate_acc = {(half, jt): bank(J_TILES * half + jt, [P, PASS]) for half, jt in tiles}
+        vector, scalar = nc.vector.tensor_copy, nc.scalar.copy
+        gather_tab(0)
+        value_passes(0, 0)
+        v2_rows = held([P, S2], U8, "v2_rows")
+        for first in (0, I_TILES // 2):
+            last = first + I_TILES // 2
+            nc.vector.tensor_copy(v2_rows[:, P * first : P * last], tab2_sc[:].indirect(key_offsets(first, last)))
+        for a in range(HALVES):
+            for r in range(ROWS):
+                nc.gpsimd.dma_start(
+                    v2_planes[:].bitcast(I32)[ROWS * (a + 1) + r : P : QUADRANT, :],
+                    v2_rows[:].bitcast(I32)[BLOCK * r + ROWS * a : P : QUADRANT, :],
+                )
+        pair_order = "j (p u e) -> j u p e"
+        values = {}
+
+        def copy_values(jt):
+            values[jt] = placed([P, 2, P, 2], F32, "values%d" % jt, VALUES_AT + 2 * KIB * jt)
+            nc.scalar.copy(values[jt][:], value_acc[0, jt][:].rearrange(pair_order, u=2, e=2))
+
+        gate_acc = {}
+
+        def gate_pass(a, half, jt):
+            if a == 0:
+                gate_acc[half, jt] = bank(jt, [P, PASS])
+            cols = slice(P * jt, P * (jt + 1))
+            nc.tensor.matmul_mx(
+                out=gate_acc[half, jt][:],
+                lhsT=v_w[a][:, cols].bitcast(FP8X4),
+                lhsT_scale=v_sc[a][:, cols],
+                rhs=w1_codes[a, half][:].bitcast(FP8X4),
+                rhs_scale=w1_sc[a, half][:],
+                start=(a == 0),
+                stop=(a == K_PASSES - 1),
+            )
 
         def gate_passes(a, half):
             for jt in range(J_TILES):
-                cols = slice(P * jt, P * (jt + 1))
-                nc.tensor.matmul_mx(
-                    out=gate_acc[half, jt][:],
-                    lhsT=v_w[a][:, cols].bitcast(FP8X4),
-                    lhsT_scale=v_sc[a][:, cols],
-                    rhs=w1_codes[a, half][:].bitcast(FP8X4),
-                    rhs_scale=w1_sc[a, half][:],
-                    start=(a == 0),
-                    stop=(a == K_PASSES - 1),
-                )
+                gate_pass(a, half, jt)
 
         h_codes = {}
         h_sc = {}
@@ -267,12 +266,22 @@ def tile_list_residue_contact_strength_kernel(
             )
 
         def gated(half, jt):
-            h_rows[half, jt] = held([P, 2, P, 2], BF16, "h_rows%d%d" % (half, jt))
-            nc.vector.tensor_tensor(h_rows[half, jt][:], values[half, jt][:], gates[half, jt][:], MULT)
+            name = "h_rows%d%d" % (half, jt)
+            if half == 0:
+                h_rows[half, jt] = placed([P, 2, P, 2], BF16, name, H_ROWS_AT[jt])
+                value = values[jt][:]
+            else:
+                h_rows[half, jt] = held([P, 2, P, 2], BF16, name)
+                value = value_acc[half, jt][:].rearrange(pair_order, u=2, e=2)
+            nc.vector.tensor_tensor(h_rows[half, jt][:], value, gates[half, jt][:], MULT)
 
         def turn(half, jt):
             words = h_rows[half, jt][:].rearrange("j u p e -> j (u p e)").bitcast(F32)
-            turned[half, jt] = bank(J_TILES * half + jt, [P, 2, P])
+            if half == 1:
+                turned[half, jt] = bank(jt, [P, 2, P])[:]
+            elif jt % 2 == 0:
+                pair = bank(J_TILES + 2 + jt // 2, [P, 2, 2, P])
+                turned[half, jt], turned[half, jt + 1] = pair[:, 0], pair[:, 1]
             for u in range(2):
                 nc.tensor.transpose(turned[half, jt][:, u, :], words[:, P * u : P * (u + 1)], identity[:])
 
@@ -281,89 +290,103 @@ def tile_list_residue_contact_strength_kernel(
                 h_grouped[half] = placed([P, S * PACK], BF16, "h_grouped%d" % half, H_GROUPED_AT[half])
             nc.scalar.copy(
                 h_grouped[half][:, PASS * jt : PASS * (jt + 1)].bitcast(F32).rearrange("p (j u) -> p j u", u=2),
-                turned[half, jt][:].rearrange("p u j -> p j u"),
+                turned[half, jt].rearrange("p u j -> p j u"),
             )
 
         def quantise_h(half):
-            h_codes[half] = held([P, S], U32, "h_codes%d" % half)
+            h_codes[half] = placed([P, S], U32, "h_codes%d" % half, H_CODES_AT[half])
             h_sc[half] = held([P, S], U8, "h_sc%d" % half)
             nc.vector.quantize_mx(out=h_codes[half][:].bitcast(FP8X4), scales=h_sc[half][:], in_=h_grouped[half][:])
 
-        vector, scalar = nc.vector.tensor_copy, nc.scalar.copy
-        round_w1(vector, 0, 0, 0, PASS)
-        round_w1(vector, 0, 1, 0, PASS)
-        load_tab2(0)
+        def round_shared(a, half):
+            round_w1(vector, a, half, 0, VECTOR_COLS[a, half])
+            round_w1(scalar, a, half, VECTOR_COLS[a, half], PASS)
+
+        round_w1(scalar, 0, 0, 0, PASS)
         quantise_w1(0, 0)
+        gather_tab(1)
+        value_passes(1, 0)
         gate_passes(0, 0)
-        quantise_w1(0, 1)
-        round_w1(vector, 1, 0, 0, VECTOR_COLS)
-        round_w1(scalar, 1, 0, VECTOR_COLS, PASS)
-        round_w1(scalar, 1, 1, 0, VECTOR_COLS)
+        gather_tab(2)
+        value_passes(2, 0)
+        for jt in range(J_TILES):
+            copy_values(jt)
+        round_w1(vector, 1, 0, 0, PASS)
         quantise_w1(1, 0)
         gate_passes(1, 0)
-        round_w1(vector, 2, 0, 0, VECTOR_COLS)
-        round_w1(scalar, 2, 0, VECTOR_COLS, PASS)
-        round_w1(scalar, 1, 1, VECTOR_COLS, PASS)
-        load_tab2(1)
+        round_shared(2, 0)
         quantise_w1(2, 0)
         gate_passes(2, 0)
+        for jt in range(J_TILES):
+            gelu(0, jt)
+        round_w1(vector, 0, 1, 0, PASS)
+        gated(0, 0)
+        quantise_w1(0, 1)
+        for jt in range(1, J_TILES):
+            gated(0, jt)
+        for jt in range(2):
+            for a in range(K_PASSES):
+                value_passes(a, 1, [jt])
         gate_passes(0, 1)
+        for jt in range(J_TILES):
+            turn(0, jt)
+        round_w1(scalar, 1, 1, 0, PASS)
         quantise_w1(1, 1)
         gate_passes(1, 1)
-        round_w1(vector, 2, 1, 0, VECTOR_COLS)
-        gelu(0, 0)
-        gelu(0, 1)
-        round_w1(scalar, 2, 1, VECTOR_COLS, PASS)
-        gated(0, 0)
-        gated(0, 1)
+        round_shared(2, 1)
         quantise_w1(2, 1)
         gate_passes(2, 1)
-        gelu(0, 2)
-        gelu(0, 3)
-        gated(0, 2)
-        gated(0, 3)
-        for step, half in ((turn, 0), (gelu, 1), (group_h, 0), (gated, 1), (turn, 1), (group_h, 1)):
+        for jt in range(J_TILES):
+            group_h(0, jt)
+        for jt in range(2, J_TILES):
+            for a in range(K_PASSES):
+                value_passes(a, 1, [jt])
+        quantise_h(0)
+        for step in (gelu, gated, turn, group_h):
             for jt in range(J_TILES):
-                step(half, jt)
+                step(1, jt)
+
         v2_w = {}
 
-        def gather_tab2(a, g, tile):
-            v2_w[a, g] = tile
-            nc.vector.tensor_copy(v2_w[a, g][:], tab2_w[a][:].bitcast(U32).indirect(group_offsets(g)))
+        def gather_tab2(a, first, last, tile):
+            nc.vector.tensor_copy(tile[:], tab2_w[a][:].bitcast(U32).indirect(key_offsets(first, last)))
+            for it in range(first, last):
+                v2_w[a, it] = tile[:, P * (it - first) : P * (it - first + 1)]
 
         one = held([P, 1], F32, "one", "h_rows13")
         nc.scalar.activation(one[:], gelu_bias[:], ACT.Abs_reciprocal_sqrt, bias=1.0)
 
-        y_acc = [bank(it, [P, S]) for it in range(I_TILES)]
+        y_acc = [bank(J_TILES + jt, [P, S]) for jt in range(J_TILES)]
+        y_acc.extend(bank(jt, [P, S]) for jt in range(J_TILES))
 
-        def contact_passes(a, g):
-            for it in range(I_TILES // 2 * g, I_TILES // 2 * (g + 1)):
-                first = P * it - GROUP * g
-                nc.tensor.matmul_mx(
-                    out=y_acc[it][:],
-                    lhsT=v2_w[a, g][:, first : first + P].bitcast(FP8X4),
-                    lhsT_scale=v2_planes[ROWS * (a + 1) : P, P * it : P * (it + 1)],
-                    rhs=h_codes[a][:].bitcast(FP8X4),
-                    rhs_scale=h_sc[a][:],
-                    start=(a == g),
-                    stop=(a != g),
-                )
+        def contact_pass(a, it):
+            nc.tensor.matmul_mx(
+                out=y_acc[it][:],
+                lhsT=v2_w[a, it].bitcast(FP8X4),
+                lhsT_scale=v2_planes[ROWS * (a + 1) : P, P * it : P * (it + 1)],
+                rhs=h_codes[a][:].bitcast(FP8X4),
+                rhs_scale=h_sc[a][:],
+                start=(a == it // 4),
+                stop=(a != it // 4),
+            )
 
-        gather_tab2(0, 0, held([P, GROUP], U32, "v2_w00", "gate3"))
-        quantise_h(0)
-        contact_passes(0, 0)
+        gather_tab2(0, 0, 4, held([P, 4 * P], U32, "v2_w00", "gate3"))
+        gather_tab2(0, 4, 8, held([P, 4 * P], U32, "v2_w01", "gate2"))
+        for it in range(4):
+            contact_pass(0, it)
         quantise_h(1)
-        gather_tab2(1, 0, placed([P, GROUP], U32, "v2_w10", H_GROUPED_AT[1]))
-        contact_passes(1, 0)
-        gather_tab2(1, 1, placed([P, GROUP], U32, "v2_w11", H_GROUPED_AT[1] + 2 * KIB))
-        contact_passes(1, 1)
-        gather_tab2(0, 1, placed([P, GROUP], U32, "v2_w01", TAB2_AT[1]))
-        contact_passes(0, 1)
+        for first, last in LAST_GATHERS:
+            gather_tab2(1, first, last, held([P, P * (last - first)], U32, "v2_w1%d" % first))
+            for it in range(first, last):
+                contact_pass(1, it)
+                if it >= 4:
+                    contact_pass(0, it)
 
         pieces = [(it, 0, S) for it in range(I_TILES - 1)] + [(I_TILES - 1, 0, S // 2), (I_TILES - 1, S // 2, S)]
         squares = {}
         roots = {}
         normalised = {}
+        root_ring = ["w1_codes10", "w1_codes11", "w1_codes20", "w1_codes21", "gate0", "gate1"]
 
         def scratch(kind, n, ring):
             it, c0, c1 = pieces[n]
@@ -371,27 +394,31 @@ def tile_list_residue_contact_strength_kernel(
 
         def square(n):
             it, c0, c1 = pieces[n]
-            if n in VECTOR_SQUARES:
-                plain = scratch("y", n, ["gate0"])
-                squares[n] = scratch("x", n, ["gate1"])
-                nc.vector.tensor_copy(plain[:], y_acc[it][:, c0:c1])
-                nc.vector.tensor_tensor(squares[n][:], y_acc[it][:, c0:c1], plain[:], MULT)
-            else:
-                squares[n] = scratch("x", n, ["w1_codes00", "w1_codes01"])
-                nc.scalar.activation(squares[n][:], y_acc[it][:, c0:c1], ACT.Square)
+            squares[n] = placed([P, c1 - c0], F32, "x%d" % n, SQUARE_AT + 2 * KIB * (n % 2))
+            nc.scalar.activation(squares[n][:], y_acc[it][:, c0:c1], ACT.Square)
+
+        def vector_square(n, after):
+            it, c0, c1 = pieces[n]
+            plain = held([P, c1 - c0], F32, "y%d" % n, root_ring[after])
+            squares[n] = placed([P, c1 - c0], F32, "x%d" % n, UNIT_AT + 2 * KIB * (len(pieces) + after))
+            nc.vector.tensor_copy(plain[:], y_acc[it][:, c0:c1])
+            nc.vector.tensor_tensor(squares[n][:], y_acc[it][:, c0:c1], plain[:], MULT)
 
         def root(n):
-            roots[n] = scratch("root", n, ["w1_codes10", "w1_codes11", "w1_codes20", "w1_codes21"])
+            roots[n] = scratch("root", n, root_ring)
             nc.scalar.activation(roots[n][:], squares[n][:], ACT.Abs_reciprocal_sqrt, bias=one[:])
 
         def normalise(n):
             it, c0, c1 = pieces[n]
-            normalised[n] = placed([P, c1 - c0], F32, "unit%d" % n, GROUPED_AT + 2 * KIB * n)
+            normalised[n] = placed([P, c1 - c0], F32, "unit%d" % n, UNIT_AT + 2 * KIB * n)
             nc.vector.tensor_tensor(normalised[n][:], y_acc[it][:, c0:c1], roots[n][:], MULT)
+            for m, after in VECTOR_SQUARES.items():
+                if after == n:
+                    vector_square(m, after)
 
         def strength(n):
             it, c0, c1 = pieces[n]
-            result = scratch("result", n, ["values%d%d" % tile for tile in tiles] + ["gate2"])
+            result = placed([P, c1 - c0], F32, "result%d" % n, 2 * KIB * n)
             if n in SCALAR_FINALS:
                 nc.scalar.activation(result[:], normalised[n][:], ACT.Square)
             else:
@@ -405,5 +432,3 @@ def tile_list_residue_contact_strength_kernel(
                 n = time - lag
                 if 0 <= n < len(pieces) and not (step is square and n in VECTOR_SQUARES):
                     step(n)
-            if time + VECTOR_LEAD in VECTOR_SQUARES:
-                square(time + VECTOR_LEAD)

@@ -33,7 +33,7 @@ KIB = 1024
 TAB_AT = [0, 20 * KIB, 28 * KIB]
 W4_AT = [8 * KIB, 60 * KIB]
 W1_AT = {(0, 0): 12, (1, 0): 36, (2, 0): 44, (0, 1): 52, (1, 1): 64, (2, 1): 72}
-TAB2_AT = [80 * KIB, 96 * KIB]
+TAB2_AT = [80 * KIB, 36 * KIB]
 CLEARED_AT, CLEARED_EXTENT = 8 * KIB, 20 * KIB
 TAB_SC_AT, TAB_SC_EXTENT = 28 * KIB, 86 * KIB
 V_W_AT = [112 * KIB, 114 * KIB, 116 * KIB]
@@ -45,11 +45,11 @@ VALUES_AT = 132 * KIB
 UNIT_AT = 28 * KIB
 SQUARE_AT = 20 * KIB
 
-VECTOR_COLS = {(2, 0): 320, (2, 1): 256}
+VECTOR_COLS = {(2, 1): 256}
 LAST_GATHERS = [(0, 2), (2, 4), (4, 8)]
-VECTOR_SQUARES = {5: 0, 6: 2}
-GPSIMD_FINALS = (0, 1, 3)
-SCALAR_FINALS = (2, 6, 8)
+VECTOR_SQUARES = {6: 1}
+GPSIMD_FINALS = (1, 2, 3)
+SCALAR_FINALS = (4, 8)
 
 
 def tile_list_residue_contact_strength_kernel(
@@ -157,8 +157,7 @@ def tile_list_residue_contact_strength_kernel(
         load_w4(1)
         load_w1(1, 1)
         load_w1(2, 1)
-        for a in range(HALVES):
-            load_tab2(a)
+        load_tab2(0)
 
         v_w = {}
 
@@ -279,9 +278,9 @@ def tile_list_residue_contact_strength_kernel(
             words = h_rows[half, jt][:].rearrange("j u p e -> j (u p e)").bitcast(F32)
             if half == 1:
                 turned[half, jt] = bank(jt, [P, 2, P])[:]
-            elif jt % 2 == 0:
-                pair = bank(J_TILES + 2 + jt // 2, [P, 2, 2, P])
-                turned[half, jt], turned[half, jt + 1] = pair[:, 0], pair[:, 1]
+            elif jt < 2:
+                pair = bank(J_TILES + 2 + jt, [P, 2, 2, P])
+                turned[half, jt], turned[half, 3 - jt] = pair[:, 0], pair[:, 1]
             for u in range(2):
                 nc.tensor.transpose(turned[half, jt][:, u, :], words[:, P * u : P * (u + 1)], identity[:])
 
@@ -314,7 +313,7 @@ def tile_list_residue_contact_strength_kernel(
         round_w1(vector, 1, 0, 0, PASS)
         quantise_w1(1, 0)
         gate_passes(1, 0)
-        round_shared(2, 0)
+        round_w1(vector, 2, 0, 0, PASS)
         quantise_w1(2, 0)
         gate_passes(2, 0)
         for jt in range(J_TILES):
@@ -322,6 +321,7 @@ def tile_list_residue_contact_strength_kernel(
         round_w1(vector, 0, 1, 0, PASS)
         gated(0, 0)
         quantise_w1(0, 1)
+        load_tab2(1)
         for jt in range(1, J_TILES):
             gated(0, jt)
         for jt in range(2):
@@ -370,8 +370,8 @@ def tile_list_residue_contact_strength_kernel(
                 stop=(a != it // 4),
             )
 
-        gather_tab2(0, 0, 4, held([P, 4 * P], U32, "v2_w00", "gate3"))
-        gather_tab2(0, 4, 8, held([P, 4 * P], U32, "v2_w01", "gate2"))
+        gather_tab2(0, 0, 4, held([P, 4 * P], U32, "v2_w00", "gate2"))
+        gather_tab2(0, 4, 8, held([P, 4 * P], U32, "v2_w01", "gate1"))
         for it in range(4):
             contact_pass(0, it)
         quantise_h(1)
@@ -386,7 +386,7 @@ def tile_list_residue_contact_strength_kernel(
         squares = {}
         roots = {}
         normalised = {}
-        root_ring = ["w1_codes10", "w1_codes11", "w1_codes20", "w1_codes21", "gate0", "gate1"]
+        root_ring = ["w1_codes10", "w1_codes11", "w1_codes20", "w1_codes21", "gate0", "gate3"]
 
         def scratch(kind, n, ring):
             it, c0, c1 = pieces[n]

@@ -35,7 +35,7 @@ W4_AT = [8 * KIB, 60 * KIB]
 W1_AT = {(0, 0): 12, (1, 0): 36, (2, 0): 44, (0, 1): 52, (1, 1): 64, (2, 1): 72}
 TAB2_AT = [80 * KIB, 36 * KIB]
 CLEARED_AT, CLEARED_EXTENT = 8 * KIB, 20 * KIB
-TAB_SC_AT, TAB_SC_EXTENT = 28 * KIB, 86 * KIB
+TAB_SC_AT, TAB_SC_EXTENT = [28 * KIB, 44 * KIB], [16 * KIB, 70 * KIB]
 V_W_AT = [112 * KIB, 114 * KIB, 116 * KIB]
 GROUPED_AT = {(0, 0): 118, (1, 0): 28, (2, 0): 36, (0, 1): 36, (1, 1): 118, (2, 1): 122}
 H_ROWS_AT = [52 * KIB, 53 * KIB, 54 * KIB, 55 * KIB]
@@ -105,12 +105,11 @@ def tile_list_residue_contact_strength_kernel(
 
         cleared = placed([P, CLEARED_EXTENT // 4], F32, "cleared", CLEARED_AT)
         nc.vector.memset(cleared[:, 0:1], 0.0)
-        tab_sc = placed([P, TAB_SC_EXTENT], U8, "tab_sc", TAB_SC_AT)
-        nc.vector.memset(tab_sc[:, : 2 * T].bitcast(I32), 0)
-        nc.sync.dma_start(
-            tab_sc[:, :T].bitcast(I32)[0:P:ROWS, :], tab_scales[:2].rearrange("a q t -> q a t").bitcast(I32)
-        )
-        nc.sync.dma_start(tab_sc[:, T : 2 * T].bitcast(I32)[ROWS:P:BLOCK, :], tab_scales[2].bitcast(I32))
+        tab_sc = [placed([P, TAB_SC_EXTENT[n]], U8, "tab_sc%d" % n, TAB_SC_AT[n])[:, :T] for n in range(2)]
+        for window in tab_sc:
+            nc.vector.memset(window.bitcast(I32), 0)
+        nc.sync.dma_start(tab_sc[0].bitcast(I32)[0:P:ROWS, :], tab_scales[:2].rearrange("a q t -> q a t").bitcast(I32))
+        nc.sync.dma_start(tab_sc[1].bitcast(I32)[ROWS:P:BLOCK, :], tab_scales[2].bitcast(I32))
         tab2_sc = held([P, T2], U8, "tab2_sc")
         nc.vector.memset(tab2_sc[:].bitcast(I32), 0)
         nc.sync.dma_start(tab2_sc[:].bitcast(I32)[0:P:ROWS, :], tab2_scales.rearrange("a q t -> q a t").bitcast(I32))
@@ -138,7 +137,7 @@ def tile_list_residue_contact_strength_kernel(
         nc.vector.memset(v2_planes[:].bitcast(I32), 0)
         v_rows = held([P, 2 * S], U8, "v_rows")
         for n in range(2):
-            nc.vector.tensor_copy(v_rows[:, S * n : S * (n + 1)], tab_sc[:, T * n : T * (n + 1)].indirect(idx[:]))
+            nc.vector.tensor_copy(v_rows[:, S * n : S * (n + 1)], tab_sc[n].indirect(idx[:]))
 
         def move_planes(first, c0, width):
             for r in range(ROWS):
@@ -149,9 +148,9 @@ def tile_list_residue_contact_strength_kernel(
 
         move_planes(0, 0, S)
         load_tab(2)
+        load_w1(1, 0)
         move_planes(ROWS, S, 2 * S)
         v_sc = [v_planes[:, S * a : S * (a + 1)] for a in range(K_PASSES)]
-        load_w1(1, 0)
         load_w1(2, 0)
         load_w1(0, 1)
         load_w4(1)

from contextlib import ExitStack

import concourse.mybir as mybir
from concourse.masks import make_identity

K, H, T, S, T2, S2 = 1536, 1024, 2048, 512, 4096, 1024
FLOPS = 2 * (2 * K * H * S + H * S2 * S)

F32 = mybir.dt.float32
BF16 = mybir.dt.bfloat16
I32 = mybir.dt.int32
U32 = mybir.dt.uint32
U16 = mybir.dt.uint16
U8 = mybir.dt.uint8
FP8X4 = mybir.dt.float8_e4m3fn_x4
FP4X4 = mybir.dt.float4_e2m1fn_x4
ACT = mybir.ActivationFunctionType
MULT = mybir.AluOpType.mult

P = 128
PACK = 4
PASS = P * PACK
K_PASSES = K // PASS
HALVES = H // PASS
J_TILES = S // P
I_TILES = S2 // P
QUADRANT = 32
ROWS = 4
BLOCK = 8
LIST_ROWS = 16
KIB = 1024

TAB_AT = [0, 20 * KIB, 28 * KIB]
W4_AT = [8 * KIB, 60 * KIB]
W1_AT = {(0, 0): 12, (1, 0): 36, (2, 0): 44, (0, 1): 52, (1, 1): 64, (2, 1): 72}
TAB2_AT = [80 * KIB, 36 * KIB]
CLEARED_AT, CLEARED_EXTENT = 8 * KIB, 20 * KIB
TAB_SC_AT, TAB_SC_EXTENT = [28 * KIB, 44 * KIB], [16 * KIB, 70 * KIB]
V_W_AT = [112 * KIB, 114 * KIB, 116 * KIB]
GROUPED_AT = {(0, 0): 118, (1, 0): 28, (2, 0): 36, (0, 1): 36, (1, 1): 118, (2, 1): 122}
H_ROWS_AT = [52 * KIB, 53 * KIB, 54 * KIB, 55 * KIB]
H_GROUPED_AT = [70 * KIB, 126 * KIB]
H_CODES_AT = [130 * KIB, TAB2_AT[0]]
VALUES_AT = 132 * KIB
UNIT_AT = 28 * KIB
SQUARE_AT = 20 * KIB

VECTOR_COLS = {(2, 1): 256}
LAST_GATHERS = [(0, 2), (2, 4), (4, 8)]
VECTOR_SQUARES = {6: 1}
GPSIMD_FINALS = (1, 2, 3)
SCALAR_FINALS = (4, 8)


def tile_list_residue_contact_strength_kernel(
    tc, tab_words, tab_scales, offs, tab2_words, tab2_scales, offs2, w1, w4_words, w4_scales, out
):
    nc = tc.nc
    with ExitStack() as ctx:
        keep = ctx.enter_context(tc.tile_pool(name="keep", bufs=1))
        stage = ctx.enter_context(tc.tile_pool(name="stage", bufs=1))
        psum = ctx.enter_context(tc.psum_pool(name="psum", bufs=1))

        def held(shape, dtype, name, after=None):
            return keep.tile(shape, dtype, name=name, tag=after or name, align_bytes=64)

        def placed(shape, dtype, name, at):
            return stage.tile(shape, dtype, name=name, tag=name, align_bytes=64, offset=at)

        def bank(number, shape):
            return psum.tile(shape, F32, name="bank%d" % number, tag="bank%d" % number)

        idx = keep.tile([P, S // LIST_ROWS], U16, name="idx")
        idx2 = keep.tile([P, S2 // LIST_ROWS], U16, name="idx2")

        tab_w = {}
        tab2_w = {}
        w1_raw = {}
        w4 = {}

        def load_tab(a):
            tab_w[a] = placed([P, T], I32, "tab_w%d" % a, TAB_AT[a])
            nc.sync.dma_start(tab_w[a][:], tab_words[a].rearrange("p t i -> p (t i)").bitcast(I32))

        def load_tab2(a):
            tab2_w[a] = placed([P, T2], I32, "tab2_w%d" % a, TAB2_AT[a])
            nc.sync.dma_start(tab2_w[a][:], tab2_words[a].rearrange("p t i -> p (t i)").bitcast(I32))

        def load_w1(a, half):
            tile = placed([P, PACK, PASS], F32, "w1_raw%d%d" % (a, half), KIB * W1_AT[a, half])
            rows = w1[PASS * a : PASS * (a + 1), PASS * half : PASS * (half + 1)]
            nc.sync.dma_start(tile[:], rows.rearrange("(p t) c -> p t c", t=PACK))
            w1_raw[a, half] = tile[:]

        def load_w4(half):
            w4[half] = placed([P, K_PASSES * 2 * PASS], U8, "w4_%d" % half, W4_AT[half])
            nc.sync.dma_start(
                w4[half][:].bitcast(I32).rearrange("p (a w) -> p a w", a=K_PASSES),
                w4_words[:, :, 2 * PASS * half : 2 * PASS * (half + 1)].rearrange("a p c -> p a c").bitcast(I32),
            )

        load_tab(0)
        nc.sync.dma_start(idx[:], offs)
        nc.sync.dma_start(idx2[:], offs2)

        cleared = placed([P, CLEARED_EXTENT // 4], F32, "cleared", CLEARED_AT)
        nc.vector.memset(cleared[:, 0:1], 0.0)
        tab_sc = [placed([P, TAB_SC_EXTENT[n]], U8, "tab_sc%d" % n, TAB_SC_AT[n])[:, :T] for n in range(2)]
        for window in tab_sc:
            nc.vector.memset(window.bitcast(I32), 0)
        nc.sync.dma_start(tab_sc[0].bitcast(I32)[0:P:ROWS, :], tab_scales[:2].rearrange("a q t -> q a t").bitcast(I32))
        nc.sync.dma_start(tab_sc[1].bitcast(I32)[ROWS:P:BLOCK, :], tab_scales[2].bitcast(I32))
        tab2_sc = held([P, T2], U8, "tab2_sc")
        nc.vector.memset(tab2_sc[:].bitcast(I32), 0)
        nc.sync.dma_start(tab2_sc[:].bitcast(I32)[0:P:ROWS, :], tab2_scales.rearrange("a q t -> q a t").bitcast(I32))
        origin = held([P, 1], F32, "origin")
        nc.vector.tensor_copy(origin[:], cleared[:, 0:1])
        w4_sc = held([P, K_PASSES * H], U8, "w4_sc")
        nc.gpsimd.memset(w4_sc[:].bitcast(I32), 0)
        for r in range(ROWS):
            nc.gpsimd.dma_start(
                w4_sc[:].bitcast(I32)[r:P:QUADRANT, :].rearrange("q (a w) -> q a w", a=K_PASSES),
                w4_scales.rearrange("a (q r) t -> r q a t", r=ROWS)[r].bitcast(I32),
            )
        load_w4(0)
        load_w1(0, 0)
        load_tab(1)
        identity = held([P, P], F32, "identity")
        make_identity(nc, identity[:])

        gelu_bias = held([P, 1], F32, "gelu_bias")
        nc.scalar.activation(gelu_bias[:], origin[:], ACT.Gelu_apprx_tanh)

        v_planes = held([P, K_PASSES * S], U8, "v_planes")
        nc.vector.memset(v_planes[:].bitcast(I32), 0)
        v2_planes = held([P, S2], U8, "v2_planes")
        nc.vector.memset(v2_planes[:].bitcast(I32), 0)
        v_rows = held([P, 2 * S], U8, "v_rows")
        for n in range(2):
            nc.vector.tensor_copy(v_rows[:, S * n : S * (n + 1)], tab_sc[n].indirect(idx[:]))

        def move_planes(first, c0, width):
            for r in range(ROWS):
                nc.sync.dma_start(
                    v_planes[:, c0 : c0 + width].bitcast(I32)[r:P:QUADRANT, :],
                    v_rows[:, :width].bitcast(I32)[BLOCK * r + first : P : QUADRANT, :],
                )

        move_planes(0, 0, S)
        load_tab(2)
        load_w1(1, 0)
        move_planes(ROWS, S, 2 * S)
        v_sc = [v_planes[:, S * a : S * (a + 1)] for a in range(K_PASSES)]
        load_w1(2, 0)
        load_w1(0, 1)
        load_w4(1)
        load_w1(1, 1)
        load_w1(2, 1)
        load_tab2(0)

        v_w = {}

        def gather_tab(a):
            v_w[a] = placed([P, S], U32, "v_w%d" % a, V_W_AT[a])
            nc.vector.tensor_copy(v_w[a][:], tab_w[a][:].bitcast(U32).indirect(idx[:]))

        def key_offsets(first, last):
            return idx2[:, P // LIST_ROWS * first : P // LIST_ROWS * last]

        value_acc = {}

        def value_passes(a, half, j_tiles=range(J_TILES)):
            for jt in j_tiles:
                if a == 0:
                    value_acc[half, jt] = bank(J_TILES + jt, [P, PASS])
                cols = slice(P * jt, P * (jt + 1))
                first = H * a + PASS * half
                nc.tensor.matmul_mx(
                    out=value_acc[half, jt][:],
                    lhsT=v_w[a][:, cols].bitcast(FP8X4),
                    lhsT_scale=v_sc[a][:, cols],
                    rhs=w4[half][:, 2 * PASS * a : 2 * PASS * (a + 1)].bitcast(FP4X4),
                    rhs_scale=w4_sc[:, first : first + PASS],
                    start=(a == 0),
                    stop=(a == K_PASSES - 1),
                )

        w1_codes = {}
        w1_sc = {}
        w1_grouped = {}

        def round_w1(copy, a, half, c0, c1):
            if (a, half) not in w1_grouped:
                at = KIB * GROUPED_AT[a, half]
                w1_grouped[a, half] = placed([P, PASS, PACK], BF16, "w1_grouped%d%d" % (a, half), at)
            copy(
                w1_grouped[a, half][:, c0:c1, :].rearrange("p (c i) t -> p c t i", i=4),
                w1_raw[a, half][:, :, c0:c1].rearrange("p t (c i) -> p c t i", i=4),
            )

        def quantise_w1(a, half):
            w1_codes[a, half] = held([P, PASS], U32, "w1_codes%d%d" % (a, half))
            w1_sc[a, half] = held([P, PASS], U8, "w1_sc%d%d" % (a, half))
            nc.vector.quantize_mx(
                out=w1_codes[a, half][:].bitcast(FP8X4),
                scales=w1_sc[a, half][:],
                in_=w1_grouped[a, half][:].rearrange("p c t -> p (c t)"),
            )

        vector, scalar = nc.vector.tensor_copy, nc.scalar.copy
        gather_tab(0)
        value_passes(0, 0)
        v2_rows = held([P, S2], U8, "v2_rows")
        for first in (0, I_TILES // 2):
            last = first + I_TILES // 2
            nc.vector.tensor_copy(v2_rows[:, P * first : P * last], tab2_sc[:].indirect(key_offsets(first, last)))
        for a in range(HALVES):
            for r in range(ROWS):
                nc.gpsimd.dma_start(
                    v2_planes[:].bitcast(I32)[ROWS * (a + 1) + r : P : QUADRANT, :],
                    v2_rows[:].bitcast(I32)[BLOCK * r + ROWS * a : P : QUADRANT, :],
                )
        pair_order = "j (p u e) -> j u p e"
        values = {}

        def copy_values(jt):
            values[jt] = placed([P, 2, P, 2], F32, "values%d" % jt, VALUES_AT + 2 * KIB * jt)
            nc.scalar.copy(values[jt][:], value_acc[0, jt][:].rearrange(pair_order, u=2, e=2))

        gate_acc = {}

        def gate_pass(a, half, jt):
            if a == 0:
                gate_acc[half, jt] = bank(jt, [P, PASS])
            cols = slice(P * jt, P * (jt + 1))
            nc.tensor.matmul_mx(
                out=gate_acc[half, jt][:],
                lhsT=v_w[a][:, cols].bitcast(FP8X4),
                lhsT_scale=v_sc[a][:, cols],
                rhs=w1_codes[a, half][:].bitcast(FP8X4),
                rhs_scale=w1_sc[a, half][:],
                start=(a == 0),
                stop=(a == K_PASSES - 1),
            )

        def gate_passes(a, half):
            for jt in range(J_TILES):
                gate_pass(a, half, jt)

        h_codes = {}
        h_sc = {}
        gates = {}
        h_rows = {}
        h_grouped = {}
        turned = {}

        def gelu(half, jt):
            gates[half, jt] = held([P, 2, P, 2], F32, "gate%d%d" % (half, jt), "gate%d" % jt)
            nc.scalar.activation(
                gates[half, jt][:],
                gate_acc[half, jt][:].rearrange(pair_order, u=2, e=2),
                ACT.Gelu_apprx_tanh,
                bias=gelu_bias[:],
            )

        def gated(half, jt):
            name = "h_rows%d%d" % (half, jt)
            if half == 0:
                h_rows[half, jt] = placed([P, 2, P, 2], BF16, name, H_ROWS_AT[jt])
                value = values[jt][:]
            else:
                h_rows[half, jt] = held([P, 2, P, 2], BF16, name)
                value = value_acc[half, jt][:].rearrange(pair_order, u=2, e=2)
            nc.vector.tensor_tensor(h_rows[half, jt][:], value, gates[half, jt][:], MULT)

        def turn(half, jt):
            words = h_rows[half, jt][:].rearrange("j u p e -> j (u p e)").bitcast(F32)
            if half == 1:
                turned[half, jt] = bank(jt, [P, 2, P])[:]
            elif jt < 2:
                pair = bank(J_TILES + 2 + jt, [P, 2, 2, P])
                turned[half, jt], turned[half, 3 - jt] = pair[:, 0], pair[:, 1]
            for u in range(2):
                nc.tensor.transpose(turned[half, jt][:, u, :], words[:, P * u : P * (u + 1)], identity[:])

        def group_h(half, jt):
            if jt == 0:
                h_grouped[half] = placed([P, S * PACK], BF16, "h_grouped%d" % half, H_GROUPED_AT[half])
            nc.scalar.copy(
                h_grouped[half][:, PASS * jt : PASS * (jt + 1)].bitcast(F32).rearrange("p (j u) -> p j u", u=2),
                turned[half, jt].rearrange("p u j -> p j u"),
            )

        def quantise_h(half):
            h_codes[half] = placed([P, S], U32, "h_codes%d" % half, H_CODES_AT[half])
            h_sc[half] = held([P, S], U8, "h_sc%d" % half)
            nc.vector.quantize_mx(out=h_codes[half][:].bitcast(FP8X4), scales=h_sc[half][:], in_=h_grouped[half][:])

        def round_shared(a, half):
            round_w1(vector, a, half, 0, VECTOR_COLS[a, half])
            round_w1(scalar, a, half, VECTOR_COLS[a, half], PASS)

        round_w1(scalar, 0, 0, 0, PASS)
        quantise_w1(0, 0)
        gather_tab(1)
        value_passes(1, 0)
        gate_passes(0, 0)
        gather_tab(2)
        value_passes(2, 0)
        for jt in range(J_TILES):
            copy_values(jt)
        round_w1(vector, 1, 0, 0, PASS)
        quantise_w1(1, 0)
        gate_passes(1, 0)
        round_w1(vector, 2, 0, 0, PASS)
        quantise_w1(2, 0)
        gate_passes(2, 0)
        for jt in range(J_TILES):
            gelu(0, jt)
        round_w1(vector, 0, 1, 0, PASS)
        gated(0, 0)
        quantise_w1(0, 1)
        load_tab2(1)
        for jt in range(1, J_TILES):
            gated(0, jt)
        for jt in range(2):
            for a in range(K_PASSES):
                value_passes(a, 1, [jt])
        gate_passes(0, 1)
        for jt in range(J_TILES):
            turn(0, jt)
        round_w1(scalar, 1, 1, 0, PASS)
        quantise_w1(1, 1)
        gate_passes(1, 1)
        round_shared(2, 1)
        quantise_w1(2, 1)
        gate_passes(2, 1)
        for jt in range(J_TILES):
            group_h(0, jt)
        for jt in range(2, J_TILES):
            for a in range(K_PASSES):
                value_passes(a, 1, [jt])
        quantise_h(0)
        for step in (gelu, gated, turn, group_h):
            for jt in range(J_TILES):
                step(1, jt)

        v2_w = {}

        def gather_tab2(a, first, last, tile):
            nc.vector.tensor_copy(tile[:], tab2_w[a][:].bitcast(U32).indirect(key_offsets(first, last)))
            for it in range(first, last):
                v2_w[a, it] = tile[:, P * (it - first) : P * (it - first + 1)]

        one = held([P, 1], F32, "one", "h_rows13")
        nc.scalar.activation(one[:], gelu_bias[:], ACT.Abs_reciprocal_sqrt, bias=1.0)

        y_acc = [bank(J_TILES + jt, [P, S]) for jt in range(J_TILES)]
        y_acc.extend(bank(jt, [P, S]) for jt in range(J_TILES))

        def contact_pass(a, it):
            nc.tensor.matmul_mx(
                out=y_acc[it][:],
                lhsT=v2_w[a, it].bitcast(FP8X4),
                lhsT_scale=v2_planes[ROWS * (a + 1) : P, P * it : P * (it + 1)],
                rhs=h_codes[a][:].bitcast(FP8X4),
                rhs_scale=h_sc[a][:],
                start=(a == it // 4),
                stop=(a != it // 4),
            )

        gather_tab2(0, 0, 4, held([P, 4 * P], U32, "v2_w00", "gate2"))
        gather_tab2(0, 4, 8, held([P, 4 * P], U32, "v2_w01", "gate1"))
        for it in range(4):
            contact_pass(0, it)
        quantise_h(1)
        for first, last in LAST_GATHERS:
            gather_tab2(1, first, last, held([P, P * (last - first)], U32, "v2_w1%d" % first))
            for it in range(first, last):
                contact_pass(1, it)
                if it >= 4:
                    contact_pass(0, it)

        pieces = [(it, 0, S) for it in range(I_TILES - 1)] + [(I_TILES - 1, 0, S // 2), (I_TILES - 1, S // 2, S)]
        squares = {}
        roots = {}
        normalised = {}
        root_ring = ["w1_codes10", "w1_codes11", "w1_codes20", "w1_codes21", "gate0", "gate3"]

        def scratch(kind, n, ring):
            it, c0, c1 = pieces[n]
            return held([P, c1 - c0], F32, "%s%d" % (kind, n), ring[n % len(ring)])

        def square(n):
            it, c0, c1 = pieces[n]
            squares[n] = placed([P, c1 - c0], F32, "x%d" % n, SQUARE_AT + 2 * KIB * (n % 2))
            nc.scalar.activation(squares[n][:], y_acc[it][:, c0:c1], ACT.Square)

        def vector_square(n, after):
            it, c0, c1 = pieces[n]
            plain = held([P, c1 - c0], F32, "y%d" % n, root_ring[after])
            squares[n] = placed([P, c1 - c0], F32, "x%d" % n, UNIT_AT + 2 * KIB * (len(pieces) + after))
            nc.vector.tensor_copy(plain[:], y_acc[it][:, c0:c1])
            nc.vector.tensor_tensor(squares[n][:], y_acc[it][:, c0:c1], plain[:], MULT)

        def root(n):
            roots[n] = scratch("root", n, root_ring)
            nc.scalar.activation(roots[n][:], squares[n][:], ACT.Abs_reciprocal_sqrt, bias=one[:])

        def normalise(n):
            it, c0, c1 = pieces[n]
            normalised[n] = placed([P, c1 - c0], F32, "unit%d" % n, UNIT_AT + 2 * KIB * n)
            nc.vector.tensor_tensor(normalised[n][:], y_acc[it][:, c0:c1], roots[n][:], MULT)
            for m, after in VECTOR_SQUARES.items():
                if after == n:
                    vector_square(m, after)

        def strength(n):
            it, c0, c1 = pieces[n]
            result = placed([P, c1 - c0], F32, "result%d" % n, 2 * KIB * n)
            if n in SCALAR_FINALS:
                nc.scalar.activation(result[:], normalised[n][:], ACT.Square)
            else:
                engine = nc.gpsimd if n in GPSIMD_FINALS else nc.vector
                engine.tensor_tensor(result[:], normalised[n][:], normalised[n][:], MULT)
            nc.sync.dma_start(out[P * it : P * (it + 1), c0:c1], result[:])

        steps = (square, root, normalise, strength)
        for time in range(len(pieces) + len(steps) - 1):
            for lag, step in enumerate(steps):
                n = time - lag
                if 0 <= n < len(pieces) and not (step is square and n in VECTOR_SQUARES):
                    step(n)
